import numpy as np, ml_dtypes
CORES = [16,17,18,19,32,33,34,35]
N = 8
BF = ml_dtypes.bfloat16
P, CAP, J, W, D, RO = 256, 32, 16, 8192, 3, 8
WT = np.array([1, 3, 7, 13, 21, 35, 49, 67, 85, 107, 129, 155, 181, 211, 241, 253], np.int32)
KA = np.array([17, 101, 263, 389, 547, 701, 859, 1021, 1171, 1319, 1487, 1637, 1801, 1949, 2111, 2269], np.int32)
def mark(s):
    return np.add.reduce(s * WT[:, None], axis=-2) & 4095
def columns(u, e):
    return ((u * u >> 4)[..., None, :] + KA[:, None] * u[..., None, :] + 811 * e) & (W - 1)
def lanes(rng, v, k):
    return np.minimum((rng.random((N, 8, 16, k), dtype=np.float32) * (v + 1)[:, None, None]).astype(np.int32), v[:, None, None])
def toward(s, r):
    z = np.array(s); z[0] = (s[0] & (64 - N)) + ((s[0] + r - mark(s)) & (N - 1))
    return z
def pack(o, s, c):
    return {"opr": np.ascontiguousarray(o.reshape(N, 128, W)).astype(np.float32).astype(BF), "s0": np.ascontiguousarray(s.reshape(N, 128, P)).astype(np.float32).astype(BF),
            "f0": np.ascontiguousarray(c).astype(np.int32)}
def setup_inputs(rng):
    t = rng.permutation(8); v = np.full(8, 63); v[t[0]] = rng.choice(np.array([1, 3])); v[t[1]] = 15
    span = rng.choice(np.array([40, 100, 200, 400]), (8, 1)); span[t[0]] = 1
    c = (rng.random((N, 8, P)) * (span + 1)).astype(np.int64)
    c = np.where(rng.random((N, 8, P)) < rng.choice(np.array([0.0, 0.1, 0.3]), (N, 8, 1)), 1023, c)
    return pack(lanes(rng, v, W), lanes(rng, v, P), c)
def setup_inputs_spread(rng):
    o = np.minimum((np.exp2(6 * rng.random((N, 8, 1, W))) * rng.random((N, 8, 16, W))).astype(np.int64), 63)
    s = np.minimum((np.exp2(6 * rng.random((N, 8, 1, P))) * rng.random((N, 8, 16, P))).astype(np.int64), 63)
    c = np.minimum(np.exp2(10 * rng.random((N, 8, P))).astype(np.int64) - 1, 1022)
    return pack(o, s, np.where(rng.random((N, 8, P)) < 0.125, 1023, c))
def setup_inputs_ends(rng):
    o = 63 * rng.integers(0, 2, (N, 8, 16, W)); s = 63 * rng.integers(0, 2, (N, 8, 16, P))
    share = rng.permutation(np.array([1.0, 1.0, 1.0, 0.9, 0.7, 0.5, 0.3, 0.1]))
    c = np.where(rng.random((N, 8, P)) < share[:, None], 0, 1023)
    m = 63 * ((np.arange(65536)[:, None] >> np.arange(16)) & 1)
    u = np.arange(4096); free = np.zeros((4096, 16), np.int64)
    free[:, 15] = u // 253; free[:, 4] = (u % 253) // 21; free[:, 0] = (u % 253) % 21
    every = columns(mark(free.T), 0)
    for k, x in ((P - 3, int(np.max(every))), (P // 2, int(np.min(every)))):
        for b in (m, free):
            z = np.nonzero(np.any(columns(mark(b.T), 0) == x, axis=0))[0]
            if len(z):
                s[:, :, :, k] = b[rng.choice(z, (N, 8))]; c[:, :, k] = 0
                break
    s[..., [0, 1, P - 2, P - 1]] = 63; c[..., [0, P - 1]] = 0; c[..., [1, P - 2]] = 1023
    a = columns(mark(np.full((16, 1), 63)), 0)[:, 0]
    o[..., a[0]] = 0; o[..., a[J - 1]] = 63
    return pack(o, s, c)
def setup_inputs_corners(rng):
    t = rng.permutation(8); v = np.full(8, 63); v[t[6]] = 1; v[t[7]] = 7
    o = lanes(rng, v, W); s = lanes(rng, v, P); c = np.full((N, 8, P), 1023); n = CAP // J; big = int(rng.integers(0, N))
    o[:, t[7]] = 0; c[:, t[0]] = 0; c[N - 1, t[2], P - 1] = 0
    c[:, t[6]] = rng.integers(1012, 1024, (N, P)); c[:, t[7]] = rng.integers(0, 101, (N, P))
    a = columns(mark(np.full((16, 1), 63)), 0)[:, 0]
    for q in range(N):
        for k in (3, 4, 5):
            g = int(t[k]); x = rng.integers(0, 16, 16); x[0] = 0
            x[0] = (q + 1 - int(mark(x[:, None])[0])) & (N - 1)
            o[q, g][:, a] = (63 - x)[:, None]; b = 300 - (int(np.add.reduce(x)) >> 2)
            if k == 5: c[q, g] = np.where(rng.random(P) < 0.5, rng.integers(400, 700, P), 1023)
            w = n + k - 3 if k < 5 else n + 1 if q == big else int(rng.integers(0, n + 1))
            p = np.append(P - 1, rng.permutation(P - 1))[:w]
            s[q, g][:, p] = 63; c[q, g, p] = b
            if k == 4: c[q, g, p[-1]] = b + 1
    return pack(o, s, c)
def setup_inputs_edges(rng):
    t = [int(k) for k in rng.permutation(8)]; v = np.full(8, 63); v[t[7]] = 15
    n = CAP // J; r = int(rng.integers(0, N)); big = int(rng.integers(0, N)); top = int(rng.integers(520, 1001))
    o = lanes(rng, v, W); s = lanes(rng, v, P)
    c = (rng.random((N, 8, P)) * rng.choice(np.array([41, 101, 201]), (8, 1))).astype(np.int64)
    c = np.where(rng.random((N, 8, P)) < 0.1, 1023, c)
    o[:, t[:3]] = 0; c[:, t[0]] = rng.integers(1, 201, (N, P)); c[:, t[1:5]] = 1023
    for q in range(N):
        for k in range(3):
            w = n if k == 1 else n + (k == 0) if q == big else int(rng.integers(0, n + 1))
            p = np.append(P - 1, rng.permutation(P - 1))[:w]
            z = toward(s[q, t[k]][:, p], r)
            if k == 0: z = 0 * z
            s[q, t[k]][:, p] = z; h = np.add.reduce(z, axis=0) >> 2
            if k == 0: c[q, t[k], p] = 0
            elif k == 1: c[q, t[k], p] = top + np.arange(q * n, q * n + n) * 8 // (N * n) - 2 * h
            else: c[q, t[k], p] = 1022 - 2 * h
    for k in (3, 4):
        x = t[k]; z = rng.integers(1, 8, 16); z[0] += (2 - int(mark(z[:, None])[0])) & 3
        h = int(np.add.reduce(z)) >> 2; o[:, x] = rng.integers(56, 64, (N, 16, W))
        for e in range(D): o[:, x, :, int(columns(mark(z[:, None]), e)[0, 0])] = 0
        q = rng.permutation(N); a = int(q[0]); p = np.append(P - 1, rng.permutation(P - 1))[:CAP + 1]
        if k == 3: b = int(q[1]); low = 1022 - 3 * h; more = 1
        else: b = a; low = int(rng.integers(850, 911)); more = h
        s[a, x][:, p[1:]] = z[:, None]; c[a, x, p[1:]] = low + more
        s[b, x, :, P - 1] = z; c[b, x, P - 1] = low
    return pack(o, s, c)
def setup_inputs_ties(rng):
    v = rng.permutation(np.array([1, 1, 3, 3, 7, 15, 31, 63])); o = lanes(rng, v, W); s = lanes(rng, v, P)
    c = rng.choice(np.array([0, 5, 9]), (1, 8, 1)) + rng.integers(0, 2, (N, 8, P)) * rng.choice(np.array([0, 1, 3]), (1, 8, 1))
    s[:, 1::2, :, P // 2:] = s[:, 1::2, :, :P // 2]
    c = np.where(rng.random((N, 8, P)) < 0.05, 1023, c)
    x = int(np.nonzero(v == 1)[0][0]); y = int(np.nonzero(v == 3)[0][0])
    o[:, x] = 0; c[:, x] = 1023
    s[:, x] = rng.integers(0, 64, (N, 16, P)); s[:, x, 0] = np.maximum(s[:, x, 0], 4)
    for q in range(N):
        p = np.append(P - 1, rng.permutation(P - 1))[:CAP // J]
        a = np.add.reduce(s[q, x][:, p], axis=0) >> 2
        c[q, x, p] = 1022 - a - rng.integers(0, a)
    z = rng.integers(1, 8, 16); z[0] += (2 - int(mark(z[:, None])[0])) & 3
    a = int(np.add.reduce(z)) >> 2; b = int(rng.integers(850, 931))
    o[:, y] = rng.integers(56, 64, (N, 16, W)); c[:, y] = 1023
    for e in range(D): o[:, y, :, int(columns(mark(z[:, None]), e)[0, 0])] = 0
    q = rng.permutation(N); p = rng.permutation(P)[:CAP]
    s[int(q[0]), y][:, p] = z[:, None]; c[int(q[0]), y, p] = b + a
    s[int(q[1]), y, :, P - 1] = z; c[int(q[1]), y, P - 1] = b
    return pack(o, s, c)
def check_inputs(d):
    bad = []
    for k, lo, hi in (("opr", 0, 63), ("s0", 0, 63), ("f0", 0, 1023)):
        x = np.asarray(d[k]).astype(np.float64)
        if not (np.min(x) >= lo and np.max(x) <= hi): bad.append("range of " + k)
        elif np.any(x != np.floor(x)): bad.append("whole numbers of " + k)
    return bad
def reference(opr, s0, f0):
    o = opr.astype(np.float32).astype(np.int32).reshape(N, 8, 16, W); gi = np.arange(8)
    S = np.zeros((N, 8, D + 1, 16, P), np.int32); F = np.full((N, 8, D + 1, P), 1023, np.int32)
    S[:, :, 0] = s0.astype(np.float32).astype(np.int32).reshape(N, 8, 16, P); F[:, :, 0] = f0
    lo = np.zeros((8, D), np.int32); hi = np.zeros((8, D), np.int32); U = np.full(8, 1023, np.int32); lev = np.zeros(8, np.int32)
    for rnd in range(RO):
        s = S[:, gi, lev]; f = F[:, gi, lev]; low = lo[gi, lev][:, None]
        h = columns(mark(s), lev[:, None, None]).reshape(N, 8, 1, J * P)
        c = np.abs(np.tile(s, (1, 1, 1, J)) - np.take_along_axis(o, h.astype(np.int64), axis=3))
        fc = np.tile(f, (1, 1, J)) + (np.add.reduce(c, axis=2) >> 2); own = mark(c) & (N - 1)
        B = np.full(8, 1023, np.int32)
        for a in range(N):
            x = np.partition(np.where((fc >= low) & (own == a), fc, 4000), CAP, axis=2)[:, :, CAP]
            B = np.minimum(B, np.min(x, axis=0))
        keep = (fc >= low) & (fc < B[:, None])
        m = np.min(np.where(keep, fc, 4000), axis=(0, 2))
        ns = np.zeros((N, 8, 16, P), np.int32); nf = np.full((N, 8, P), 1023, np.int32)
        for a in range(N):
            k = keep & (own == a); place = np.add.accumulate(k, axis=2, dtype=np.int64) - 1
            qi, ji, ci = np.nonzero(k); t = qi * CAP + place[qi, ji, ci]
            ns[a, ji, :, t] = c[qi, ji, :, ci]; nf[a, ji, t] = fc[qi, ji, ci]
        S[:, gi, lev + 1] = ns; F[:, gi, lev + 1] = nf; hi[gi, lev] = B
        U = np.where(lev == D - 1, np.minimum(U, m), U)
        for g in range(8):
            e = int(lev[g])
            if e == D - 1 or m[g] >= U[g]:
                lo[g, e] = max(int(B[g]), int(lo[g, e]) + 1)
                if lo[g, e] >= U[g] and e > 0:
                    lo[g, e] = 0; e -= 1; lo[g, e] = max(int(hi[g, e]), int(lo[g, e]) + 1)
            else:
                e += 1; lo[g, e] = 0
            lev[g] = e
    yl = np.ascontiguousarray(S[:, :, 1:].transpose(0, 1, 3, 2, 4)).reshape(N, 128, D * P)
    yt = np.concatenate([lo, hi, lev[:, None], U[:, None]], axis=1)
    return {"yl": yl.astype(np.float32).astype(BF), "yf": np.ascontiguousarray(F[:, :, 1:]).reshape(N, 8, D * P).astype(np.float32), "yt": np.stack([yt] * N).astype(np.float32)}

@@ -1,0 +1,606 @@
+from concourse.bass import DstId, RemoteDMATransfer
+from concourse.mybir import AluOpType, AxisListType, ActivationFunctionType
+import comms_topo
+
+N, RO, J = 8, 8, 16
+HACT = 8
+WT = [1, 3, 7, 13, 21, 35, 49, 67, 85, 107, 129, 155, 181, 211, 241, 253]
+KA = [17, 101, 263, 389, 547, 701, 859, 1021, 1171, 1319, 1487, 1637, 1801, 1949, 2111, 2269]
+BF, F32, I32, U16 = "bfloat16", "float32", "int32", "uint16"
+_B = {
+    "OPR": (8192, BF), "CR": (4096, BF), "C": (4096, BF), "WIN": (2560, BF), "G": (512, BF), "SREP": (512, BF), "FP": (256, BF),
+    "M1": (3840, BF), "M2": (1792, BF), "OH": (2048, BF), "A": (4096, BF), "H": (4096, BF), "DB": (256, BF), "DC": (256, BF),
+    "KEP": (256, BF), "XR": (256, BF), "MK": (512, BF), "TOTB": (256, BF), "D": (256, BF), "E": (256, BF), "OH2": (128, BF),
+    "S1": (128, BF), "SEND": (1024, BF), "SC": (512, BF), "L1": (128, BF), "L2": (128, BF), "L3": (128, BF),
+    "OG": (512, BF), "XH": (256, BF), "XL": (256, BF),
+    "ONES": (256, BF), "Z128": (128, BF), "C32": (128, BF), "IDB": (128, BF), "TB1": (256, BF), "BLK": (128, BF), "W16": (16, BF),
+    "WF16": (16, BF), "LBW": (2048, BF), "LBR": (2048, BF), "LB1": (2048, BF), "LBE": (2048, BF), "TRIM": (128, BF), "NTB": (128, BF),
+    "I8R": (256, BF), "LE0": (256, BF), "LE1": (256, BF), "LI0": (256, BF), "LI1": (256, BF), "JS": (2048, BF),
+    "BD15": (64, BF), "ST15": (256, BF), "SR15": (128, BF), "BD7": (64, BF), "ST7": (256, BF), "SR7": (128, BF), "BR": (256, BF),
+    "ONE0": (128, BF), "OC": (128, BF), "D0": (128, BF), "IO256": (256, BF), "W81": (8, BF), "NID": (128, BF), "DEL": (256, BF),
+    "IDF": (128, F32), "G8T": (128, F32), "TREE": (128, F32), "I16": (16, F32), "I8": (8, F32), "WROW": (32, F32),
+    "KT": (256, F32), "KU": (256, F32), "LLAY": (32, F32), "DIFF": (32, F32), "ULST": (32, F32), "TR": (16, F32), "IO6": (6, F32),
+    "COL": (32, F32), "PCOL": (1, F32), "ST0": (8, F32), "ST1": (8, F32), "LW": (128, F32), "MS": (4, F32), "XB0": (32, F32), "XB1": (32, F32),
+    "CT": (64, F32), "MX": (4, F32), "MR": (4, F32), "TM": (256, F32), "YY": (128, F32), "CY": (17, F32), "PD": (64, F32),
+    "W2": (128, F32), "DS": (64, F32), "LT": (64, F32), "YF": (768, F32), "CHL": (64, F32),
+    "F0": (256, I32), "UI": (64, I32), "HI": (256, I32), "HM": (256, I32), "YI": (256, I32), "DM": (256, I32), "VI": (256, I32), "OI": (256, I32),
+    "RI": (256, I32), "RQ": (256, I32), "NI": (32, I32), "OW": (64, I32), "RC": (2, I32),
+    "OFFC": (256, U16), "D16": (256, U16), "O16": (256, U16), "KK16": (256, U16), "LIST": (32, U16), "UPL": (32, U16), "LN": (16, U16),
+    "LP": (16, U16), "DOFF": (16, U16), "REPL": (32, U16),
+}
+_PS = ["PT", "PU", "PC", "PI", "PR", "PX", "PL", "PY"]
+SCRATCH = {k: ("sbuf", [128, n], d) for k, (n, d) in _B.items()}
+SCRATCH.update({k: ("psum", [128, 512], F32) for k in _PS})
+SEMAPHORES = ["sv", "st", "sa", "sp", "dopr", "ds0", "df0", "dout", "rt", "lt", "rn", "ln"]
+OP, ACT, AX = AluOpType, ActivationFunctionType, AxisListType.X
+
+
+def rank_program(g, core, T, topo):
+    rank = T.rank_of(core)
+    if rank is None:
+        return
+    Q = {"v": g.vector, "t": g.tensor, "a": g.scalar, "p": g, "y": g.sync}
+    SEM = {"v": "sv", "t": "st", "a": "sa", "p": "sp"}
+    cnt = {"v": 0, "t": 0, "a": 0, "p": 0}
+    seen, lastw, readers = {}, {}, {}
+
+    def wait(e, sem, val):
+        if seen.get((e, sem), 0) < val:
+            Q[e].wait_ge(T.sem[sem], val)
+            seen[(e, sem)] = val
+
+    def before(e, reads, writes):
+        need = {}
+        own = SEM.get(e)
+
+        def add(s, v, skip_own):
+            if not (skip_own and s == own):
+                need[s] = max(need.get(s, 0), v)
+        for k in reads:
+            if k in lastw:
+                add(lastw[k][0], lastw[k][1], False)
+            if k in _PS:
+                for s, v in readers.get(k, {}).items():
+                    add(s, v, True)
+        for k in writes:
+            if k in lastw:
+                add(lastw[k][0], lastw[k][1], True)
+            for s, v in readers.get(k, {}).items():
+                add(s, v, e == "t")
+        for s, v in need.items():
+            wait(e, s, v)
+
+    def after(sem, val, reads, writes):
+        for k in writes:
+            lastw[k] = (sem, val)
+            readers[k] = {}
+        for k in reads:
+            readers.setdefault(k, {})[sem] = val
+
+    def R(name, a=None, b=None, s=None, p=None, key=None):
+        t = T[name]
+        ap = t[:, a:b:s] if p is None else t[0:p, a:b:s]
+        k = [name] if key is None else (key if isinstance(key, list) else [key])
+        return (k, ap)
+
+    def IND(w, o):
+        return (w[0] + o[0], w[1].indirect(o[1]))
+
+    def run(e, fn, outs, ins, *args, inc=True, **kw):
+        reads = [k for x in ins if isinstance(x, tuple) for k in x[0]]
+        writes = [k for x in outs for k in x[0]]
+        before(e, reads, writes)
+        u = [x[1] if isinstance(x, tuple) else x for x in list(outs) + list(ins)]
+        ins_ = fn(*u, *args, **kw)
+        if inc:
+            ins_.then_inc(T.sem[SEM[e]], 1)
+            cnt[e] += 1
+        after(SEM[e], cnt[e] + (0 if inc else 1), reads, writes)
+
+    V = g.vector
+
+    def ts(out, in0, s1, op0, s2=None, op1=None):
+        reads = [in0] + [x for x in (s1, s2) if isinstance(x, tuple)]
+        u1 = s1[1] if isinstance(s1, tuple) else s1
+        u2 = s2[1] if isinstance(s2, tuple) else s2
+        f = lambda o, i, *rest: (V.tensor_scalar(o, i, u1, u2, op0) if op1 is None else V.tensor_scalar(o, i, u1, u2, op0, op1))
+        run("v", f, [out], reads)
+
+    def tt(out, a, b, op):
+        run("v", V.tensor_tensor, [out], [a, b], op)
+
+    def cp(out, a):
+        run("v", V.tensor_copy, [out], [a])
+
+    def gath(out, win, offs):
+        run("v", V.tensor_copy, [out], [IND(win, offs)])
+
+    def scat(win, offs, src):
+        for k in win[0]:
+            wait("v", *lastw[k])
+        run("v", lambda o, i, x: V.tensor_copy(o, i), [(win[0], win[1].indirect(offs[1]))], [src, offs])
+
+    def fill(out, c, drain=False):
+        run("v", V.memset, [out], [], c)
+        if drain:
+            wait("v", "sv", cnt["v"])
+
+    def red(out, a, op):
+        run("v", V.tensor_reduce, [out], [a], AX, op)
+
+    def mm(out, lhsT, rhs, start, stop):
+        run("t", g.tensor.matmul, [out], [lhsT, rhs], start, stop, inc=stop)
+
+    def act(out, a, func, **kw):
+        col = kw.get("scale")
+        if isinstance(col, tuple):
+            kw["scale"] = col[1]
+            run("a", lambda o, i, c, f, **k: g.scalar.activation(o, i, f, **k), [out], [a, col], func, **kw)
+        else:
+            run("a", g.scalar.activation, [out], [a], func, **kw)
+
+    def sel(out, a, pat, op, base, cm):
+        run("p", g.affine_select, [out], [a], pat, op, 0.0, base, cm)
+
+    def iota(out, pat, base, cm):
+        run("p", g.iota, [out], [], pat, base, cm, allow_small_or_imprecise_dtypes=True)
+
+    C = lambda i: R("COL", i, i + 1, key="COL%d" % i)
+    ICOL, WCOL, RCOL, WE, AM8B, CF, ONEC, W81C = [C(i) for i in range(8)]
+
+    g.sync.dma_start(T.WIN[:, 0:256], T.s0[:, :]).then_inc(T.sem.ds0, 16)
+    lastw["L0S"] = ("ds0", 16)
+    for q in range(4):
+        g.sync.dma_start(T.OPR[32 * q:32 * q + 32, :], T.opr[32 * q:32 * q + 32, :]).then_inc(T.sem.dopr, 16)
+    lastw["OPR"] = ("dopr", 64)
+    fill(R("F0"), 0)
+    wait("a", "sv", cnt["v"])
+    g.scalar.dma_start(T.F0[0:128:16, :], T.f0[:, :]).then_inc(T.sem.df0, 16)
+    g.scalar.dma_start(T.F0[1:128:16, :], T.f0[:, :]).then_inc(T.sem.df0, 16)
+    lastw["F0"] = ("df0", 32)
+
+    fill(R("ONES"), 1.0)
+    fill(R("Z128"), 0.0)
+    ONES = lambda n: R("ONES", 0, n)
+    IO16, WROW = R("WROW", 16, 32, key="IO16"), R("WROW", 0, 16, key="WROW")
+    sel(R("TB1", 0, 128), ONES(128), [[-16, 8], [0, 16]], OP.is_ge, 0, 1)
+    sel(R("BLK"), R("TB1", 0, 128), [[16, 8], [0, 16]], OP.is_ge, 15, -1)
+    sel(R("IDB"), ONES(128), [[-1, 128]], OP.is_equal, 0, 1)
+    iota(IO16, [[1, 16]], 0, 0)
+    iota(R("LLAY"), [[16, 32]], 0, 0)
+    iota(R("DIFF"), [[32, 2], [64, 8], [16, 2]], 2048, 0)
+    iota(R("IO6"), [[0, 2], [1, 3]], 0, 0)
+    iota(R("PCOL"), [[0, 1]], 0, 1)
+    iota(R("ULST"), [[32, 8], [256, 2], [16, 2]], 0, 0)
+    iota(R("TR"), [[16, 16]], 512, 0)
+    sel(R("TRIM"), ONES(128), [[1, 128]], OP.is_gt, 0, -1)
+    sel(R("NTB"), R("BLK"), [[-1, 128]], OP.is_ge, 0, 1)
+    for i in range(16):
+        fill(R("WROW", i, i + 1, key="WROW"), float(WT[i]))
+    for j in range(J):
+        fill(R("KT", 16 * j, 16 * j + 16), float(KA[j]))
+    fill(ONEC, 1.0)
+    TRE = lambda a, b: R("TREE", a, b)
+    tt(TRE(0, 64), R("IDB", 0, 64), R("IDB", 64, 128), OP.add)
+    tt(TRE(64, 96), TRE(0, 32), TRE(32, 64), OP.add)
+    tt(R("I16"), TRE(64, 80), TRE(80, 96), OP.add)
+    tt(TRE(96, 112), TRE(64, 80), TRE(80, 96), OP.add)
+    tt(R("I8"), TRE(96, 104), TRE(104, 112), OP.add)
+    tt(TRE(0, 16), R("I16"), IO16, OP.mult)
+    red(ICOL, TRE(0, 16), OP.add)
+    tt(TRE(16, 32), R("I16"), WROW, OP.mult)
+    red(WCOL, TRE(16, 32), OP.add)
+
+    def lb(name, col):
+        fill(R(name), 0.0, True)
+        for q in range(8):
+            ts(R(name, 16 * q, 16 * q + 129 * 15 + 1, 129), R("BLK", 16 * q, 16 * q + 16), col, OP.mult)
+    lb("LBW", WCOL)
+    ts(R("REPL", 0, 16), R("Z128", 0, 16), ICOL, OP.add)
+    AL, BE = R("I16", 0, 1), R("I16", 1, 2)
+    ts(AM8B, BE, -8.0, OP.mult, AL, OP.add)
+    ts(CF, AL, 128.0, OP.mult, BE, OP.subtract)
+    ts(W81C, AL, 8.0, OP.mult, BE, OP.add)
+    ts(WE, W81C, 4.0, OP.mult)
+    cp(R("RC", 0, 1), WCOL)
+    ts(R("RC", 1, 2), R("RC", 0, 1), 7, OP.bitwise_and)
+    cp(RCOL, R("RC", 1, 2))
+    cp(R("W16", 0, None, 2), R("BLK", 0, None, 16))
+    ts(R("W16", 1, None, 2), R("BLK", 0, None, 16), RCOL, OP.mult)
+    fill(R("WF16"), 0.0, True)
+    ts(R("WF16", 0, None, 2), R("BLK", 0, None, 16), WE, OP.mult)
+    cp(R("I8R", 0, 8), R("I8"))
+    for n in (8, 16, 32, 64, 128):
+        cp(R("I8R", n, 2 * n), R("I8R", 0, n))
+
+    ts(R("HI"), R("F0"), 3, OP.arith_shift_right)
+    ts(R("HM"), R("F0"), 7, OP.bitwise_and)
+    ts(R("KEP"), R("HI"), AL, OP.mult)
+    ts(R("XR"), R("HM"), BE, OP.mult)
+    tt(R("WIN", 256, 512, key="L0F"), R("KEP"), R("XR"), OP.add)
+    fill(R("WIN", 512, 2048, key="LU"), 0.0, True)
+    for l in (1, 2, 3):
+        ts(R("WIN", 512 * l + 256, 512 * l + 512, key="LU"), ONES(256), CF, OP.mult)
+    fill(R("WIN", 2048, 2560, key="NEW"), 0.0)
+    WALL = R("WIN", key=["L0S", "L0F", "LU", "NEW"])
+    ts(R("LT", 0, 32), R("LLAY"), ICOL, OP.add)
+    tt(R("DIFF"), R("DIFF"), R("LLAY"), OP.subtract)
+    cp(R("LLAY"), R("LT", 0, 32))
+    cp(R("LIST"), R("LT", 0, 32))
+    LWn = {}
+
+    def L(name, n=1):
+        if name not in LWn:
+            LWn[name] = (sum(x[1] for x in LWn.values()), n)
+        a = LWn[name][0]
+        return R("LW", a, a + n, key="LW_" + name)
+    for nm in ("clo", "lod", "e811", "e512"):
+        fill(L(nm), 0.0)
+    fill(R("ST0", 0, 7, key=["ST0v", "ST0e"]), 0.0)
+    fill(R("ST0", 7, 8, key="ST0U"), 1023.0)
+    fill(R("G8T"), 1.0)
+    fill(R("C32"), 32.5)
+
+    def kmats(k, p):
+        for nm, w, n in (("BD", [[-k, 8], [0, 8]], 64), ("ST", [[0, 32], [-k, 8]], 256), ("SR", [[-k, 8], [0, 16]], 128)):
+            sel(R("TB1", 0, n, p=p), R("ONES", 0, n, p=p), w, OP.is_ge, 0, 1)
+            sel(R(nm + str(k), p=p), R("TB1", 0, n, p=p), [[-a, b] for a, b in w], OP.is_ge, k - 1, -1)
+    kmats(7, 56)
+    kmats(15, 120)
+    sel(R("G8T", p=8), R("G8T", p=8), [[-1, 8], [0, 16]], OP.is_equal, 0, 1)
+    for t in (0, 1):
+        sel(R("LE%d" % t), R("I8R"), [[8, 32], [0, 8]], OP.is_gt, -128 * t, -1)
+        sel(R("LI%d" % t), R("I8R"), [[8, 32], [0, 8]], OP.is_gt, 8 - 128 * t, -1)
+    iota(R("IO256"), [[1, 256]], 0, 0)
+    sel(R("ONE0"), ONES(128), [[0, 128]], OP.is_equal, 0, 1)
+    iota(R("OC"), [[64, 8], [0, 16]], 0, 0)
+    sel(R("D0"), ONES(128), [[0, 8], [1, 16]], OP.is_gt, 0, 0)
+
+    def late_constants():
+        ts(R("NID"), R("IDB"), -256.0, OP.mult)
+        tt(R("TRIM"), R("TRIM"), R("NID"), OP.add)
+        ts(R("NID"), R("IDB"), -1.0, OP.mult)
+        ts(R("NTB"), R("NTB"), -1.0, OP.mult)
+        cp(R("IDF"), R("IDB"))
+        ts(R("ULST"), R("ULST"), ICOL, OP.add)
+        ts(R("TR"), R("TR"), ICOL, OP.add)
+        fill(R("JS"), 0.0, True)
+        for q in range(8):
+            ts(R("JS", 16 * q, 16 * q + 129 * 15 + 1, 129), ONES(16), 128.0, OP.mult, R("I8", q, q + 1), OP.mult)
+        lb("LB1", ONEC)
+        act(R("LBR"), R("LB1"), ACT.Copy, scale=RCOL)
+        act(R("LBE"), R("LB1"), ACT.Copy, scale=WE)
+        cp(R("DEL", 0, 16), R("I16"))
+        for n in (16, 32, 64, 128):
+            cp(R("DEL", n, 2 * n), R("DEL", 0, n))
+        fill(R("BR"), 0.0, True)
+        for q in range(8):
+            for i in (0, 1):
+                cp(R("BR", 128 * i + 16 * q + i, 128 * i + 16 * q + i + 1), R("BLK", 16 * q, 16 * q + 1))
+        cp(R("REPL", 16, 32, key="REPA"), IO16)
+        ts(R("W81"), R("BLK", 0, None, 16), W81C, OP.mult)
+        fill(R("SC"), 0.0, True)
+        for o in range(8):
+            ts(R("SC", 64 * o + 32, 64 * o + 64), ONES(32), CF, OP.mult)
+        cp(R("H", 0, None, 16, key="H0"), ONES(256))
+        fill(R("CY", 16, 17, key="CY16"), 0.0)
+        fill(R("MS"), 0.0)
+
+    dests = [c for c in T.cores if c != core]
+    dests.sort(key=lambda c: len(topo.engines(core, c)))
+    used, plan = set(), []
+    for c in dests:
+        free = [x for x in topo.engines(core, c) if x not in used][:2]
+        used.update(free)
+        rid, pid, _s = topo.addr(c)
+        plan.append((c, DstId(rid=rid, pnc=pid), sum(1 << x for x in free), len(free)))
+    per = sum(x[3] for x in plan)
+
+    def to_all(src, dst, rsem, lsem):
+        g.remote_dma_fused([RemoteDMATransfer(dst_ids=[d], dma_engine_mask=m, remote_sem=T.sem[rsem], src=src(c), dst=dst)
+                            for c, d, m, _n in plan], local_sem=T.sem[lsem])
+
+    GS = R("G", 0, 256, key="GS")
+    GF = R("G", 256, 512, key="GF")
+    blocks = [(512 * c, 512) for c in range(7)] + [(3584, 256), (3840, 256)]
+    CALL = R("C", key=["C%d" % c for c in range(len(blocks))])
+
+    def update_half(h):
+        scat(R("WIN", 512, 2048, key="LU"), R("UPL", 16 * h, 16 * h + 16), R("WIN", 2048 + 256 * h, 2304 + 256 * h, key="NEW"))
+
+    for rnd in range(RO):
+        ST, SN = ("ST0", "ST1") if rnd % 2 == 0 else ("ST1", "ST0")
+        XB = "XB%d" % (rnd % 2)
+        if rnd:
+            wait("v", "rn", per * rnd)
+            wait("a", "rn", per * rnd)
+        gath(GS, WALL, R("LIST", 0, 16))
+        for b in range(16):
+            mm(R("PU", 0, 16), R("LBW", 128 * b, 128 * b + 128), R("G", b, 256, 16, key="GS"), b == 0, b == 15)
+        act(R("SREP", 0, 256, key="SR0"), GS, ACT.Copy)
+        act(R("SREP", 256, 512, key="SR1"), GS, ACT.Copy)
+        act(GF, IND(WALL, R("LIST", 16, 32)), ACT.Copy)
+        ui, um, sq, s4 = [R("UI", 16 * k, 16 * k + 16, key="UI%d" % k) for k in range(4)]
+        cp(ui, R("PU", 0, 16))
+        ts(um, ui, 4095, OP.bitwise_and)
+        tt(sq, um, um, OP.mult)
+        ts(s4, sq, 4, OP.arith_shift_right)
+        ts(sq, s4, L("e811"), OP.add)
+        tt(R("KU"), IND(um, R("REPL", 0, 16)), R("KT"), OP.mult)
+        tt(R("HI"), IND(sq, R("REPL", 0, 16)), R("KU"), OP.add)
+        ts(R("HM"), R("HI"), 8191, OP.bitwise_and)
+        cp(R("OFFC"), R("HM"))
+        ts(R("FP"), GF, L("lod"), OP.subtract)
+        if rnd == 0:
+            late_constants()
+            act(R("SEND", 0, 512), R("SC"), ACT.Copy)
+        SR = lambda n: R("SREP", 0, n, key=["SR0", "SR1"])
+        act(R("OG"), IND(R("OPR"), R("OFFC", 128, 160)), ACT.Copy)
+        for c, (a, n) in enumerate(blocks):
+            cr = R("CR", a, a + n, key="CR%d" % c)
+            if c == 4:
+                cr = R("PX")
+            else:
+                tt(cr, IND(R("OPR"), R("OFFC", a // 16, (a + n) // 16)), SR(n), OP.subtract)
+            act(R("C", a, a + n, key="C%d" % c), cr, ACT.Abs)
+            if c == 0:
+                mm(R("PX"), R("IDB"), SR(512), True, False)
+                mm(R("PX"), R("NID"), R("OG"), False, True)
+            for x in range(a // 128, (a + n) // 128):
+                o = R("PT", 16 * x, 16 * x + 16)
+                mm(o, R("FP", 128 * (x % 2), 128 * (x % 2) + 128), R("WF16"), True, False)
+                mm(o, R("C", 128 * x, 128 * x + 128, key="C%d" % c), R("W16"), False, True)
+        if rnd:
+            wait("a", "ln", per * rnd)
+            act(R("SEND", 0, 512), R("SC"), ACT.Copy)
+        cp(R("YI"), R("PT", 0, None, 2))
+        cp(R("VI"), R("PT", 1, None, 2))
+        ts(R("DM"), R("YI"), 2, OP.arith_shift_right, 4095, OP.bitwise_and)
+        ts(R("OI"), R("VI"), 7, OP.bitwise_and)
+        cp(R("D16"), R("DM"))
+        cp(R("O16"), R("OI"))
+
+        def half(name, k, K, h, tag):
+            return R(name, 128 * K * h + k, 128 * K * (h + 1), K, key="%s%s%d" % (name, tag, h))
+
+        def cols(name, h):
+            return R(name, 128 * h, 128 * h + 128)
+
+        def digit(K, Lx, step):
+            p = 8 * K
+            tt(R("CT", p=p), R("PC", 0, 64, p=p), R("BD%d" % K, p=p), OP.mult)
+            red(R("MX", 0, 1, p=p), R("CT", p=p), OP.max)
+            ts(R(Lx, p=p), R("C32", p=p), R("MX", 0, 1, p=p), OP.is_ge, float(step), OP.mult)
+            mm(R("PI", 0, 256), R(Lx, p=p), R("ST%d" % K, p=p), True, True)
+
+        def masks(K, M, src, step, na):
+            for h in (0, 1):
+                for k in range(K - na, K):
+                    act(half(M, k, K, h, "a"), cols(src, h), ACT.Sigmoid, scale=-1000.0, bias=1000.0 * step * (k + 1) - 500.0)
+                for k in range(K - na):
+                    ts(half(M, k, K, h, "v"), cols(src, h), float(step * (k + 1)), OP.is_lt)
+                if na == 0:
+                    for o in range(8):
+                        ts(half("OH", o, 8, h, "v"), cols("O16", h), float(o), OP.is_equal)
+            for x in range(32):
+                h = x // 16
+                mm(R("PC", 0, 64, p=8 * K), R(M, 8 * K * x, 8 * K * x + 8 * K, key=["%sv%d" % (M, h), "%sa%d" % (M, h)]),
+                   R("OH", 64 * x, 64 * x + 64, key="OHv%d" % h), x == 0, x == 31)
+        masks(7, "M2", "D16", 128, 0)
+        TM = lambda a, b, k=None: R("TM", a, b, key="TM%d" % (a if k is None else k))
+        tt(TM(0, 128), R("DM", 0, 128), R("DM", 128, 256), OP.min)
+        tt(TM(128, 192), TM(0, 64, 0), TM(64, 128, 0), OP.min)
+        tt(TM(192, 224), TM(128, 160, 128), TM(160, 192, 128), OP.min)
+        tt(TM(224, 240), TM(192, 208, 192), TM(208, 224, 192), OP.min)
+        tt(TM(240, 248), TM(224, 232, 224), TM(232, 240, 224), OP.min)
+        digit(7, "L1", 128)
+        run("t", g.tensor.transpose, [R("PU", 0, 128, p=8)], [TM(240, 248), R("IDF")])
+        tt(R("DB"), R("DM"), R("PI", 0, 256), OP.subtract)
+        masks(15, "M1", "DB", 8, 4)
+        red(R("MR", 0, 1, p=8), R("PU", 0, 128, p=8), OP.min)
+        if rnd:
+            update_half(0)
+        digit(15, "L2", 8)
+        mm(R("PU", 1, 2), R("G8T", p=8), R("MR", 0, 1, p=8), True, True)
+        tt(R("DC"), R("DB"), R("PI", 0, 256), OP.subtract)
+        masks(7, "M2", "DC", 1, 2)
+        if rnd:
+            update_half(1)
+        digit(7, "L3", 1)
+        mm(R("PU", 0, 1), R("SR7", p=56), R("L1", 0, 1, p=56), True, False)
+        mm(R("PU", 0, 1), R("SR15", p=120), R("L2", 0, 1, p=120), False, False)
+        mm(R("PU", 0, 1), R("SR7", p=56), R("L3", 0, 1, p=56), False, True)
+        tt(R("KEP"), R("DC"), R("PI", 0, 256), OP.is_lt)
+        if rnd:
+            wait("v", "lt", per * rnd)
+        cp(R("MS", 0, 2), R("PU", 0, 2))
+        act(R(XB, 4 * rank, 4 * rank + 2), R("MS", 0, 2), ACT.Copy)
+        before("p", ["MS"], ["NEW", "LU"])
+        to_all(lambda c: T.MS[:, 0:4], T[XB][:, 4 * rank:4 * rank + 4], "rt", "lt")
+        for t in (0, 1):
+            mm(R("PL", t, t + 1), R("KEP", 128 * t, 128 * t + 128), ONES(1), True, True)
+        mm(R("PR", 0, 256), R("TRIM"), R("KEP"), True, False)
+        for t in (0, 1):
+            ts(R("TOTB", 128 * t, 128 * t + 128, key="TOT%d" % t), R("Z128"), R("PL", t, t + 1), OP.add)
+        for t in (0, 1):
+            mm(R("PR", 0, 256), R("TOTB", 128 * t, 128 * t + 128, key="TOT%d" % t), R("LE%d" % t), False, t == 1)
+        mm(R("PY", 0, 1), R("LI0", 0, 128), R("TOTB", 0, 1, key="TOT0"), True, True)
+        mm(R("PY", 1, 2), R("LI0", 128, 256), R("TOTB", 0, 1, key="TOT0"), True, False)
+        mm(R("PY", 1, 2), R("LI1", 128, 256), R("TOTB", 128, 129, key="TOT1"), False, True)
+        cp(R("RI"), R("PR", 0, 256))
+        act(R("XR"), R("PR", 0, 256), ACT.Copy)
+        for t in (0, 1):
+            ts(R("MK", 256 * t, 256 * t + 256, key="MK%d" % t), R("IO256"), R("PY", t, t + 1), OP.is_ge)
+        for t in (0, 1):
+            for k in range(16):
+                mm(R("PL", 0, 16), R("JS", 128 * k, 128 * k + 128), R("MK", 256 * t + k, 256 * t + 256, 16, key="MK%d" % t), t == 0 and k == 0, t == 1 and k == 15)
+        ts(R("RQ"), R("RI"), 527, OP.bitwise_and)
+        cp(R("KK16"), R("RQ"))
+        for h in (0, 1):
+            for c in range(16 - HACT, 16):
+                act(half("H", c, 16, h, "a"), cols("XR", h), ACT.Sigmoid, scale=1000.0, bias=-1000.0 * (16 * c - 256) + 500.0)
+            for c in range(16):
+                ts(half("A", c, 16, h, "v"), cols("KK16", h), float(512 + c), OP.is_equal, R("PCOL"), OP.mult)
+            for c in range(1, 16 - HACT):
+                ts(half("H", c, 16, h, "v"), cols("XR", h), float(16 * c - 256), OP.is_ge)
+        for x in range(32):
+            h = x // 16
+            mm(R("PX", 0, 128), R("A", 128 * x, 128 * x + 128, key="Av%d" % h), R("H", 128 * x, 128 * x + 128, key=["H0", "Ha%d" % h, "Hv%d" % h]), x == 0, x == 31)
+        wait("v", "rt", per * (rnd + 1))
+        red(L("TG"), R(XB, 0, None, 4), OP.min)
+        red(L("MG"), R(XB, 1, None, 4), OP.min)
+        clo, e, U = L("clo"), R(ST, 6, 7, key=ST + "e"), R(ST, 7, 8, key=ST + "U")
+        eN, UN = R(SN, 6, 7, key=SN + "e"), R(SN, 7, 8, key=SN + "U")
+        ts(L("B"), L("TG"), clo, OP.add, 1023.0, OP.min)
+        ts(L("m"), L("MG"), clo, OP.add)
+        lev = []
+        lts = lambda *x: lev.append((ts, x))
+        ltt = lambda *x: lev.append((tt, x))
+
+        def pump(k):
+            for f, x in lev[:k]:
+                f(*x)
+            del lev[:k]
+        lts(L("e2"), e, 2.0, OP.is_equal)
+        lts(L("ne2"), e, 2.0, OP.is_lt)
+        lts(L("g0"), e, 0.0, OP.is_gt)
+        lts(L("el", 6), R("IO6"), e, OP.is_equal)
+        lts(L("e512"), e, 512.0, OP.mult)
+        lts(L("nlo"), clo, 1.0, OP.add, L("B"), OP.max)
+        lts(L("ea"), L("m"), L("B"), OP.is_lt, L("e2"), OP.mult)
+        lts(L("nel", 6), L("el", 6), -1.0, OP.mult, 1.0, OP.add)
+        lts(L("q"), L("ea"), -4096.0, OP.mult, 4096.0, OP.add)
+        ltt(L("t1", 6), R(ST, 0, 6, key=ST + "v"), L("nel", 6), OP.mult)
+        lts(UN, L("m"), L("q"), OP.add, U, OP.min)
+        lts(R("UPL"), R("ULST"), L("e512"), OP.add)
+        ltt(L("mbu"), L("B"), UN, OP.min)
+        lts(L("bk0"), L("nlo"), UN, OP.is_ge, L("g0"), OP.mult)
+        lts(L("adv"), L("m"), L("mbu"), OP.is_lt, L("ne2"), OP.mult)
+        lts(L("nadv"), L("adv"), -1.0, OP.mult, 1.0, OP.add)
+        lts(L("va"), clo, L("adv"), OP.mult)
+        ltt(L("back"), L("bk0"), L("nadv"), OP.mult)
+        ltt(L("stay"), L("nadv"), L("back"), OP.subtract)
+        lts(eN, e, L("adv"), OP.add, L("back"), OP.subtract)
+        ltt(L("ch"), L("adv"), L("back"), OP.add)
+        lts(L("val"), L("nlo"), L("stay"), OP.mult, L("va"), OP.add)
+        L("t2", 6)
+        L("t3", 6)
+        a2, ae, a3 = LWn["t2"][0], LWn["el"][0], LWn["t3"][0]
+        ELS = R("LW", ae, ae + 3, key="LW_el")
+        lts(R("LW", a2, a2 + 3, key="LW_t2"), ELS, L("val"), OP.mult)
+        lts(R("LW", a2 + 3, a2 + 6, key="LW_t2"), ELS, L("B"), OP.mult)
+        ltt(L("t3", 6), L("t1", 6), L("t2", 6), OP.add)
+        lts(L("en", 3), R("IO6", 0, 3), eN, OP.is_equal)
+        lo1, hi1 = R("LW", a3, a3 + 3, key="LW_t3"), R("LW", a3 + 3, a3 + 6, key="LW_t3")
+        lts(L("w1", 3), lo1, 1.0, OP.add)
+        lts(L("enc", 3), L("en", 3), L("ch"), OP.mult)
+        ltt(L("w2", 3), L("w1", 3), hi1, OP.max)
+        lts(L("nen", 3), L("enc", 3), -1.0, OP.mult, 1.0, OP.add)
+        lts(L("w3", 3), L("w2", 3), L("back"), OP.mult)
+        ltt(L("w4", 3), lo1, L("nen", 3), OP.mult)
+        ltt(L("w5", 3), L("w3", 3), L("enc", 3), OP.mult)
+        ltt(R(SN, 0, 3, key=SN + "v"), L("w4", 3), L("w5", 3), OP.add)
+        lev.append((cp, (R(SN, 3, 6, key=SN + "v"), hi1)))
+        lts(L("e811"), eN, 811.0, OP.mult)
+        lts(L("p1"), eN, 512.0, OP.mult, L("nadv"), OP.mult)
+        lts(R("LT", 0, 32), R("DIFF"), L("adv"), OP.mult, L("p1"), OP.add)
+        ltt(R("LT", 32, 64), R("LLAY"), R("LT", 0, 32), OP.add)
+        lev.append((cp, (R("LIST"), R("LT", 32, 64))))
+        ltt(L("w6", 3), L("en", 3), R(SN, 0, 3, key=SN + "v"), OP.mult)
+        lev.append((red, (clo, L("w6", 3), OP.add)))
+        lts(R("RC", 0, 1), clo, 0.125, OP.mult)
+        lts(L("x1"), R("RC", 0, 1), AM8B, OP.mult)
+        lts(L("lod"), clo, BE, OP.mult, L("x1"), OP.add)
+        pump(8)
+        tt(R("YY"), R("PX", 0, 128), R("BLK"), OP.mult)
+        pump(1)
+        tt(TRE(0, 64), R("YY", 0, 64), R("YY", 64, 128), OP.add)
+        pump(1)
+        tt(TRE(64, 96), TRE(0, 32), TRE(32, 64), OP.add)
+        pump(1)
+        tt(R("CY", 0, 16), TRE(64, 80), TRE(80, 96), OP.add)
+        pump(1)
+        PD = [R("PD", 16 * k, 16 * k + 16, key="PD%d" % k) for k in range(3)]
+        tt(PD[0], R("CY", 0, 16), R("CY", 1, 17, key=["CY", "CY16"]), OP.subtract)
+        pump(1)
+        tt(PD[1], PD[0], R("PL", 0, 16), OP.add)
+        ts(R("LN"), PD[1], 4095.0, OP.min)
+        NI = [R("NI", 16 * k, 16 * k + 16, key="NI%d" % k) for k in range(2)]
+        cp(NI[0], PD[1])
+        gath(R("D"), CALL, R("LN"))
+        for b in range(16):
+            mm(R("PL", 0, 16), R("LBR", 128 * b, 128 * b + 128), R("D", b, 256, 16), b == 0, b == 15)
+        for b in range(16):
+            mm(R("PC", 0, 16), R("LB1", 128 * b, 128 * b + 128), R("D", b, 256, 16), b == 0, False)
+        ts(NI[1], NI[0], 255, OP.bitwise_and)
+        pump(1)
+        cp(R("LP"), NI[1])
+        act(R("E"), IND(GF, R("LP")), ACT.Copy)
+        for b in range(16):
+            mm(R("PC", 0, 16), R("LBE", 128 * b, 128 * b + 128), R("E", b, 256, 16), False, b == 15)
+        ts(PD[2], PD[1], 4096.0, OP.is_ge, 4096.0, OP.mult)
+        ow = [R("OW", 16 * k, 16 * k + 16, key="OW%d" % k) for k in range(4)]
+        pump(2)
+        cp(ow[0], R("PL", 0, 16))
+        pump(2)
+        ts(ow[1], ow[0], 7, OP.bitwise_and)
+        pump(4)
+        cp(ow[2], R("PC", 0, 16))
+        pump(1)
+        ts(ow[3], ow[2], 2, OP.arith_shift_right)
+        dsx = [R("DS", 16 * k, 16 * k + 16, key="DS%d" % k) for k in range(4)]
+        pump(1)
+        tt(dsx[0], ow[3], PD[2], OP.add)
+        ts(ow[0], ow[3], 3, OP.arith_shift_right)
+        ts(dsx[1], dsx[0], L("B"), OP.is_lt, 8.0, OP.mult)
+        ts(ow[2], ow[3], 7, OP.bitwise_and)
+        tt(dsx[2], ow[1], dsx[1], OP.subtract)
+        CHL = [R("CHL", 16 * k, 16 * k + 16, key="CHL%d" % k) for k in range(2)]
+        cp(CHL[0], ow[0])
+        for o in range(8):
+            ts(R("OH2", 16 * o, 16 * o + 16), dsx[2], float(o - 8), OP.is_equal)
+        cp(CHL[1], ow[2])
+        run("v", V.tensor_tensor_scan, [R("S1")], [R("D0"), R("OH2")], 0.0, OP.mult, OP.add)
+        mm(R("PR", 0, 128), R("NTB"), R("OH2"), True, False)
+        mm(R("PR", 0, 128), R("ONE0"), R("OC"), False, False)
+        mm(R("PR", 0, 128), R("BLK"), R("S1"), False, True)
+        ts(dsx[0], dsx[2], 0.0, OP.is_ge)
+        REPA = R("REPL", 16, 32, key="REPA")
+        tt(R("XH"), IND(CHL[0], REPA), R("DEL"), OP.mult)
+        tt(dsx[3], dsx[0], R("TR"), OP.mult)
+        tt(R("W2"), R("PR", 0, 128), R("OH2"), OP.mult)
+        pump(1)
+        tt(TRE(0, 64), R("W2", 0, 64), R("W2", 64, 128), OP.add)
+        pump(1)
+        tt(TRE(64, 96), TRE(0, 32), TRE(32, 64), OP.add)
+        pump(1)
+        tt(TRE(96, 112), TRE(64, 80), TRE(80, 96), OP.add)
+        pump(1)
+        tt(dsx[1], TRE(96, 112), dsx[3], OP.add)
+        tt(R("XL"), IND(CHL[1], REPA), R("DEL"), OP.mult)
+        mm(R("PY", 0, 256), R("BR", 0, 128), R("XH"), True, False)
+        mm(R("PY", 0, 256), R("BR", 128, 256), R("XL"), False, True)
+        act(R("E"), R("PY", 0, 256), ACT.Copy)
+        cp(R("DOFF"), dsx[1])
+        pump(1)
+        scat(R("SEND"), R("DOFF"), R("D"))
+        scat(R("SEND", 32, 1024), R("DOFF"), R("E"))
+        act(R("WIN", 2048 + 64 * rank, 2112 + 64 * rank, key="NEW"), R("SEND", 64 * rank, 64 * rank + 64), ACT.Copy)
+        before("p", ["SEND"], [])
+        to_all(lambda c: T.SEND[:, 64 * T.rank_of(c):64 * T.rank_of(c) + 64], T.WIN[:, 2048 + 64 * rank:2112 + 64 * rank], "rn", "ln")
+        pump(99)
+
+    wait("v", "rn", per * RO)
+    scat(R("WIN", 512, 2048, key="LU"), R("UPL"), R("WIN", 2048, 2560, key="NEW"))
+    before("y", ["LU"], [])
+    for l in (1, 2, 3):
+        g.sync.dma_start(T.yl[:, 256 * (l - 1):256 * l], T.WIN[:, 512 * l:512 * l + 256]).then_inc(T.sem.dout, 16)
+        o = R(("PT", "PX", "PY")[l - 1], 0, 256, p=8)
+        mm(o, R("W81"), R("WIN", 512 * l + 256, 512 * l + 512, key="LU"), True, True)
+        cp(R("YF", 256 * (l - 1), 256 * l, p=8), o)
+    SF = "ST%d" % (RO % 2)
+    before("y", ["YF", SF + "v", SF + "e", SF + "U"], [])
+    g.sync.dma_start(T.yf[:, :], T.YF[0:8, :]).then_inc(T.sem.dout, 16)
+    g.sync.dma_start(T.yt[:, :], T[SF][0:128:16, :]).then_inc(T.sem.dout, 16)
+    for sem, val in (("dout", 80), ("lt", per * RO), ("ln", per * RO), ("sv", cnt["v"]), ("st", cnt["t"]), ("sa", cnt["a"]), ("sp", cnt["p"])):
+        g.wait_ge(T.sem[sem], val)

@@ -3,35 +3,46 @@ from concourse.mybir import AluOpType, AxisListType, ActivationFunctionType
 import comms_topo
 
 N, RO, J = 8, 8, 16
-HACT = 8
+HACT = 10
+MACT = ((2, 7), (5, 5), (2, 2))
 WT = [1, 3, 7, 13, 21, 35, 49, 67, 85, 107, 129, 155, 181, 211, 241, 253]
 KA = [17, 101, 263, 389, 547, 701, 859, 1021, 1171, 1319, 1487, 1637, 1801, 1949, 2111, 2269]
+M1, M8 = 1.5 * 2 ** 23, 1.5 * 2 ** 26
+EPS = 2.0 ** -10
 BF, F32, I32, U16 = "bfloat16", "float32", "int32", "uint16"
 _B = {
-    "OPR": (8192, BF), "CR": (4096, BF), "C": (4096, BF), "WIN": (2560, BF), "G": (512, BF), "SREP": (512, BF), "FP": (256, BF),
-    "M1": (3840, BF), "M2": (1792, BF), "OH": (2048, BF), "A": (4096, BF), "H": (4096, BF), "DB": (256, BF), "DC": (256, BF),
-    "KEP": (256, BF), "XR": (256, BF), "MK": (512, BF), "TOTB": (256, BF), "D": (256, BF), "E": (256, BF), "OH2": (128, BF),
-    "S1": (128, BF), "SEND": (1024, BF), "SC": (512, BF), "L1": (128, BF), "L2": (128, BF), "L3": (128, BF),
-    "OG": (512, BF), "XH": (256, BF), "XL": (256, BF),
-    "ONES": (256, BF), "Z128": (128, BF), "C32": (128, BF), "IDB": (128, BF), "TB1": (256, BF), "BLK": (128, BF), "W16": (16, BF),
-    "WF16": (16, BF), "LBW": (2048, BF), "LBR": (2048, BF), "LB1": (2048, BF), "LBE": (2048, BF), "TRIM": (128, BF), "NTB": (128, BF),
-    "I8R": (256, BF), "LE0": (256, BF), "LE1": (256, BF), "LI0": (256, BF), "LI1": (256, BF), "JS": (2048, BF),
-    "BD15": (64, BF), "ST15": (256, BF), "SR15": (128, BF), "BD7": (64, BF), "ST7": (256, BF), "SR7": (128, BF), "BR": (256, BF),
-    "ONE0": (128, BF), "OC": (128, BF), "D0": (128, BF), "IO256": (256, BF), "W81": (8, BF), "NID": (128, BF), "DEL": (256, BF),
-    "IDF": (128, F32), "G8T": (128, F32), "TREE": (128, F32), "I16": (16, F32), "I8": (8, F32), "WROW": (32, F32),
-    "KT": (256, F32), "KU": (256, F32), "LLAY": (32, F32), "DIFF": (32, F32), "ULST": (32, F32), "TR": (16, F32), "IO6": (6, F32),
-    "COL": (32, F32), "PCOL": (1, F32), "ST0": (8, F32), "ST1": (8, F32), "LW": (128, F32), "MS": (4, F32), "XB0": (32, F32), "XB1": (32, F32),
-    "CT": (64, F32), "MX": (4, F32), "MR": (4, F32), "TM": (256, F32), "YY": (128, F32), "CY": (17, F32), "PD": (64, F32),
-    "W2": (128, F32), "DS": (64, F32), "LT": (64, F32), "YF": (768, F32), "CHL": (64, F32),
-    "F0": (256, I32), "UI": (64, I32), "HI": (256, I32), "HM": (256, I32), "YI": (256, I32), "DM": (256, I32), "VI": (256, I32), "OI": (256, I32),
-    "RI": (256, I32), "RQ": (256, I32), "NI": (32, I32), "OW": (64, I32), "RC": (2, I32),
-    "OFFC": (256, U16), "D16": (256, U16), "O16": (256, U16), "KK16": (256, U16), "LIST": (32, U16), "UPL": (32, U16), "LN": (16, U16),
-    "LP": (16, U16), "DOFF": (16, U16), "REPL": (32, U16),
+    "OPR": (8192, BF), "CR": (4096, BF), "C": (4096, BF), "WS": (2560, BF), "WC": (2560, BF), "SREP": (512, BF), "FP": (272, BF),
+    "MA": (3840, BF), "MB": (1792, BF), "OH": (2048, BF), "A": (4096, BF), "H": (4096, BF), "OG": (1024, BF),
+    "D1": (256, BF), "DB": (256, BF), "DC": (256, BF), "OK": (256, BF), "F": (256, BF), "KEP": (256, BF), "ZR": (256, BF), "BR": (256, BF),
+    "MK": (512, BF), "TOTB": (256, BF), "D": (256, BF), "E": (256, BF), "E2": (256, BF), "OH2": (144, BF), "LT2": (256, BF),
+    "SEND": (512, BF), "SENDC": (512, BF), "SC": (256, BF), "L1": (128, BF), "L2": (128, BF), "L3": (128, BF), "LQ": (128, BF),
+    "YL": (768, BF), "YC": (768, BF),
+    "ONES": (256, BF), "Z256": (256, BF), "C32": (128, BF), "C24": (128, BF), "IDB": (128, BF), "NID": (128, BF), "TB1": (256, BF), "TB2": (256, BF),
+    "BLK": (128, BF), "W16": (16, BF), "W4": (16, BF), "WE4": (16, BF), "WF": (256, BF), "CST": (256, BF), "LBW": (144, BF), "JS": (144, BF),
+    "TRIM": (128, BF), "TRI2": (128, BF), "I8R": (256, BF), "LE0": (256, BF), "LE1": (256, BF), "LI0": (256, BF), "LI1": (256, BF),
+    "BD15": (64, BF), "ST15": (256, BF), "SR15": (128, BF), "BD7": (64, BF), "ST7": (256, BF), "SR7": (128, BF),
+    "OC2": (144, BF), "IOT2": (144, BF), "D0": (144, BF), "IO256": (256, BF), "W81": (8, BF), "DEL": (256, BF), "RA": (8, BF), "IK": (128, BF),
+    "ROWI": (128, BF), "J16": (16, F32),
+    "IDF": (128, F32), "ONEF": (128, F32), "G8F": (128, F32), "TREE": (128, F32), "I16": (16, F32), "I8": (8, F32), "VEC": (80, F32),
+    "KT": (256, F32), "KU": (256, F32), "Y0": (256, F32), "ZO": (256, F32), "SBASE": (32, F32), "IO9": (12, F32), "SELA": (16, F32), "RB": (32, F32),
+    "COL": (32, F32), "ST0": (11, F32), "ST1": (11, F32), "LW": (128, F32), "MS": (4, F32), "XB0": (32, F32), "XB1": (32, F32),
+    "MX": (4, F32), "MJ": (16, F32), "PXS": (136, F32), "PLS": (16, F32), "PD": (32, F32), "KQ": (64, F32), "S2": (144, F32), "YF": (768, F32),
+    "F0": (256, I32), "UT": (160, I32), "UI": (48, I32), "HI": (256, I32), "HM": (256, I32), "NI": (32, I32), "RC": (2, I32), "MI": (1, I32),
+    "OFFC": (256, U16), "SLIST": (32, U16), "ULIST": (2, U16), "LN": (16, U16), "LP": (16, U16), "DOFF": (16, U16), "REPL": (16, U16),
+    "LAB": (4, U16), "L9": (10, U16), "L16": (16, U16), "OLIST": (48, U16),
 }
-_PS = ["PT", "PU", "PC", "PI", "PR", "PX", "PL", "PY"]
+_PS = ["PT0", "PT1", "PU", "PC", "PI", "PR", "PX", "PL"]
+_JOIN = {"ORD": ("LE0", "LE1", "LI0", "LI1"), "KM": ("ST15", "ST7", "SR15", "SR7", "BD15", "BD7"), "WTS": ("W16", "W4", "WE4", "W81", "RA")}
+_AT = {k: (k, 0, n) for k, (n, d) in _B.items()}
+for _k, _names in _JOIN.items():
+    _B[_k] = (0, BF)
+    for _x in _names:
+        _AT[_x] = (_k, _B[_k][0], _B[_x][0])
+        _B[_k] = (_B[_k][0] + _B.pop(_x)[0], BF)
+_AT.update({k: (k, 0, 512) for k in _PS})
 SCRATCH = {k: ("sbuf", [128, n], d) for k, (n, d) in _B.items()}
 SCRATCH.update({k: ("psum", [128, 512], F32) for k in _PS})
-SEMAPHORES = ["sv", "st", "sa", "sp", "dopr", "ds0", "df0", "dout", "rt", "lt", "rn", "ln"]
+SEMAPHORES = ["sv", "st", "sa", "sp", "dopr", "ds0", "df0", "dout", "rt", "lt", "rn", "ln", "rc", "lc"]
 OP, ACT, AX = AluOpType, ActivationFunctionType, AxisListType.X
 
 
@@ -42,7 +53,7 @@ def rank_program(g, core, T, topo):
     Q = {"v": g.vector, "t": g.tensor, "a": g.scalar, "p": g, "y": g.sync}
     SEM = {"v": "sv", "t": "st", "a": "sa", "p": "sp"}
     cnt = {"v": 0, "t": 0, "a": 0, "p": 0}
-    seen, lastw, readers = {}, {}, {}
+    seen, log = {}, {}
 
     def wait(e, sem, val):
         if seen.get((e, sem), 0) < val:
@@ -50,38 +61,28 @@ def rank_program(g, core, T, topo):
             seen[(e, sem)] = val
 
     def before(e, reads, writes):
-        need = {}
-        own = SEM.get(e)
-
-        def add(s, v, skip_own):
-            if not (skip_own and s == own):
-                need[s] = max(need.get(s, 0), v)
-        for k in reads:
-            if k in lastw:
-                add(lastw[k][0], lastw[k][1], False)
-            if k in _PS:
-                for s, v in readers.get(k, {}).items():
-                    add(s, v, True)
-        for k in writes:
-            if k in lastw:
-                add(lastw[k][0], lastw[k][1], True)
-            for s, v in readers.get(k, {}).items():
-                add(s, v, e == "t")
+        need, own = {}, SEM.get(e)
+        for names, wr in ((reads, False), (writes, True)):
+            for name, m in names:
+                for m2, w2, s, v in log.get(name, ()):
+                    bank = name in _PS and s != own
+                    if (bank or (m & m2 and (wr or w2))) and not (e == "t" and s == own):
+                        need[s] = max(need.get(s, 0), v)
         for s, v in need.items():
             wait(e, s, v)
 
     def after(sem, val, reads, writes):
-        for k in writes:
-            lastw[k] = (sem, val)
-            readers[k] = {}
-        for k in reads:
-            readers.setdefault(k, {})[sem] = val
+        for name, m in writes:
+            log[name] = [x for x in log.get(name, ()) if x[0] & ~m] + [(m, True, sem, val)]
+        for name, m in reads:
+            log[name] = [x for x in log.get(name, ()) if x[1] or x[2] != sem or x[0] & ~m] + [(m, False, sem, val)]
 
-    def R(name, a=None, b=None, s=None, p=None, key=None):
-        t = T[name]
-        ap = t[:, a:b:s] if p is None else t[0:p, a:b:s]
-        k = [name] if key is None else (key if isinstance(key, list) else [key])
-        return (k, ap)
+    def R(name, a=None, b=None, s=None, p=None):
+        name, at, n = _AT[name]
+        cols = range(at, at + n)[a:b:s]
+        m = ((1 << len(cols)) - 1) << cols[0] if s is None else sum(1 << c for c in cols)
+        a, b = cols[0], cols[-1] + 1
+        return ([(name, m)], T[name][:, a:b:s] if p is None else T[name][0:p, a:b:s])
 
     def IND(w, o):
         return (w[0] + o[0], w[1].indirect(o[1]))
@@ -112,179 +113,221 @@ def rank_program(g, core, T, topo):
     def cp(out, a):
         run("v", V.tensor_copy, [out], [a])
 
-    def gath(out, win, offs):
-        run("v", V.tensor_copy, [out], [IND(win, offs)])
-
     def scat(win, offs, src):
-        for k in win[0]:
-            wait("v", *lastw[k])
         run("v", lambda o, i, x: V.tensor_copy(o, i), [(win[0], win[1].indirect(offs[1]))], [src, offs])
 
-    def fill(out, c, drain=False):
+    def fill(out, c):
         run("v", V.memset, [out], [], c)
-        if drain:
-            wait("v", "sv", cnt["v"])
 
     def red(out, a, op):
         run("v", V.tensor_reduce, [out], [a], AX, op)
 
-    def mm(out, lhsT, rhs, start, stop):
-        run("t", g.tensor.matmul, [out], [lhsT, rhs], start, stop, inc=stop)
+    def mm(out, lhsT, rhs, start, stop, inc=None):
+        run("t", g.tensor.matmul, [out], [lhsT, rhs], start, stop, inc=stop if inc is None else inc)
 
-    def act(out, a, func, **kw):
-        col = kw.get("scale")
-        if isinstance(col, tuple):
-            kw["scale"] = col[1]
-            run("a", lambda o, i, c, f, **k: g.scalar.activation(o, i, f, **k), [out], [a, col], func, **kw)
-        else:
-            run("a", g.scalar.activation, [out], [a], func, **kw)
+    def act(out, a, func=ACT.Copy, **kw):
+        col = [x for x in kw.values() if isinstance(x, tuple)]
+        kw = {k: x[1] if isinstance(x, tuple) else x for k, x in kw.items()}
+        run("a", lambda o, i, *rest: g.scalar.activation(o, i, func, **kw), [out], [a] + col)
 
-    def sel(out, a, pat, op, base, cm):
-        run("p", g.affine_select, [out], [a], pat, op, 0.0, base, cm)
+    def lin(out, a, scale, bias=0.0):
+        act(out, a, ACT.Identity, scale=scale, bias=bias)
+
+    def step(out, a, thr):
+        act(out, a, ACT.Sigmoid, scale=-4096.0, bias=4096.0 * thr)
+
+    def sel(out, a, pat, op, base, cm, other=0.0):
+        run("p", g.affine_select, [out], [a], pat, op, other, base, cm)
 
     def iota(out, pat, base, cm):
         run("p", g.iota, [out], [], pat, base, cm, allow_small_or_imprecise_dtypes=True)
 
-    C = lambda i: R("COL", i, i + 1, key="COL%d" % i)
-    ICOL, WCOL, RCOL, WE, AM8B, CF, ONEC, W81C = [C(i) for i in range(8)]
+    def spread(name, n, full):
+        while n < full:
+            act(R(name, n, 2 * n), R(name, 0, n))
+            n *= 2
 
-    g.sync.dma_start(T.WIN[:, 0:256], T.s0[:, :]).then_inc(T.sem.ds0, 16)
-    lastw["L0S"] = ("ds0", 16)
+    ICOL, WCOL, RCOL, WY, W81C, CF, AM, NB6, PCOL, I16C = [R("COL", i, i + 1) for i in range(10)]
+    TMP = [R("COL", i, i + 1) for i in range(10, 32)]
+
+    g.sync.dma_start(T.WS[:, 0:256], T.s0[:, :]).then_inc(T.sem.ds0, 16)
+    after("ds0", 16, [], R("WS", 0, 256)[0])
     for q in range(4):
         g.sync.dma_start(T.OPR[32 * q:32 * q + 32, :], T.opr[32 * q:32 * q + 32, :]).then_inc(T.sem.dopr, 16)
-    lastw["OPR"] = ("dopr", 64)
+    after("dopr", 64, [], R("OPR")[0])
+    fill(R("ONES"), 1.0)
     fill(R("F0"), 0)
     wait("a", "sv", cnt["v"])
     g.scalar.dma_start(T.F0[0:128:16, :], T.f0[:, :]).then_inc(T.sem.df0, 16)
     g.scalar.dma_start(T.F0[1:128:16, :], T.f0[:, :]).then_inc(T.sem.df0, 16)
-    lastw["F0"] = ("df0", 32)
+    after("df0", 32, [], R("F0")[0])
 
-    fill(R("ONES"), 1.0)
-    fill(R("Z128"), 0.0)
     ONES = lambda n: R("ONES", 0, n)
-    IO16, WROW = R("WROW", 16, 32, key="IO16"), R("WROW", 0, 16, key="WROW")
+    IO16, WROW = R("VEC", 0, 16), R("VEC", 16, 32)
+    sel(R("IDB"), ONES(128), [[-1, 128]], OP.is_equal, 0, 1)
     sel(R("TB1", 0, 128), ONES(128), [[-16, 8], [0, 16]], OP.is_ge, 0, 1)
     sel(R("BLK"), R("TB1", 0, 128), [[16, 8], [0, 16]], OP.is_ge, 15, -1)
-    sel(R("IDB"), ONES(128), [[-1, 128]], OP.is_equal, 0, 1)
     iota(IO16, [[1, 16]], 0, 0)
-    iota(R("LLAY"), [[16, 32]], 0, 0)
-    iota(R("DIFF"), [[32, 2], [64, 8], [16, 2]], 2048, 0)
-    iota(R("IO6"), [[0, 2], [1, 3]], 0, 0)
-    iota(R("PCOL"), [[0, 1]], 0, 1)
-    iota(R("ULST"), [[32, 8], [256, 2], [16, 2]], 0, 0)
-    iota(R("TR"), [[16, 16]], 512, 0)
-    sel(R("TRIM"), ONES(128), [[1, 128]], OP.is_gt, 0, -1)
-    sel(R("NTB"), R("BLK"), [[-1, 128]], OP.is_ge, 0, 1)
+    iota(R("SBASE"), [[0, 2], [16, 16]], 0, 0)
+    iota(PCOL, [[0, 1]], 0, 1)
+    iota(R("PD", 0, 9), [[16, 9]], 0, 0)
+    iota(R("IO9", 0, 9), [[0, 3], [1, 3]], 0, 0)
+    iota(R("IO9", 9, 12), [[1, 3]], 1, 0)
+    BLK8 = R("BLK", 0, None, 16)
+    fill(R("Z256"), 0.0)
+    fill(R("LBW"), 0.0)
     for i in range(16):
-        fill(R("WROW", i, i + 1, key="WROW"), float(WT[i]))
-    for j in range(J):
-        fill(R("KT", 16 * j, 16 * j + 16), float(KA[j]))
-    fill(ONEC, 1.0)
+        fill(R("VEC", 16 + i, 17 + i), float(WT[i]))
     TRE = lambda a, b: R("TREE", a, b)
     tt(TRE(0, 64), R("IDB", 0, 64), R("IDB", 64, 128), OP.add)
+    fill(R("UT", 16, 32), 0)
     tt(TRE(64, 96), TRE(0, 32), TRE(32, 64), OP.add)
+    fill(R("WS", 256, 512), 0.0)
     tt(R("I16"), TRE(64, 80), TRE(80, 96), OP.add)
-    tt(TRE(96, 112), TRE(64, 80), TRE(80, 96), OP.add)
-    tt(R("I8"), TRE(96, 104), TRE(104, 112), OP.add)
-    tt(TRE(0, 16), R("I16"), IO16, OP.mult)
-    red(ICOL, TRE(0, 16), OP.add)
-    tt(TRE(16, 32), R("I16"), WROW, OP.mult)
-    red(WCOL, TRE(16, 32), OP.add)
-
-    def lb(name, col):
-        fill(R(name), 0.0, True)
-        for q in range(8):
-            ts(R(name, 16 * q, 16 * q + 129 * 15 + 1, 129), R("BLK", 16 * q, 16 * q + 16), col, OP.mult)
-    lb("LBW", WCOL)
-    ts(R("REPL", 0, 16), R("Z128", 0, 16), ICOL, OP.add)
-    AL, BE = R("I16", 0, 1), R("I16", 1, 2)
-    ts(AM8B, BE, -8.0, OP.mult, AL, OP.add)
-    ts(CF, AL, 128.0, OP.mult, BE, OP.subtract)
-    ts(W81C, AL, 8.0, OP.mult, BE, OP.add)
-    ts(WE, W81C, 4.0, OP.mult)
-    cp(R("RC", 0, 1), WCOL)
-    ts(R("RC", 1, 2), R("RC", 0, 1), 7, OP.bitwise_and)
-    cp(RCOL, R("RC", 1, 2))
-    cp(R("W16", 0, None, 2), R("BLK", 0, None, 16))
-    ts(R("W16", 1, None, 2), R("BLK", 0, None, 16), RCOL, OP.mult)
-    fill(R("WF16"), 0.0, True)
-    ts(R("WF16", 0, None, 2), R("BLK", 0, None, 16), WE, OP.mult)
-    cp(R("I8R", 0, 8), R("I8"))
-    for n in (8, 16, 32, 64, 128):
-        cp(R("I8R", n, 2 * n), R("I8R", 0, n))
-
-    ts(R("HI"), R("F0"), 3, OP.arith_shift_right)
-    ts(R("HM"), R("F0"), 7, OP.bitwise_and)
-    ts(R("KEP"), R("HI"), AL, OP.mult)
-    ts(R("XR"), R("HM"), BE, OP.mult)
-    tt(R("WIN", 256, 512, key="L0F"), R("KEP"), R("XR"), OP.add)
-    fill(R("WIN", 512, 2048, key="LU"), 0.0, True)
-    for l in (1, 2, 3):
-        ts(R("WIN", 512 * l + 256, 512 * l + 512, key="LU"), ONES(256), CF, OP.mult)
-    fill(R("WIN", 2048, 2560, key="NEW"), 0.0)
-    WALL = R("WIN", key=["L0S", "L0F", "LU", "NEW"])
-    ts(R("LT", 0, 32), R("LLAY"), ICOL, OP.add)
-    tt(R("DIFF"), R("DIFF"), R("LLAY"), OP.subtract)
-    cp(R("LLAY"), R("LT", 0, 32))
-    cp(R("LIST"), R("LT", 0, 32))
+    ROW = lambda i: R("I16", i, i + 1)
     LWn = {}
 
-    def L(name, n=1):
+    def L(name, n=1, a=0, b=None):
         if name not in LWn:
             LWn[name] = (sum(x[1] for x in LWn.values()), n)
-        a = LWn[name][0]
-        return R("LW", a, a + n, key="LW_" + name)
-    for nm in ("clo", "lod", "e811", "e512"):
-        fill(L(nm), 0.0)
-    fill(R("ST0", 0, 7, key=["ST0v", "ST0e"]), 0.0)
-    fill(R("ST0", 7, 8, key="ST0U"), 1023.0)
-    fill(R("G8T"), 1.0)
-    fill(R("C32"), 32.5)
-
-    def kmats(k, p):
+        at, n = LWn[name]
+        return R("LW", at + a, at + (n if b is None else b))
+    fill(L("clo"), 0.0)
+    tt(TRE(0, 16), R("I16"), WROW, OP.mult)
+    tt(TRE(16, 32), R("I16"), IO16, OP.mult)
+    red(WCOL, TRE(0, 16), OP.add)
+    red(ICOL, TRE(16, 32), OP.add)
+    ts(R("LBW", 15, 128, 16), BLK8, WCOL, OP.mult)
+    ts(R("SBASE"), R("SBASE"), ICOL, OP.add)
+    cp(R("ULIST", 0, 1), ICOL)
+    cp(R("SLIST"), R("SBASE"))
+    ts(R("REPL"), R("Z256", 0, 16), ICOL, OP.add)
+    tt(R("I8"), R("I16", 0, 8), R("I16", 8, 16), OP.add)
+    fill(L("lod"), 0.0)
+    fill(L("e811"), -0.25)
+    for j in range(J):
+        fill(R("KT", 16 * j, 16 * j + 16), float(KA[j]))
+    lin(R("ST15"), ONES(256), 1.0)
+    lin(R("ST7"), ONES(256), 1.0)
+    lin(R("ONEF"), ONES(128), 1.0)
+    act(R("I8R", 0, 8), R("I8"))
+    spread("I8R", 8, 256)
+    for k, p in ((7, 56), (15, 120)):
         for nm, w, n in (("BD", [[-k, 8], [0, 8]], 64), ("ST", [[0, 32], [-k, 8]], 256), ("SR", [[-k, 8], [0, 16]], 128)):
-            sel(R("TB1", 0, n, p=p), R("ONES", 0, n, p=p), w, OP.is_ge, 0, 1)
-            sel(R(nm + str(k), p=p), R("TB1", 0, n, p=p), [[-a, b] for a, b in w], OP.is_ge, k - 1, -1)
-    kmats(7, 56)
-    kmats(15, 120)
-    sel(R("G8T", p=8), R("G8T", p=8), [[-1, 8], [0, 16]], OP.is_equal, 0, 1)
+            far = -4096.0 if nm == "BD" else 0.0
+            sel(R("TB2", 0, n, p=p), R("Z256" if far else "ONES", 0, n, p=p), w, OP.is_ge, 0, 1, far)
+            sel(R(nm + str(k), p=p), R("TB2", 0, n, p=p), [[-a, b] for a, b in w], OP.is_ge, k - 1, -1, far)
+    sel(R("TB2", 0, 16), ONES(16), [[-8, 16]], OP.is_ge, 0, 1)
+    sel(R("J16"), R("TB2", 0, 16), [[8, 16]], OP.is_ge, 7, -1)
+    sel(R("TB2", 128, 256), ONES(128), [[1, 128]], OP.is_gt, 0, -1)
+    sel(R("TRIM"), R("TB2", 128, 256), [[1, 128]], OP.not_equal, 0, -1, -256.0)
     for t in (0, 1):
-        sel(R("LE%d" % t), R("I8R"), [[8, 32], [0, 8]], OP.is_gt, -128 * t, -1)
-        sel(R("LI%d" % t), R("I8R"), [[8, 32], [0, 8]], OP.is_gt, 8 - 128 * t, -1)
+        sel(R("LE%d" % t), R("I8R"), [[8, 2], [16, 16], [2, 8]], OP.is_gt, -8 * t, -2)
+        sel(R("LI%d" % t), R("I8R"), [[8, 2], [16, 16], [2, 8]], OP.is_ge, -8 * t, -2)
     iota(R("IO256"), [[1, 256]], 0, 0)
-    sel(R("ONE0"), ONES(128), [[0, 128]], OP.is_equal, 0, 1)
-    iota(R("OC"), [[64, 8], [0, 16]], 0, 0)
-    sel(R("D0"), ONES(128), [[0, 8], [1, 16]], OP.is_gt, 0, 0)
+    iota(R("TB1", 0, 128), [[0, 8], [1, 16]], -2, 0)
+    sel(R("TB1", 128, 256), R("TB1", 0, 128), [[-16, 8], [0, 16]], OP.is_ge, 0, 1, -9.0)
+    sel(R("ROWI"), R("TB1", 128, 256), [[16, 8], [0, 16]], OP.is_ge, 15, -1, -9.0)
+    sel(R("TRI2"), R("TB2", 128, 256), [[1, 128]], OP.not_equal, 0, -1, 1024.0)
+    iota(R("OC2"), [[0, 16], [1, 9]], 0, 0)
+    sel(R("D0"), R("Z256", 0, 144), [[0, 16], [1, 9]], OP.not_equal, 0, 0, -4096.0)
 
-    def late_constants():
-        ts(R("NID"), R("IDB"), -256.0, OP.mult)
-        tt(R("TRIM"), R("TRIM"), R("NID"), OP.add)
-        ts(R("NID"), R("IDB"), -1.0, OP.mult)
-        ts(R("NTB"), R("NTB"), -1.0, OP.mult)
-        cp(R("IDF"), R("IDB"))
-        ts(R("ULST"), R("ULST"), ICOL, OP.add)
-        ts(R("TR"), R("TR"), ICOL, OP.add)
-        fill(R("JS"), 0.0, True)
-        for q in range(8):
-            ts(R("JS", 16 * q, 16 * q + 129 * 15 + 1, 129), ONES(16), 128.0, OP.mult, R("I8", q, q + 1), OP.mult)
-        lb("LB1", ONEC)
-        act(R("LBR"), R("LB1"), ACT.Copy, scale=RCOL)
-        act(R("LBE"), R("LB1"), ACT.Copy, scale=WE)
-        cp(R("DEL", 0, 16), R("I16"))
-        for n in (16, 32, 64, 128):
-            cp(R("DEL", n, 2 * n), R("DEL", 0, n))
-        fill(R("BR"), 0.0, True)
-        for q in range(8):
-            for i in (0, 1):
-                cp(R("BR", 128 * i + 16 * q + i, 128 * i + 16 * q + i + 1), R("BLK", 16 * q, 16 * q + 1))
-        cp(R("REPL", 16, 32, key="REPA"), IO16)
-        ts(R("W81"), R("BLK", 0, None, 16), W81C, OP.mult)
-        fill(R("SC"), 0.0, True)
-        for o in range(8):
-            ts(R("SC", 64 * o + 32, 64 * o + 64), ONES(32), CF, OP.mult)
-        cp(R("H", 0, None, 16, key="H0"), ONES(256))
-        fill(R("CY", 16, 17, key="CY16"), 0.0)
+    def constants_1():
+        runs = ((0, 1, 8.0), (1, 5, 1.0), (5, 16, 0.0), (16, 17, 127.0), (17, 18, 7.0), (18, 31, 0.0), (31, 32, 1.0))
+        for a, b, v in runs:
+            fill(R("VEC", 32 + a, 32 + b), v)
+        cp(R("RC", 0, 1), WCOL)
+        tt(TRE(0, 16), R("I16"), R("VEC", 32, 48), OP.mult)
+        ts(R("RC", 1, 2), R("RC", 0, 1), 7, OP.bitwise_and)
+        tt(TRE(16, 32), R("I16"), R("VEC", 48, 64), OP.mult)
+        red(W81C, TRE(0, 16), OP.add)
+        cp(RCOL, R("RC", 1, 2))
+        red(CF, TRE(16, 32), OP.add)
+        ts(TMP[0], ROW(5), 8.0, OP.mult, ROW(6), OP.add)
+        ts(TMP[1], R("IDB", 0, 1), 896.0, OP.mult)
+        ts(R("W16", 0, None, 2), BLK8, 0.25, OP.mult)
+        tt(WY, TMP[0], W81C, OP.add)
+        ts(TMP[2], R("IDB", 1, 2), 4.125, OP.mult, TMP[1], OP.add)
+        ts(R("W16", 1, None, 2), BLK8, RCOL, OP.mult)
+        fill(R("WF", 1, 16, 2), 0.0)
+        ts(R("WF", 0, 16, 2), BLK8, WY, OP.mult)
+        lin(R("NID"), R("IDB"), -1.0)
+        lin(R("CST", 0, None, 2), ONES(128), TMP[2])
+        lin(R("CST", 1, None, 2), ONES(128), -3.5 / 128)
+        spread("WF", 16, 256)
+        lin(R("SC"), ONES(256), CF)
+        act(R("WC", 256, 512), R("SC"))
+        ts(R("HI"), R("F0"), 3, OP.arith_shift_right)
+        ts(R("HM"), R("F0"), 7, OP.bitwise_and)
+        ts(R("KEP"), R("HI"), ROW(0), OP.mult, ROW(15), OP.add)
+        ts(R("ZR"), R("HM"), ROW(1), OP.mult)
+        ts(TMP[3], R("IDB", 56, 57), 896.0, OP.mult)
+        tt(R("WC", 0, 256), R("KEP"), R("ZR"), OP.add)
+        ts(TMP[4], R("IDB", 57, 58), 4.25, OP.mult, TMP[3], OP.add)
+        ts(TMP[5], R("IDB", 120, 121), -0.125, OP.mult)
+        lin(R("L1"), ONES(128), TMP[4])
+        lin(R("L2"), ONES(128), TMP[5])
+        lin(R("C32"), ONES(128), 32.5)
+        lin(R("C24"), ONES(128), 24.0)
+        act(R("IDF"), R("IDB"))
         fill(R("MS"), 0.0)
+        fill(R("JS"), 0.0)
+        fill(R("RB"), 0.0)
+        fill(R("PXS", 128, 136), 0.0)
+        fill(R("ST0", 0, 3), 1.0)
+        fill(R("ST0", 3, 10), 0.0)
+        fill(R("ST0", 10, 11), 1023.0)
+        ts(R("JS", 15, 128, 16), R("I8"), 128.0, OP.mult)
+
+    def constants_2():
+        for i in range(16):
+            cp(R("G8F", i, None, 16), R("I8"))
+        ts(R("SBASE"), R("SBASE"), 1.0 / 256, OP.mult)
+        ts(I16C, ICOL, 1.0 / 16, OP.mult)
+        ts(AM, ROW(6), 8.0, OP.mult, ROW(5), OP.subtract)
+        ts(NB6, ROW(6), -1.0, OP.mult)
+
+    def constants_3():
+        ts(TMP[6], ROW(0), 128.0, OP.mult, ROW(15), OP.add)
+        tt(TMP[7], ROW(5), ROW(6), OP.add)
+        ts(TMP[9], ROW(15), 4.0, OP.mult)
+        ts(R("FP", 256, 272), ONES(16), TMP[6], OP.mult)
+        ts(TMP[8], TMP[7], -1.0, OP.mult, 1.0, OP.add)
+        ts(TMP[10], WY, EPS, OP.mult, TMP[9], OP.add)
+        ts(R("E", 128, 256), R("BLK"), ROW(15), OP.mult, -0.375, OP.mult)
+        ts(R("E", 0, 128), R("IDB"), TMP[8], OP.mult)
+        ts(R("WE4", 1, None, 2), BLK8, TMP[10], OP.mult)
+        ts(R("W4", 0, None, 2), BLK8, RCOL, OP.mult)
+        tt(R("IK"), R("E", 0, 128), R("E", 128, 256), OP.add)
+        ts(R("W4", 1, None, 2), BLK8, EPS / 4, OP.mult)
+        ts(R("WE4", 0, None, 2), BLK8, ROW(15), OP.mult, -3.5, OP.mult)
+        for h in (0, 1):
+            ts(R("SELA", 8 * h, 8 * h + 8), BLK8, ROW(0), OP.mult, -EPS, OP.mult)
+        cp(R("RA"), BLK8)
+        ts(R("W81"), BLK8, W81C, OP.mult)
+        act(R("DEL", 0, 16), R("I16"))
+        spread("DEL", 16, 256)
+        lin(R("IOT2"), R("OC2"), 1.0, -3.5)
+        lin(R("IOT2", 8, None, 9), ONES(16), 8.0)
+        lin(R("OC2"), R("OC2"), 0.25, -10.0)
+        for buf in ("SEND", "SENDC"):
+            act(R(buf, 256, 512), R("Z256"))
+
+    def constants_4():
+        ts(R("PD", 0, 9), R("PD", 0, 9), ICOL, OP.add)
+        ts(TMP[11], PCOL, -1.0, OP.mult, 129.0, OP.add)
+        ts(R("NI", 0, 9), R("PD", 0, 9), 1.0 / 9, OP.mult, -4.0 / 9, OP.add)
+        ts(TMP[12], TMP[11], ROW(0), OP.mult, PCOL, OP.add)
+        ts(R("PD", 16, 25), R("NI", 0, 9), -9.0, OP.mult, -8.0, OP.add)
+        ts(R("LAB", 2, 3), TMP[12], -1.0, OP.add)
+        tt(R("PD", 0, 9), R("PD", 0, 9), R("PD", 16, 25), OP.add)
+        cp(R("LAB", 0, 1), PCOL)
+        ts(R("PD", 16, 25), R("NI", 0, 9), 17.0, OP.add)
+        ts(R("PD", 0, 9), R("PD", 0, 9), 0.0, OP.is_equal)
+        ts(R("L16"), IO16, 9.0, OP.mult, 8.0, OP.add)
+        tt(R("PD", 0, 9), R("PD", 0, 9), R("PD", 16, 25), OP.mult)
+        tt(R("PD", 16, 25), R("PD", 0, 9), R("NI", 0, 9), OP.add)
+        cp(R("L9", 0, 9), R("PD", 16, 25))
 
     dests = [c for c in T.cores if c != core]
     dests.sort(key=lambda c: len(topo.engines(core, c)))
@@ -300,307 +343,328 @@ def rank_program(g, core, T, topo):
         g.remote_dma_fused([RemoteDMATransfer(dst_ids=[d], dma_engine_mask=m, remote_sem=T.sem[rsem], src=src(c), dst=dst)
                             for c, d, m, _n in plan], local_sem=T.sem[lsem])
 
-    GS = R("G", 0, 256, key="GS")
-    GF = R("G", 256, 512, key="GF")
-    blocks = [(512 * c, 512) for c in range(7)] + [(3584, 256), (3840, 256)]
-    CALL = R("C", key=["C%d" % c for c in range(len(blocks))])
+    def half(name, k, K, h):
+        return R(name, 128 * K * h + k, 128 * K * (h + 1), K)
 
-    def update_half(h):
-        scat(R("WIN", 512, 2048, key="LU"), R("UPL", 16 * h, 16 * h + 16), R("WIN", 2048 + 256 * h, 2304 + 256 * h, key="NEW"))
+    def cols(name, h, p=None):
+        return R(name, 128 * h, 128 * h + 128, p=p)
+
+    lev = []
+
+    def pump(k):
+        for f, x in lev[:k]:
+            f(*x)
+        del lev[:k]
+
+    blocks = [(512 * c, 512) for c in range(7)] + [(3584, 256), (3840, 256)]
+    PA = lambda h: R("PT%d" % h, 256, 384)
+    PB = lambda h: R(("PI", "PR")[h], 0, 128)
 
     for rnd in range(RO):
         ST, SN = ("ST0", "ST1") if rnd % 2 == 0 else ("ST1", "ST0")
         XB = "XB%d" % (rnd % 2)
+        new = rnd + 1 if rnd else 0
+        land = 256 * (rnd + 2)
         if rnd:
-            wait("v", "rn", per * rnd)
+            wait("t", "rn", per * rnd)
             wait("a", "rn", per * rnd)
-        gath(GS, WALL, R("LIST", 0, 16))
         for b in range(16):
-            mm(R("PU", 0, 16), R("LBW", 128 * b, 128 * b + 128), R("G", b, 256, 16, key="GS"), b == 0, b == 15)
-        act(R("SREP", 0, 256, key="SR0"), GS, ACT.Copy)
-        act(R("SREP", 256, 512, key="SR1"), GS, ACT.Copy)
-        act(GF, IND(WALL, R("LIST", 16, 32)), ACT.Copy)
-        ui, um, sq, s4 = [R("UI", 16 * k, 16 * k + 16, key="UI%d" % k) for k in range(4)]
-        cp(ui, R("PU", 0, 16))
-        ts(um, ui, 4095, OP.bitwise_and)
+            mm(R("PU", 0, 16), R("LBW", 15 - b, 143 - b), R("WS", 256 * new + b, 256 * new + 256, 16), b == 0, b == 15)
+        act(R("SREP"), IND(R("WS", 0, land), R("SLIST")))
+        um, sq, s4 = [R("UI", 16 * k, 16 * k + 16) for k in range(3)]
+        cp(R("UT", 16 * new, 16 * new + 16), R("PU", 0, 16))
+        ts(um, IND(R("UT", 0, 16 * (rnd + 2)), R("ULIST", 0, 1)), 4095, OP.bitwise_and)
         tt(sq, um, um, OP.mult)
-        ts(s4, sq, 4, OP.arith_shift_right)
-        ts(sq, s4, L("e811"), OP.add)
-        tt(R("KU"), IND(um, R("REPL", 0, 16)), R("KT"), OP.mult)
-        tt(R("HI"), IND(sq, R("REPL", 0, 16)), R("KU"), OP.add)
-        ts(R("HM"), R("HI"), 8191, OP.bitwise_and)
-        cp(R("OFFC"), R("HM"))
-        ts(R("FP"), GF, L("lod"), OP.subtract)
+        for a, b in ((0, 64), (64, 256)):
+            rep = R("REPL", a // 16, b // 16)
+            tt(R("KU", a, b), IND(um, rep), R("KT", a, b), OP.mult)
+            if a == 0:
+                ts(s4, sq, 1.0 / 16, OP.mult, L("e811"), OP.add)
+            tt(R("HI", a, b), IND(s4, rep), R("KU", a, b), OP.add)
+            ts(R("HM", a, b), R("HI", a, b), 8191, OP.bitwise_and)
+            cp(R("OFFC", a, b), R("HM", a, b))
         if rnd == 0:
-            late_constants()
-            act(R("SEND", 0, 512), R("SC"), ACT.Copy)
-        SR = lambda n: R("SREP", 0, n, key=["SR0", "SR1"])
-        act(R("OG"), IND(R("OPR"), R("OFFC", 128, 160)), ACT.Copy)
-        for c, (a, n) in enumerate(blocks):
-            cr = R("CR", a, a + n, key="CR%d" % c)
-            if c == 4:
-                cr = R("PX")
+            constants_1()
+        for c, bank in ((0, "PX"), (1, "PR")):
+            mm(R(bank), R("IDB"), R("SREP"), True, False, inc=True)
+            act(R("OG", 512 * c, 512 * c + 512), IND(R("OPR"), R("OFFC", 32 * c, 32 * c + 32)))
+        for h in (0, 1):
+            mm(R("PT%d" % h, 0, 256), ONES(128), R("CST"), True, False, inc=True)
+        for c, bank in ((0, "PX"), (1, "PR")):
+            mm(R(bank), R("NID"), R("OG", 512 * c, 512 * c + 512), False, True)
+        for c in (0, 2, 1, 3, 4, 5, 6, 7, 8):
+            a, n = blocks[c]
+            cr = R("CR", a, a + n)
+            if c < 2:
+                cr = R(("PX", "PR")[c])
             else:
-                tt(cr, IND(R("OPR"), R("OFFC", a // 16, (a + n) // 16)), SR(n), OP.subtract)
-            act(R("C", a, a + n, key="C%d" % c), cr, ACT.Abs)
-            if c == 0:
-                mm(R("PX"), R("IDB"), SR(512), True, False)
-                mm(R("PX"), R("NID"), R("OG"), False, True)
+                tt(cr, IND(R("OPR"), R("OFFC", a // 16, (a + n) // 16)), R("SREP", 0, n), OP.subtract)
+            act(R("C", a, a + n), cr, ACT.Abs)
             for x in range(a // 128, (a + n) // 128):
-                o = R("PT", 16 * x, 16 * x + 16)
-                mm(o, R("FP", 128 * (x % 2), 128 * (x % 2) + 128), R("WF16"), True, False)
-                mm(o, R("C", 128 * x, 128 * x + 128, key="C%d" % c), R("W16"), False, True)
+                mm(R("PT%d" % (x % 2), 16 * (x // 2), 16 * (x // 2) + 16), R("C", 128 * x, 128 * x + 128), R("W16"), False, x >= 30, inc=True)
+            if c == 1:
+                if rnd:
+                    wait("a", "rc", per * rnd)
+                act(R("FP", 0, 256), IND(R("WC", 0, land), R("SLIST", 0, 16)), ACT.Identity, bias=L("lod"))
+                for h in (0, 1):
+                    mm(R("PT%d" % h, 0, 256), cols("FP", h), R("WF"), False, False, inc=True)
+        PY = lambda h: R("PT%d" % h, 0, 256, 2)
+        PV = lambda h: R("PT%d" % h, 1, 256, 2)
+
+        def owners(h):
+            ts(cols("ZO", h), PV(h), M8, OP.add, M8, OP.subtract)
+            tt(cols("OK", h), PV(h), cols("ZO", h), OP.subtract)
+
+        def hots(h):
+            for o in range(8):
+                ts(half("OH", o, 8, h), cols("OK", h), o - 3.5, OP.is_equal)
+
+        def far(h):
+            act(cols("F", h), PY(h), ACT.Relu, scale=-65536.0, bias=65536.0 * 899.9375)
+            act(cols("Y0", h), PY(h))
+
+        def masks(K, M, src, thr, na, h):
+            for k in range(K - na, K):
+                step(half(M, k, K, h), cols(src, h), thr(k + 1))
+            for k in range(K - na):
+                ts(half(M, k, K, h), cols(src, h), thr(k + 1), OP.is_lt)
+
+        def count(K, M, h):
+            p = 8 * K
+            if h == 0:
+                mm(R("PC", 0, 64, p=p), R("IDB", 0, p, p=p), R("BD%d" % K, p=p), True, False, inc=True)
+            for x in range(16 * h, 16 * h + 16):
+                mm(R("PC", 0, 64, p=p), R(M, p * x, p * x + p), R("OH", 64 * x, 64 * x + 64), False, x == 31)
+
+        def digit(K, Lx, mx, stp):
+            p = 8 * K
+            red(R("MX", mx, mx + 1, p=p), R("PC", 0, 64, p=p), OP.max)
+            ts(R(Lx, p=p), R("C32", p=p), R("MX", mx, mx + 1, p=p), OP.is_ge, float(stp), OP.mult)
+
+        def turn(h):
+            mm(R("PX", 128 * h, 128 * h + 128), cols("Y0", h), R("IDF"), True, False, inc=True)
+            mm(R("PX", 128 * h, 128 * h + 128), cols("F", h), R("IDB"), False, True)
+        th1 = lambda k: 128.0 * k + 900.0
+        far(1)
+        owners(0)
+        far(0)
+        hots(0)
+        for h in (0, 1):
+            tt(cols("D1", h), PY(h), cols("F", h), OP.add)
+        turn(1)
+        masks(7, "MB", "D1", th1, MACT[0][0], 0)
+        count(7, "MB", 0)
+        owners(1)
+        masks(7, "MB", "D1", th1, MACT[0][1], 1)
+        hots(1)
+        for h in (0, 1):
+            mm(PA(h), R("NID"), cols("F", h), True, False, inc=True)
+        count(7, "MB", 1)
+        act(R("SEND", 0, 256), R("Z256")) if rnd == 0 else None
         if rnd:
             wait("a", "ln", per * rnd)
-            act(R("SEND", 0, 512), R("SC"), ACT.Copy)
-        cp(R("YI"), R("PT", 0, None, 2))
-        cp(R("VI"), R("PT", 1, None, 2))
-        ts(R("DM"), R("YI"), 2, OP.arith_shift_right, 4095, OP.bitwise_and)
-        ts(R("OI"), R("VI"), 7, OP.bitwise_and)
-        cp(R("D16"), R("DM"))
-        cp(R("O16"), R("OI"))
-
-        def half(name, k, K, h, tag):
-            return R(name, 128 * K * h + k, 128 * K * (h + 1), K, key="%s%s%d" % (name, tag, h))
-
-        def cols(name, h):
-            return R(name, 128 * h, 128 * h + 128)
-
-        def digit(K, Lx, step):
-            p = 8 * K
-            tt(R("CT", p=p), R("PC", 0, 64, p=p), R("BD%d" % K, p=p), OP.mult)
-            red(R("MX", 0, 1, p=p), R("CT", p=p), OP.max)
-            ts(R(Lx, p=p), R("C32", p=p), R("MX", 0, 1, p=p), OP.is_ge, float(step), OP.mult)
-            mm(R("PI", 0, 256), R(Lx, p=p), R("ST%d" % K, p=p), True, True)
-
-        def masks(K, M, src, step, na):
-            for h in (0, 1):
-                for k in range(K - na, K):
-                    act(half(M, k, K, h, "a"), cols(src, h), ACT.Sigmoid, scale=-1000.0, bias=1000.0 * step * (k + 1) - 500.0)
-                for k in range(K - na):
-                    ts(half(M, k, K, h, "v"), cols(src, h), float(step * (k + 1)), OP.is_lt)
-                if na == 0:
-                    for o in range(8):
-                        ts(half("OH", o, 8, h, "v"), cols("O16", h), float(o), OP.is_equal)
-            for x in range(32):
-                h = x // 16
-                mm(R("PC", 0, 64, p=8 * K), R(M, 8 * K * x, 8 * K * x + 8 * K, key=["%sv%d" % (M, h), "%sa%d" % (M, h)]),
-                   R("OH", 64 * x, 64 * x + 64, key="OHv%d" % h), x == 0, x == 31)
-        masks(7, "M2", "D16", 128, 0)
-        TM = lambda a, b, k=None: R("TM", a, b, key="TM%d" % (a if k is None else k))
-        tt(TM(0, 128), R("DM", 0, 128), R("DM", 128, 256), OP.min)
-        tt(TM(128, 192), TM(0, 64, 0), TM(64, 128, 0), OP.min)
-        tt(TM(192, 224), TM(128, 160, 128), TM(160, 192, 128), OP.min)
-        tt(TM(224, 240), TM(192, 208, 192), TM(208, 224, 192), OP.min)
-        tt(TM(240, 248), TM(224, 232, 224), TM(232, 240, 224), OP.min)
-        digit(7, "L1", 128)
-        run("t", g.tensor.transpose, [R("PU", 0, 128, p=8)], [TM(240, 248), R("IDF")])
-        tt(R("DB"), R("DM"), R("PI", 0, 256), OP.subtract)
-        masks(15, "M1", "DB", 8, 4)
-        red(R("MR", 0, 1, p=8), R("PU", 0, 128, p=8), OP.min)
+            act(R("SEND", 0, 256), R("Z256"))
+        else:
+            constants_2()
+        digit(7, "L1", 0, 128)
+        for h in (0, 1):
+            mm(PA(h), R("L1", p=58), cols("ST7", h, 58), False, True)
+        turn(0)
+        for h in (0, 1):
+            tt(cols("DB", h), cols("Y0", h), PA(h), OP.subtract)
+            masks(15, "MA", "DB", lambda k: 8.0 * k - 0.1875, MACT[1][h], h)
+            mm(PB(h), R("NID"), cols("F", h), True, False, inc=True)
+            mm(PB(h), R("L1", p=58), cols("ST7", h, 58), False, False, inc=True)
+            count(15, "MA", h)
+        red(R("MX", 3, 4), R("PX", 0, 256), OP.min)
         if rnd:
-            update_half(0)
-        digit(15, "L2", 8)
-        mm(R("PU", 1, 2), R("G8T", p=8), R("MR", 0, 1, p=8), True, True)
-        tt(R("DC"), R("DB"), R("PI", 0, 256), OP.subtract)
-        masks(7, "M2", "DC", 1, 2)
+            wait("a", "lc", per * rnd)
+        else:
+            constants_3()
+        act(R("SENDC", 0, 256), R("SC"))
+        ts(R("MJ"), R("J16"), R("MX", 3, 4), OP.mult)
+        digit(15, "L2", 1, 8)
+        for h in (0, 1):
+            mm(PB(h), R("L2", p=121), cols("ST15", h, 121), False, True)
+        mm(R("PU", 16, 32), R("G8F"), R("MJ"), True, True)
+        for h in (0, 1):
+            tt(cols("DC", h), cols("Y0", h), PB(h), OP.subtract)
+            masks(7, "MB", "DC", lambda k: k - 0.125, MACT[2][h], h)
+            count(7, "MB", h)
+            mm(PB(h), ONES(128), R("C24"), True, False, inc=True) if h == 0 else None
         if rnd:
-            update_half(1)
-        digit(7, "L3", 1)
+            wait("v", "lt", per * rnd)
+        else:
+            constants_4()
+        red(R("MS", 1, 2), R("PU", 16, 32), OP.min)
+        digit(7, "L3", 2, 1)
+        for h in (0, 1):
+            mm(PA(h), R("L3", p=56), cols("ST7", h, 56), True, True)
+        mm(PB(1), ONES(128), R("C24"), True, False, inc=True)
+        for h in (0, 1):
+            tt(cols("KEP", h), cols("DC", h), PA(h), OP.is_lt)
+            mm(R("PL", h, h + 1), cols("KEP", h), ONES(1), True, True)
+        for h in (0, 1):
+            mm(PB(h), R("TRIM"), cols("KEP", h), False, False, inc=True)
+        for t in (0, 1):
+            ts(cols("TOTB", t), R("Z256", 0, 128), R("PL", t, t + 1), OP.add)
+        for h in (0, 1):
+            for t in (0, 1):
+                mm(PB(h), cols("TOTB", t), cols("LE%d" % t, h), False, t == 1)
+        for t in (0, 1):
+            for t2 in (0, 1):
+                mm(R("PL", 2 + t, 3 + t), cols("LI%d" % t2, t), R("TOTB", 128 * t2, 128 * t2 + 1), t2 == 0, t2 == 1)
         mm(R("PU", 0, 1), R("SR7", p=56), R("L1", 0, 1, p=56), True, False)
         mm(R("PU", 0, 1), R("SR15", p=120), R("L2", 0, 1, p=120), False, False)
         mm(R("PU", 0, 1), R("SR7", p=56), R("L3", 0, 1, p=56), False, True)
-        tt(R("KEP"), R("DC"), R("PI", 0, 256), OP.is_lt)
-        if rnd:
-            wait("v", "lt", per * rnd)
-        cp(R("MS", 0, 2), R("PU", 0, 2))
-        act(R(XB, 4 * rank, 4 * rank + 2), R("MS", 0, 2), ACT.Copy)
-        before("p", ["MS"], ["NEW", "LU"])
+        act(R("MS", 0, 1), R("PU", 0, 1))
+        before("p", R("MS")[0] + R("SREP")[0] + R("FP")[0] + R("UT")[0], [])
         to_all(lambda c: T.MS[:, 0:4], T[XB][:, 4 * rank:4 * rank + 4], "rt", "lt")
-        for t in (0, 1):
-            mm(R("PL", t, t + 1), R("KEP", 128 * t, 128 * t + 128), ONES(1), True, True)
-        mm(R("PR", 0, 256), R("TRIM"), R("KEP"), True, False)
-        for t in (0, 1):
-            ts(R("TOTB", 128 * t, 128 * t + 128, key="TOT%d" % t), R("Z128"), R("PL", t, t + 1), OP.add)
-        for t in (0, 1):
-            mm(R("PR", 0, 256), R("TOTB", 128 * t, 128 * t + 128, key="TOT%d" % t), R("LE%d" % t), False, t == 1)
-        mm(R("PY", 0, 1), R("LI0", 0, 128), R("TOTB", 0, 1, key="TOT0"), True, True)
-        mm(R("PY", 1, 2), R("LI0", 128, 256), R("TOTB", 0, 1, key="TOT0"), True, False)
-        mm(R("PY", 1, 2), R("LI1", 128, 256), R("TOTB", 128, 129, key="TOT1"), False, True)
-        cp(R("RI"), R("PR", 0, 256))
-        act(R("XR"), R("PR", 0, 256), ACT.Copy)
-        for t in (0, 1):
-            ts(R("MK", 256 * t, 256 * t + 256, key="MK%d" % t), R("IO256"), R("PY", t, t + 1), OP.is_ge)
-        for t in (0, 1):
-            for k in range(16):
-                mm(R("PL", 0, 16), R("JS", 128 * k, 128 * k + 128), R("MK", 256 * t + k, 256 * t + 256, 16, key="MK%d" % t), t == 0 and k == 0, t == 1 and k == 15)
-        ts(R("RQ"), R("RI"), 527, OP.bitwise_and)
-        cp(R("KK16"), R("RQ"))
         for h in (0, 1):
+            ts(cols("ZR", h), PB(h), -7.5, OP.add)
+            tt(cols("BR", h), PB(h), cols("ZR", h), OP.subtract)
             for c in range(16 - HACT, 16):
-                act(half("H", c, 16, h, "a"), cols("XR", h), ACT.Sigmoid, scale=1000.0, bias=-1000.0 * (16 * c - 256) + 500.0)
+                step(half("H", c, 16, h), cols("ZR", h), 2816.0 + 16 * c + 8)
+            if h == 0:
+                for t in (0, 1):
+                    ts(R("MK", 256 * t, 256 * t + 256), R("IO256"), R("PL", 2 + t, 3 + t), OP.is_ge)
+                for t in (0, 1):
+                    for k in range(16):
+                        mm(R("PU", 0, 16), R("JS", 15 - k, 143 - k), R("MK", 256 * t + k, 256 * t + 256, 16), t == 0 and k == 0, t == 1 and k == 15)
             for c in range(16):
-                ts(half("A", c, 16, h, "v"), cols("KK16", h), float(512 + c), OP.is_equal, R("PCOL"), OP.mult)
-            for c in range(1, 16 - HACT):
-                ts(half("H", c, 16, h, "v"), cols("XR", h), float(16 * c - 256), OP.is_ge)
-        for x in range(32):
-            h = x // 16
-            mm(R("PX", 0, 128), R("A", 128 * x, 128 * x + 128, key="Av%d" % h), R("H", 128 * x, 128 * x + 128, key=["H0", "Ha%d" % h, "Hv%d" % h]), x == 0, x == 31)
+                ts(half("A", c, 16, h), cols("BR", h), float(c), OP.is_equal, PCOL, OP.mult)
+            for c in range(16 - HACT):
+                ts(half("H", c, 16, h), cols("ZR", h), 2816.0 + 16 * c + 8, OP.is_lt)
+            for x in range(16 * h, 16 * h + 16):
+                mm(R("PX", 0, 128), R("A", 128 * x, 128 * x + 128), R("H", 128 * x, 128 * x + 128), x == 0, x == 31)
+        act(R(XB, 4 * rank, 4 * rank + 2), R("MS", 0, 2))
+        act(R("PLS"), R("PU", 0, 16))
         wait("v", "rt", per * (rnd + 1))
         red(L("TG"), R(XB, 0, None, 4), OP.min)
         red(L("MG"), R(XB, 1, None, 4), OP.min)
-        clo, e, U = L("clo"), R(ST, 6, 7, key=ST + "e"), R(ST, 7, 8, key=ST + "U")
-        eN, UN = R(SN, 6, 7, key=SN + "e"), R(SN, 7, 8, key=SN + "U")
+        clo, e, U, m = L("clo"), R(ST, 9, 10), R(ST, 10, 11), R("MI")
+        eN, UN = R(SN, 9, 10), R(SN, 10, 11)
         ts(L("B"), L("TG"), clo, OP.add, 1023.0, OP.min)
-        ts(L("m"), L("MG"), clo, OP.add)
-        lev = []
+        ts(m, L("MG"), clo, OP.add, -900.5, OP.add)
+        ts(L("TB"), L("B"), clo, OP.subtract, 0.125, OP.subtract)
+        ts(R("LQ"), R("ROWI"), e, OP.is_equal, 0.25, OP.mult)
+        ts(R("RB", 1, None, 2), R("SELA"), L("TB"), OP.mult)
+        mm(R("PC", 0, 32), R("ONEF"), R("RB"), True, False, inc=True)
+        mm(R("PI", 0, 144), ONES(128), R("OC2"), True, False, inc=True)
         lts = lambda *x: lev.append((ts, x))
         ltt = lambda *x: lev.append((tt, x))
-
-        def pump(k):
-            for f, x in lev[:k]:
-                f(*x)
-            del lev[:k]
         lts(L("e2"), e, 2.0, OP.is_equal)
         lts(L("ne2"), e, 2.0, OP.is_lt)
         lts(L("g0"), e, 0.0, OP.is_gt)
-        lts(L("el", 6), R("IO6"), e, OP.is_equal)
-        lts(L("e512"), e, 512.0, OP.mult)
+        lts(L("nel", 9), R("IO9", 0, 9), e, OP.not_equal)
         lts(L("nlo"), clo, 1.0, OP.add, L("B"), OP.max)
-        lts(L("ea"), L("m"), L("B"), OP.is_lt, L("e2"), OP.mult)
-        lts(L("nel", 6), L("el", 6), -1.0, OP.mult, 1.0, OP.add)
+        lts(L("ea"), m, L("B"), OP.is_lt, L("e2"), OP.mult)
+        lts(L("el", 3), R("IO9", 0, 3), e, OP.is_equal)
         lts(L("q"), L("ea"), -4096.0, OP.mult, 4096.0, OP.add)
-        ltt(L("t1", 6), R(ST, 0, 6, key=ST + "v"), L("nel", 6), OP.mult)
-        lts(UN, L("m"), L("q"), OP.add, U, OP.min)
-        lts(R("UPL"), R("ULST"), L("e512"), OP.add)
+        ltt(L("t1", 9), R(ST, 0, 9), L("nel"), OP.mult)
+        lts(UN, m, L("q"), OP.add, U, OP.min)
+        L("t2", 9)
+        lts(L("t2", a=0, b=3), L("el"), float(rnd + 2), OP.mult)
         ltt(L("mbu"), L("B"), UN, OP.min)
         lts(L("bk0"), L("nlo"), UN, OP.is_ge, L("g0"), OP.mult)
-        lts(L("adv"), L("m"), L("mbu"), OP.is_lt, L("ne2"), OP.mult)
+        lts(L("adv"), m, L("mbu"), OP.is_lt, L("ne2"), OP.mult)
+        lts(L("t2", a=6, b=9), L("el"), L("B"), OP.mult)
         lts(L("nadv"), L("adv"), -1.0, OP.mult, 1.0, OP.add)
         lts(L("va"), clo, L("adv"), OP.mult)
         ltt(L("back"), L("bk0"), L("nadv"), OP.mult)
         ltt(L("stay"), L("nadv"), L("back"), OP.subtract)
         lts(eN, e, L("adv"), OP.add, L("back"), OP.subtract)
-        ltt(L("ch"), L("adv"), L("back"), OP.add)
         lts(L("val"), L("nlo"), L("stay"), OP.mult, L("va"), OP.add)
-        L("t2", 6)
-        L("t3", 6)
-        a2, ae, a3 = LWn["t2"][0], LWn["el"][0], LWn["t3"][0]
-        ELS = R("LW", ae, ae + 3, key="LW_el")
-        lts(R("LW", a2, a2 + 3, key="LW_t2"), ELS, L("val"), OP.mult)
-        lts(R("LW", a2 + 3, a2 + 6, key="LW_t2"), ELS, L("B"), OP.mult)
-        ltt(L("t3", 6), L("t1", 6), L("t2", 6), OP.add)
-        lts(L("en", 3), R("IO6", 0, 3), eN, OP.is_equal)
-        lo1, hi1 = R("LW", a3, a3 + 3, key="LW_t3"), R("LW", a3 + 3, a3 + 6, key="LW_t3")
+        lts(L("ep", 3), R("IO9", 9, 12), eN, OP.is_equal)
+        lts(L("t2", a=3, b=6), L("el"), L("val"), OP.mult)
+        lts(L("e811"), eN, 811.0, OP.mult, -0.25, OP.add)
+        ltt(L("t3", 9), L("t1"), L("t2"), OP.add)
+        lts(L("en", 3), R("IO9", 0, 3), eN, OP.is_equal)
+        ltt(L("w7", 3), L("t3", a=0, b=3), L("ep"), OP.mult)
+        lo1, hi1 = L("t3", a=3, b=6), L("t3", a=6, b=9)
         lts(L("w1", 3), lo1, 1.0, OP.add)
-        lts(L("enc", 3), L("en", 3), L("ch"), OP.mult)
-        ltt(L("w2", 3), L("w1", 3), hi1, OP.max)
-        lts(L("nen", 3), L("enc", 3), -1.0, OP.mult, 1.0, OP.add)
-        lts(L("w3", 3), L("w2", 3), L("back"), OP.mult)
-        ltt(L("w4", 3), lo1, L("nen", 3), OP.mult)
-        ltt(L("w5", 3), L("w3", 3), L("enc", 3), OP.mult)
-        ltt(R(SN, 0, 3, key=SN + "v"), L("w4", 3), L("w5", 3), OP.add)
-        lev.append((cp, (R(SN, 3, 6, key=SN + "v"), hi1)))
-        lts(L("e811"), eN, 811.0, OP.mult)
-        lts(L("p1"), eN, 512.0, OP.mult, L("nadv"), OP.mult)
-        lts(R("LT", 0, 32), R("DIFF"), L("adv"), OP.mult, L("p1"), OP.add)
-        ltt(R("LT", 32, 64), R("LLAY"), R("LT", 0, 32), OP.add)
-        lev.append((cp, (R("LIST"), R("LT", 32, 64))))
-        ltt(L("w6", 3), L("en", 3), R(SN, 0, 3, key=SN + "v"), OP.mult)
-        lev.append((red, (clo, L("w6", 3), OP.add)))
+        lev.append((red, (L("idx"), L("w7"), OP.add)))
+        ltt(L("ch"), L("adv"), L("back"), OP.add)
+        lts(R("SLIST"), R("SBASE"), L("idx"), OP.add, 256.0, OP.mult)
+        lts(R("ULIST", 0, 1), I16C, L("idx"), OP.add, 16.0, OP.mult)
+        ltt(L("w2", 3), L("w1"), hi1, OP.max)
+        lts(L("enc", 3), L("en"), L("ch"), OP.mult)
+        lts(L("w3", 3), L("w2"), L("back"), OP.mult)
+        lev.append((cp, (R(SN, 0, 9), L("t3"))))
+        ltt(L("w4", 3), L("w3"), lo1, OP.subtract)
+        ltt(L("w5", 3), L("w4"), L("enc"), OP.mult)
+        ltt(R(SN, 3, 6), lo1, L("w5"), OP.add)
+        ltt(L("w6", 3), L("en"), R(SN, 3, 6), OP.mult)
+        lev.append((red, (clo, L("w6"), OP.add)))
         lts(R("RC", 0, 1), clo, 0.125, OP.mult)
-        lts(L("x1"), R("RC", 0, 1), AM8B, OP.mult)
-        lts(L("lod"), clo, BE, OP.mult, L("x1"), OP.add)
-        pump(8)
-        tt(R("YY"), R("PX", 0, 128), R("BLK"), OP.mult)
+        lts(L("x1"), R("RC", 0, 1), AM, OP.mult)
+        lts(L("lod"), clo, NB6, OP.mult, L("x1"), OP.add)
+        pump(14)
+        cp(R("PXS", 0, 128), R("PX", 0, 128))
+        PD0, PD1 = R("PD", 0, 16), R("PD", 16, 32)
         pump(1)
-        tt(TRE(0, 64), R("YY", 0, 64), R("YY", 64, 128), OP.add)
+        tt(PD0, IND(R("PXS"), R("LAB", 0, 1)), R("PLS"), OP.add)
         pump(1)
-        tt(TRE(64, 96), TRE(0, 32), TRE(32, 64), OP.add)
+        tt(PD1, IND(R("PXS"), R("LAB", 2, 3)), PD0, OP.subtract)
         pump(1)
-        tt(R("CY", 0, 16), TRE(64, 80), TRE(80, 96), OP.add)
+        ts(R("LN"), PD1, -1.0, OP.mult, 4095.0, OP.min)
+        ts(R("NI", 0, 16), PD1, -1.0, OP.mult)
+        act(R("D"), IND(R("C"), R("LN")))
         pump(1)
-        PD = [R("PD", 16 * k, 16 * k + 16, key="PD%d" % k) for k in range(3)]
-        tt(PD[0], R("CY", 0, 16), R("CY", 1, 17, key=["CY", "CY16"]), OP.subtract)
+        ts(R("NI", 16, 32), R("NI", 0, 16), 4096 + 255, OP.bitwise_and)
         pump(1)
-        tt(PD[1], PD[0], R("PL", 0, 16), OP.add)
-        ts(R("LN"), PD[1], 4095.0, OP.min)
-        NI = [R("NI", 16 * k, 16 * k + 16, key="NI%d" % k) for k in range(2)]
-        cp(NI[0], PD[1])
-        gath(R("D"), CALL, R("LN"))
-        for b in range(16):
-            mm(R("PL", 0, 16), R("LBR", 128 * b, 128 * b + 128), R("D", b, 256, 16), b == 0, b == 15)
-        for b in range(16):
-            mm(R("PC", 0, 16), R("LB1", 128 * b, 128 * b + 128), R("D", b, 256, 16), b == 0, False)
-        ts(NI[1], NI[0], 255, OP.bitwise_and)
+        ts(R("LP"), R("NI", 16, 32), 256.0, OP.min)
         pump(1)
-        cp(R("LP"), NI[1])
-        act(R("E"), IND(GF, R("LP")), ACT.Copy)
-        for b in range(16):
-            mm(R("PC", 0, 16), R("LBE", 128 * b, 128 * b + 128), R("E", b, 256, 16), False, b == 15)
-        ts(PD[2], PD[1], 4096.0, OP.is_ge, 4096.0, OP.mult)
-        ow = [R("OW", 16 * k, 16 * k + 16, key="OW%d" % k) for k in range(4)]
+        cp(R("E"), IND(R("FP"), R("LP")))
+        for h in (0, 1):
+            mm(R("PC", 16 * h, 16 * h + 16), cols("D", h), R("W4"), False, False)
+        for h in (0, 1):
+            mm(R("PC", 16 * h, 16 * h + 16), cols("E", h), R("WE4"), False, h == 1)
+        mm(R("PX", 0, 256), R("IK"), R("E"), True, False)
+        mm(R("PX", 0, 256), R("LQ"), R("D"), False, True)
         pump(2)
-        cp(ow[0], R("PL", 0, 16))
+        ts(R("KQ", 16, 48), R("PC", 0, 32), M8, OP.add, M8, OP.subtract)
+        pump(1)
+        tt(R("KQ", 48, 64), R("PC", 0, 32, 2), R("KQ", 16, 48, 2), OP.subtract)
+        pump(1)
+        tt(R("KQ", 0, 16), R("KQ", 48, 64), R("KQ", 17, 48, 2), OP.add)
+        pump(1)
+        tt(R("OH2"), IND(R("KQ", 0, 48), R("L9", 0, 9)), R("IOT2"), OP.is_equal)
+        mm(R("PI", 72, 144), ONES(128), R("OH2", 0, 72), False, False)
+        mm(R("PI", 0, 144), R("TRI2"), R("OH2"), False, True)
+        ts(R("E2"), R("PX", 0, 256), M1, OP.add, M1, OP.subtract)
+        run("v", V.tensor_tensor_scan, [R("S2")], [R("D0"), R("PI", 0, 144)], 0.0, OP.add, OP.max)
+        pump(1)
+        tt(R("LT2"), IND(R("S2"), R("L16")), R("DEL"), OP.mult)
+        for h in (0, 1):
+            mm(R("PU", 8 * h, 8 * h + 8), cols("LT2", h), R("RA"), True, True)
         pump(2)
-        ts(ow[1], ow[0], 7, OP.bitwise_and)
-        pump(4)
-        cp(ow[2], R("PC", 0, 16))
+        ts(R("DOFF"), R("PU", 0, 16), 256.0, OP.add)
         pump(1)
-        ts(ow[3], ow[2], 2, OP.arith_shift_right)
-        dsx = [R("DS", 16 * k, 16 * k + 16, key="DS%d" % k) for k in range(4)]
-        pump(1)
-        tt(dsx[0], ow[3], PD[2], OP.add)
-        ts(ow[0], ow[3], 3, OP.arith_shift_right)
-        ts(dsx[1], dsx[0], L("B"), OP.is_lt, 8.0, OP.mult)
-        ts(ow[2], ow[3], 7, OP.bitwise_and)
-        tt(dsx[2], ow[1], dsx[1], OP.subtract)
-        CHL = [R("CHL", 16 * k, 16 * k + 16, key="CHL%d" % k) for k in range(2)]
-        cp(CHL[0], ow[0])
-        for o in range(8):
-            ts(R("OH2", 16 * o, 16 * o + 16), dsx[2], float(o - 8), OP.is_equal)
-        cp(CHL[1], ow[2])
-        run("v", V.tensor_tensor_scan, [R("S1")], [R("D0"), R("OH2")], 0.0, OP.mult, OP.add)
-        mm(R("PR", 0, 128), R("NTB"), R("OH2"), True, False)
-        mm(R("PR", 0, 128), R("ONE0"), R("OC"), False, False)
-        mm(R("PR", 0, 128), R("BLK"), R("S1"), False, True)
-        ts(dsx[0], dsx[2], 0.0, OP.is_ge)
-        REPA = R("REPL", 16, 32, key="REPA")
-        tt(R("XH"), IND(CHL[0], REPA), R("DEL"), OP.mult)
-        tt(dsx[3], dsx[0], R("TR"), OP.mult)
-        tt(R("W2"), R("PR", 0, 128), R("OH2"), OP.mult)
-        pump(1)
-        tt(TRE(0, 64), R("W2", 0, 64), R("W2", 64, 128), OP.add)
-        pump(1)
-        tt(TRE(64, 96), TRE(0, 32), TRE(32, 64), OP.add)
-        pump(1)
-        tt(TRE(96, 112), TRE(64, 80), TRE(80, 96), OP.add)
-        pump(1)
-        tt(dsx[1], TRE(96, 112), dsx[3], OP.add)
-        tt(R("XL"), IND(CHL[1], REPA), R("DEL"), OP.mult)
-        mm(R("PY", 0, 256), R("BR", 0, 128), R("XH"), True, False)
-        mm(R("PY", 0, 256), R("BR", 128, 256), R("XL"), False, True)
-        act(R("E"), R("PY", 0, 256), ACT.Copy)
-        cp(R("DOFF"), dsx[1])
-        pump(1)
-        scat(R("SEND"), R("DOFF"), R("D"))
-        scat(R("SEND", 32, 1024), R("DOFF"), R("E"))
-        act(R("WIN", 2048 + 64 * rank, 2112 + 64 * rank, key="NEW"), R("SEND", 64 * rank, 64 * rank + 64), ACT.Copy)
-        before("p", ["SEND"], [])
-        to_all(lambda c: T.SEND[:, 64 * T.rank_of(c):64 * T.rank_of(c) + 64], T.WIN[:, 2048 + 64 * rank:2112 + 64 * rank], "rn", "ln")
+        for buf, src, win, rs, ls in (("SEND", "D", "WS", "rn", "ln"), ("SENDC", "E2", "WC", "rc", "lc")):
+            scat(R(buf), R("DOFF"), R(src))
+            act(R(win, land + 32 * rank, land + 32 * rank + 32), R(buf, 32 * rank, 32 * rank + 32))
+            before("p", R(buf)[0], [])
+            to_all(lambda c: T[buf][:, 32 * T.rank_of(c):32 * T.rank_of(c) + 32], T[win][:, land + 32 * rank:land + 32 * rank + 32], rs, ls)
         pump(99)
 
-    wait("v", "rn", per * RO)
-    scat(R("WIN", 512, 2048, key="LU"), R("UPL"), R("WIN", 2048, 2560, key="NEW"))
-    before("y", ["LU"], [])
-    for l in (1, 2, 3):
-        g.sync.dma_start(T.yl[:, 256 * (l - 1):256 * l], T.WIN[:, 512 * l:512 * l + 256]).then_inc(T.sem.dout, 16)
-        o = R(("PT", "PX", "PY")[l - 1], 0, 256, p=8)
-        mm(o, R("W81"), R("WIN", 512 * l + 256, 512 * l + 512, key="LU"), True, True)
-        cp(R("YF", 256 * (l - 1), 256 * l, p=8), o)
     SF = "ST%d" % (RO % 2)
-    before("y", ["YF", SF + "v", SF + "e", SF + "U"], [])
+    for l in range(3):
+        ts(R("OLIST", 16 * l, 16 * l + 16), R("SBASE", 0, 16), R(SF, l, l + 1), OP.add, 256.0, OP.mult)
+    before("y", R(SF)[0], [])
+    g.sync.dma_start(T.yt[:, :], T[SF][0:128:16, 3:11]).then_inc(T.sem.dout, 16)
+    wait("v", "rn", per * RO)
+    wait("a", "rc", per * RO)
+    cp(R("YL"), IND(R("WS"), R("OLIST")))
+    before("y", R("YL")[0], [])
+    g.sync.dma_start(T.yl[:, :], T.YL[:, :]).then_inc(T.sem.dout, 16)
+    for l in range(3):
+        act(R("YC", 256 * l, 256 * l + 256), IND(R("WC"), R("OLIST", 16 * l, 16 * l + 16)))
+        o = R(("PT0", "PX", "PL")[l], 0, 256, p=8)
+        mm(o, R("W81"), R("YC", 256 * l, 256 * l + 256), True, True)
+        cp(R("YF", 256 * l, 256 * l + 256, p=8), o)
+    before("y", R("YF")[0], [])
     g.sync.dma_start(T.yf[:, :], T.YF[0:8, :]).then_inc(T.sem.dout, 16)
-    g.sync.dma_start(T.yt[:, :], T[SF][0:128:16, :]).then_inc(T.sem.dout, 16)
-    for sem, val in (("dout", 80), ("lt", per * RO), ("ln", per * RO), ("sv", cnt["v"]), ("st", cnt["t"]), ("sa", cnt["a"]), ("sp", cnt["p"])):
+    for sem, val in (("dout", 48), ("lt", per * RO), ("ln", per * RO), ("lc", per * RO), ("rt", per * RO), ("rn", per * RO), ("rc", per * RO),
+                     ("sv", cnt["v"]), ("st", cnt["t"]), ("sa", cnt["a"]), ("sp", cnt["p"])):
         g.wait_ge(T.sem[sem], val)

@@ -3,8 +3,9 @@ from concourse.mybir import AluOpType, AxisListType, ActivationFunctionType
 import comms_topo
 
 N, RO, J = 8, 8, 16
-HACT = 10
-MACT = ((2, 7), (5, 5), (2, 2))
+HACT = 7
+PUMP = 0
+MACT = ((1, 4), (4, 4), (2, 2))
 WT = [1, 3, 7, 13, 21, 35, 49, 67, 85, 107, 129, 155, 181, 211, 241, 253]
 KA = [17, 101, 263, 389, 547, 701, 859, 1021, 1171, 1319, 1487, 1637, 1801, 1949, 2111, 2269]
 M1, M8 = 1.5 * 2 ** 23, 1.5 * 2 ** 26
@@ -12,27 +13,27 @@ EPS = 2.0 ** -10
 BF, F32, I32, U16 = "bfloat16", "float32", "int32", "uint16"
 _B = {
     "OPR": (8192, BF), "CR": (4096, BF), "C": (4096, BF), "WS": (2560, BF), "WC": (2560, BF), "SREP": (512, BF), "FP": (272, BF),
-    "MA": (3840, BF), "MB": (1792, BF), "OH": (2048, BF), "A": (4096, BF), "H": (4096, BF), "OG": (1024, BF),
+    "MA": (3840, BF), "MB": (1792, BF), "OH": (2048, BF), "A": (4096, BF), "H0": (2048, BF), "H1": (2048, BF), "OG": (1024, BF),
     "D1": (256, BF), "DB": (256, BF), "DC": (256, BF), "OK": (256, BF), "F": (256, BF), "KEP": (256, BF), "ZR": (256, BF), "BR": (256, BF),
-    "MK": (512, BF), "TOTB": (256, BF), "D": (256, BF), "E": (256, BF), "E2": (256, BF), "OH2": (144, BF), "LT2": (256, BF),
+    "MK": (256, BF), "TOTB": (256, BF), "D": (256, BF), "E": (256, BF), "E2": (256, BF), "OH2": (144, BF), "LT2": (256, BF),
     "SEND": (512, BF), "SENDC": (512, BF), "SC": (256, BF), "L1": (128, BF), "L2": (128, BF), "L3": (128, BF), "LQ": (128, BF),
     "YL": (768, BF), "YC": (768, BF),
     "ONES": (256, BF), "Z256": (256, BF), "C32": (128, BF), "C24": (128, BF), "IDB": (128, BF), "NID": (128, BF), "TB1": (256, BF), "TB2": (256, BF),
-    "BLK": (128, BF), "W16": (16, BF), "W4": (16, BF), "WE4": (16, BF), "WF": (256, BF), "CST": (256, BF), "LBW": (144, BF), "JS": (144, BF),
-    "TRIM": (128, BF), "TRI2": (128, BF), "I8R": (256, BF), "LE0": (256, BF), "LE1": (256, BF), "LI0": (256, BF), "LI1": (256, BF),
+    "BLK": (128, BF), "W16": (16, BF), "W4": (16, BF), "WE4": (16, BF), "WF": (128, BF), "CST": (512, BF), "LBW": (144, BF), "JS": (144, BF),
+    "TRIM": (128, BF), "TRI2": (128, BF), "I8R": (256, BF), "LE0": (256, BF), "LE1": (256, BF), "LI": (128, BF),
     "BD15": (64, BF), "ST15": (256, BF), "SR15": (128, BF), "BD7": (64, BF), "ST7": (256, BF), "SR7": (128, BF),
     "OC2": (144, BF), "IOT2": (144, BF), "D0": (144, BF), "IO256": (256, BF), "W81": (8, BF), "DEL": (256, BF), "RA": (8, BF), "IK": (128, BF),
     "ROWI": (128, BF), "J16": (16, F32),
     "IDF": (128, F32), "ONEF": (128, F32), "G8F": (128, F32), "TREE": (128, F32), "I16": (16, F32), "I8": (8, F32), "VEC": (80, F32),
     "KT": (256, F32), "KU": (256, F32), "Y0": (256, F32), "ZO": (256, F32), "SBASE": (32, F32), "IO9": (12, F32), "SELA": (16, F32), "RB": (32, F32),
-    "COL": (32, F32), "ST0": (11, F32), "ST1": (11, F32), "LW": (128, F32), "MS": (4, F32), "XB0": (32, F32), "XB1": (32, F32),
-    "MX": (4, F32), "MJ": (16, F32), "PXS": (136, F32), "PLS": (16, F32), "PD": (32, F32), "KQ": (64, F32), "S2": (144, F32), "YF": (768, F32),
+    "COL": (32, F32), "ST0": (11, F32), "ST1": (11, F32), "LW": (128, F32), "XB0": (32, F32), "XB1": (32, F32),
+    "MX": (4, F32), "MJ": (16, F32), "PXS": (136, F32), "PLS": (32, F32), "PD": (64, F32), "KQ": (64, F32), "S2": (144, F32), "YF": (768, F32),
     "F0": (256, I32), "UT": (160, I32), "UI": (48, I32), "HI": (256, I32), "HM": (256, I32), "NI": (32, I32), "RC": (2, I32), "MI": (1, I32),
     "OFFC": (256, U16), "SLIST": (32, U16), "ULIST": (2, U16), "LN": (16, U16), "LP": (16, U16), "DOFF": (16, U16), "REPL": (16, U16),
     "LAB": (4, U16), "L9": (10, U16), "L16": (16, U16), "OLIST": (48, U16),
 }
 _PS = ["PT0", "PT1", "PU", "PC", "PI", "PR", "PX", "PL"]
-_JOIN = {"ORD": ("LE0", "LE1", "LI0", "LI1"), "KM": ("ST15", "ST7", "SR15", "SR7", "BD15", "BD7"), "WTS": ("W16", "W4", "WE4", "W81", "RA")}
+_JOIN = {"ORD": ("LE0", "LE1", "LI"), "KM": ("ST15", "ST7", "SR15", "SR7", "BD15", "BD7"), "WTS": ("W16", "W4", "WE4", "W81", "RA")}
 _AT = {k: (k, 0, n) for k, (n, d) in _B.items()}
 for _k, _names in _JOIN.items():
     _B[_k] = (0, BF)
@@ -147,8 +148,8 @@ def rank_program(g, core, T, topo):
             act(R(name, n, 2 * n), R(name, 0, n))
             n *= 2
 
-    ICOL, WCOL, RCOL, WY, W81C, CF, AM, NB6, PCOL, I16C = [R("COL", i, i + 1) for i in range(10)]
-    TMP = [R("COL", i, i + 1) for i in range(10, 32)]
+    ICOL, WCOL, RCOL, WY, W81C, CF, AM, NB6, PCOL, I16C, PC1 = [R("COL", i, i + 1) for i in range(11)]
+    TMP = [R("COL", i, i + 1) for i in range(11, 32)]
 
     g.sync.dma_start(T.WS[:, 0:256], T.s0[:, :]).then_inc(T.sem.ds0, 16)
     after("ds0", 16, [], R("WS", 0, 256)[0])
@@ -207,7 +208,7 @@ def rank_program(g, core, T, topo):
     fill(L("e811"), -0.25)
     for j in range(J):
         fill(R("KT", 16 * j, 16 * j + 16), float(KA[j]))
-    lin(R("ST15"), ONES(256), 1.0)
+    step(R("ST15"), ONES(256), 2.0)
     lin(R("ST7"), ONES(256), 1.0)
     lin(R("ONEF"), ONES(128), 1.0)
     act(R("I8R", 0, 8), R("I8"))
@@ -223,7 +224,7 @@ def rank_program(g, core, T, topo):
     sel(R("TRIM"), R("TB2", 128, 256), [[1, 128]], OP.not_equal, 0, -1, -256.0)
     for t in (0, 1):
         sel(R("LE%d" % t), R("I8R"), [[8, 2], [16, 16], [2, 8]], OP.is_gt, -8 * t, -2)
-        sel(R("LI%d" % t), R("I8R"), [[8, 2], [16, 16], [2, 8]], OP.is_ge, -8 * t, -2)
+    sel(R("LI"), R("I8R", 0, 128), [[8, 16], [1, 8]], OP.is_ge, 0, -1)
     iota(R("IO256"), [[1, 256]], 0, 0)
     iota(R("TB1", 0, 128), [[0, 8], [1, 16]], -2, 0)
     sel(R("TB1", 128, 256), R("TB1", 0, 128), [[-16, 8], [0, 16]], OP.is_ge, 0, 1, -9.0)
@@ -245,16 +246,15 @@ def rank_program(g, core, T, topo):
         red(CF, TRE(16, 32), OP.add)
         ts(TMP[0], ROW(5), 8.0, OP.mult, ROW(6), OP.add)
         ts(TMP[1], R("IDB", 0, 1), 896.0, OP.mult)
-        ts(R("W16", 0, None, 2), BLK8, 0.25, OP.mult)
+        ts(R("W16", 0, 8), BLK8, 0.25, OP.mult)
         tt(WY, TMP[0], W81C, OP.add)
         ts(TMP[2], R("IDB", 1, 2), 4.125, OP.mult, TMP[1], OP.add)
-        ts(R("W16", 1, None, 2), BLK8, RCOL, OP.mult)
-        fill(R("WF", 1, 16, 2), 0.0)
-        ts(R("WF", 0, 16, 2), BLK8, WY, OP.mult)
+        ts(R("W16", 8, 16), BLK8, RCOL, OP.mult)
+        ts(R("WF", 0, 8), BLK8, WY, OP.mult)
         lin(R("NID"), R("IDB"), -1.0)
-        lin(R("CST", 0, None, 2), ONES(128), TMP[2])
-        lin(R("CST", 1, None, 2), ONES(128), -3.5 / 128)
-        spread("WF", 16, 256)
+        lin(R("CST", 0, 256), ONES(256), TMP[2])
+        lin(R("CST", 256, 512), ONES(256), -3.5 / 128)
+        spread("WF", 8, 128)
         lin(R("SC"), ONES(256), CF)
         act(R("WC", 256, 512), R("SC"))
         ts(R("HI"), R("F0"), 3, OP.arith_shift_right)
@@ -270,19 +270,22 @@ def rank_program(g, core, T, topo):
         lin(R("C32"), ONES(128), 32.5)
         lin(R("C24"), ONES(128), 24.0)
         act(R("IDF"), R("IDB"))
-        fill(R("MS"), 0.0)
+        for xb in ("XB0", "XB1"):
+            fill(R(xb, 4 * rank, 4 * rank + 4), 0.0)
+        fill(L("idx"), 0.0)
+        ts(PC1, PCOL, 128.0, OP.add)
         fill(R("JS"), 0.0)
         fill(R("RB"), 0.0)
         fill(R("PXS", 128, 136), 0.0)
         fill(R("ST0", 0, 3), 1.0)
         fill(R("ST0", 3, 10), 0.0)
         fill(R("ST0", 10, 11), 1023.0)
-        ts(R("JS", 15, 128, 16), R("I8"), 128.0, OP.mult)
+        ts(R("JS", 15, 128, 16), R("I8"), 256.0, OP.mult)
 
     def constants_2():
-        for i in range(16):
-            cp(R("G8F", i, None, 16), R("I8"))
+        cp(R("LN"), IO16)
         ts(R("SBASE"), R("SBASE"), 1.0 / 256, OP.mult)
+        cp(R("G8F"), IND(R("I8"), R("LN", 0, 8)))
         ts(I16C, ICOL, 1.0 / 16, OP.mult)
         ts(AM, ROW(6), 8.0, OP.mult, ROW(5), OP.subtract)
         ts(NB6, ROW(6), -1.0, OP.mult)
@@ -305,8 +308,9 @@ def rank_program(g, core, T, topo):
             ts(R("SELA", 8 * h, 8 * h + 8), BLK8, ROW(0), OP.mult, -EPS, OP.mult)
         cp(R("RA"), BLK8)
         ts(R("W81"), BLK8, W81C, OP.mult)
-        act(R("DEL", 0, 16), R("I16"))
-        spread("DEL", 16, 256)
+        cp(R("DEL"), IND(R("I16"), R("REPL")))
+
+    def constants_5():
         lin(R("IOT2"), R("OC2"), 1.0, -3.5)
         lin(R("IOT2", 8, None, 9), ONES(16), 8.0)
         lin(R("OC2"), R("OC2"), 0.25, -10.0)
@@ -315,15 +319,19 @@ def rank_program(g, core, T, topo):
 
     def constants_4():
         ts(R("PD", 0, 9), R("PD", 0, 9), ICOL, OP.add)
-        ts(TMP[11], PCOL, -1.0, OP.mult, 129.0, OP.add)
+        ts(TMP[11], PCOL, ICOL, OP.subtract, 0.5, OP.mult)
+        ts(TMP[12], ICOL, 8.0, OP.is_ge, 56.0, OP.mult)
         ts(R("NI", 0, 9), R("PD", 0, 9), 1.0 / 9, OP.mult, -4.0 / 9, OP.add)
-        ts(TMP[12], TMP[11], ROW(0), OP.mult, PCOL, OP.add)
+        ts(TMP[13], TMP[11], ICOL, OP.add, TMP[12], OP.add)
+        ts(TMP[14], TMP[11], -1.0, OP.mult, 129.0, OP.add)
         ts(R("PD", 16, 25), R("NI", 0, 9), -9.0, OP.mult, -8.0, OP.add)
-        ts(R("LAB", 2, 3), TMP[12], -1.0, OP.add)
+        ts(TMP[15], ROW(8), -56.0, OP.mult, TMP[13], OP.add)
+        cp(R("LAB", 0, 1), TMP[13])
         tt(R("PD", 0, 9), R("PD", 0, 9), R("PD", 16, 25), OP.add)
-        cp(R("LAB", 0, 1), PCOL)
+        ts(TMP[16], TMP[14], ROW(0), OP.mult, TMP[15], OP.add)
         ts(R("PD", 16, 25), R("NI", 0, 9), 17.0, OP.add)
         ts(R("PD", 0, 9), R("PD", 0, 9), 0.0, OP.is_equal)
+        ts(R("LAB", 2, 3), TMP[16], -1.0, OP.add)
         ts(R("L16"), IO16, 9.0, OP.mult, 8.0, OP.add)
         tt(R("PD", 0, 9), R("PD", 0, 9), R("PD", 16, 25), OP.mult)
         tt(R("PD", 16, 25), R("PD", 0, 9), R("NI", 0, 9), OP.add)
@@ -375,21 +383,24 @@ def rank_program(g, core, T, topo):
         cp(R("UT", 16 * new, 16 * new + 16), R("PU", 0, 16))
         ts(um, IND(R("UT", 0, 16 * (rnd + 2)), R("ULIST", 0, 1)), 4095, OP.bitwise_and)
         tt(sq, um, um, OP.mult)
-        for a, b in ((0, 64), (64, 256)):
-            rep = R("REPL", a // 16, b // 16)
-            tt(R("KU", a, b), IND(um, rep), R("KT", a, b), OP.mult)
-            if a == 0:
-                ts(s4, sq, 1.0 / 16, OP.mult, L("e811"), OP.add)
-            tt(R("HI", a, b), IND(s4, rep), R("KU", a, b), OP.add)
-            ts(R("HM", a, b), R("HI", a, b), 8191, OP.bitwise_and)
-            cp(R("OFFC", a, b), R("HM", a, b))
+        ku = lambda a, b: tt(R("KU", a, b), IND(um, R("REPL", a // 16, b // 16)), R("KT", a, b), OP.mult)
+        hi = lambda a, b: tt(R("HI", a, b), IND(s4, R("REPL", a // 16, b // 16)), R("KU", a, b), OP.add)
+        hm = lambda a, b: ts(R("HM", a, b), R("HI", a, b), 8191, OP.bitwise_and)
+        of = lambda a, b: cp(R("OFFC", a, b), R("HM", a, b))
+        ku(0, 64)
+        ts(s4, sq, 1.0 / 16, OP.mult, L("e811"), OP.add)
+        for f, a, b in ((ku, 64, 160), (hi, 0, 64), (hi, 64, 160), (hm, 0, 64), (ku, 160, 256), (of, 0, 64), (hm, 64, 160), (hi, 160, 256),
+                        (of, 64, 160), (hm, 160, 256)):
+            f(a, b)
         if rnd == 0:
-            constants_1()
+            of(160, 256)
+            for f in (constants_1, constants_2, constants_4, constants_3):
+                f()
         for c, bank in ((0, "PX"), (1, "PR")):
             mm(R(bank), R("IDB"), R("SREP"), True, False, inc=True)
             act(R("OG", 512 * c, 512 * c + 512), IND(R("OPR"), R("OFFC", 32 * c, 32 * c + 32)))
-        for h in (0, 1):
-            mm(R("PT%d" % h, 0, 256), ONES(128), R("CST"), True, False, inc=True)
+        for s in (0, 1):
+            mm(R("PT%d" % s, 0, 256), ONES(128), R("CST", 256 * s, 256 * s + 256), True, False, inc=True)
         for c, bank in ((0, "PX"), (1, "PR")):
             mm(R(bank), R("NID"), R("OG", 512 * c, 512 * c + 512), False, True)
         for c in (0, 2, 1, 3, 4, 5, 6, 7, 8):
@@ -399,29 +410,23 @@ def rank_program(g, core, T, topo):
                 cr = R(("PX", "PR")[c])
             else:
                 tt(cr, IND(R("OPR"), R("OFFC", a // 16, (a + n) // 16)), R("SREP", 0, n), OP.subtract)
+            if c == 2 and rnd:
+                of(160, 256)
             act(R("C", a, a + n), cr, ACT.Abs)
-            for x in range(a // 128, (a + n) // 128):
-                mm(R("PT%d" % (x % 2), 16 * (x // 2), 16 * (x // 2) + 16), R("C", 128 * x, 128 * x + 128), R("W16"), False, x >= 30, inc=True)
-            if c == 1:
+            if c == 8:
                 if rnd:
-                    wait("a", "rc", per * rnd)
-                act(R("FP", 0, 256), IND(R("WC", 0, land), R("SLIST", 0, 16)), ACT.Identity, bias=L("lod"))
+                    wait("v", "rc", per * rnd)
+                ts(R("FP", 0, 256), IND(R("WC", 0, land), R("SLIST", 0, 16)), L("lod"), OP.add)
                 for h in (0, 1):
-                    mm(R("PT%d" % h, 0, 256), cols("FP", h), R("WF"), False, False, inc=True)
-        PY = lambda h: R("PT%d" % h, 0, 256, 2)
-        PV = lambda h: R("PT%d" % h, 1, 256, 2)
-
-        def owners(h):
-            ts(cols("ZO", h), PV(h), M8, OP.add, M8, OP.subtract)
-            tt(cols("OK", h), PV(h), cols("ZO", h), OP.subtract)
+                    mm(cols("PT0", h), cols("FP", h), R("WF"), False, False, inc=True)
+            for s in (1, 0):
+                for x in range(a // 128, (a + n) // 128):
+                    at = 128 * (x % 2) + 8 * (x // 2)
+                    mm(R("PT%d" % s, at, at + 8), R("C", 128 * x, 128 * x + 128), R("W16", 8 * s, 8 * s + 8), False, x == 31, inc=(x + 1) * 128 == a + n)
 
         def hots(h):
             for o in range(8):
                 ts(half("OH", o, 8, h), cols("OK", h), o - 3.5, OP.is_equal)
-
-        def far(h):
-            act(cols("F", h), PY(h), ACT.Relu, scale=-65536.0, bias=65536.0 * 899.9375)
-            act(cols("Y0", h), PY(h))
 
         def masks(K, M, src, thr, na, h):
             for k in range(K - na, K):
@@ -445,33 +450,59 @@ def rank_program(g, core, T, topo):
             mm(R("PX", 128 * h, 128 * h + 128), cols("Y0", h), R("IDF"), True, False, inc=True)
             mm(R("PX", 128 * h, 128 * h + 128), cols("F", h), R("IDB"), False, True)
         th1 = lambda k: 128.0 * k + 900.0
-        far(1)
-        owners(0)
-        far(0)
-        hots(0)
+        act(R("F"), R("PT0", 0, 256), ACT.Relu, scale=-65536.0, bias=65536.0 * 899.9375)
         for h in (0, 1):
-            tt(cols("D1", h), PY(h), cols("F", h), OP.add)
-        turn(1)
+            ts(cols("ZO", h), cols("PT1", h), M8, OP.add, M8, OP.subtract)
+        for h in (0, 1):
+            tt(cols("OK", h), cols("PT1", h), cols("ZO", h), OP.subtract)
+        for h in (0, 1):
+            tt(cols("D1", h), cols("PT0", h), cols("F", h), OP.add)
+        hots(0)
         masks(7, "MB", "D1", th1, MACT[0][0], 0)
         count(7, "MB", 0)
-        owners(1)
-        masks(7, "MB", "D1", th1, MACT[0][1], 1)
         hots(1)
-        for h in (0, 1):
-            mm(PA(h), R("NID"), cols("F", h), True, False, inc=True)
+        masks(7, "MB", "D1", th1, MACT[0][1], 1)
+        act(R("Y0"), R("PT0", 0, 256))
         count(7, "MB", 1)
-        act(R("SEND", 0, 256), R("Z256")) if rnd == 0 else None
+        for h in (1, 0):
+            mm(PA(h), R("NID"), cols("F", h), True, False, inc=True)
         if rnd:
             wait("a", "ln", per * rnd)
-            act(R("SEND", 0, 256), R("Z256"))
-        else:
-            constants_2()
+        act(R("SEND", 0, 256), R("Z256"))
+        clo, e, U, m = L("clo"), R(ST, 9, 10), R(ST, 10, 11), R("MI")
+        eN, UN = R(SN, 9, 10), R(SN, 10, 11)
+        lts = lambda *x: lev.append((ts, x))
+        ltt = lambda *x: lev.append((tt, x))
+        L("t2", 9)
+        lts(L("nel", 9), R("IO9", 0, 9), e, OP.not_equal)
+        lts(L("w1", 3), R(ST, 3, 6), 1.0, OP.add)
+        lts(L("el", 3), R("IO9", 0, 3), e, OP.is_equal)
+        lts(L("em", 3), R("IO9", 9, 12), e, OP.is_equal)
+        ltt(L("W", 3), L("w1"), R(ST, 6, 9), OP.max)
+        lts(L("em2", 3), R("IO9", 0, 3), 2.0, OP.add, e, OP.is_equal)
+        ltt(L("t1", 9), R(ST, 0, 9), L("nel"), OP.mult)
+        ltt(L("w2", 3), L("W"), L("em"), OP.mult)
+        ltt(L("dv", 3), L("W"), R(ST, 3, 6), OP.subtract)
+        ltt(L("w3", 3), R(ST, 0, 3), L("em2"), OP.mult)
+        lev.append((red, (L("wprev"), L("w2"), OP.add)))
+        ltt(L("dvm", 3), L("dv"), L("em"), OP.mult)
+        lev.append((red, (L("pprev"), L("w3"), OP.add)))
+        lts(L("t2", a=0, b=3), L("el"), float(rnd + 2), OP.mult)
+        lts(L("n2"), e, 2.0, OP.is_lt, 4096.0, OP.mult)
+        lts(L("ne2"), e, 2.0, OP.is_lt)
+        lts(L("g0"), e, 0.0, OP.is_gt)
+        lts(L("da"), L("idx"), -1.0, OP.mult, float(rnd + 2), OP.add)
+        ltt(L("db"), L("pprev"), L("idx"), OP.subtract)
+        lts(R("LQ"), R("ROWI"), e, OP.is_equal, 0.25, OP.mult)
+        pump(8)
         digit(7, "L1", 0, 128)
         for h in (0, 1):
             mm(PA(h), R("L1", p=58), cols("ST7", h, 58), False, True)
         turn(0)
+        turn(1)
         for h in (0, 1):
             tt(cols("DB", h), cols("Y0", h), PA(h), OP.subtract)
+        for h in (0, 1):
             masks(15, "MA", "DB", lambda k: 8.0 * k - 0.1875, MACT[1][h], h)
             mm(PB(h), R("NID"), cols("F", h), True, False, inc=True)
             mm(PB(h), R("L1", p=58), cols("ST7", h, 58), False, False, inc=True)
@@ -480,27 +511,37 @@ def rank_program(g, core, T, topo):
         if rnd:
             wait("a", "lc", per * rnd)
         else:
-            constants_3()
+            constants_5()
         act(R("SENDC", 0, 256), R("SC"))
+        pump(1)
         ts(R("MJ"), R("J16"), R("MX", 3, 4), OP.mult)
+        pump(4)
         digit(15, "L2", 1, 8)
         for h in (0, 1):
             mm(PB(h), R("L2", p=121), cols("ST15", h, 121), False, True)
         mm(R("PU", 16, 32), R("G8F"), R("MJ"), True, True)
         for h in (0, 1):
             tt(cols("DC", h), cols("Y0", h), PB(h), OP.subtract)
+        for h in (0, 1):
             masks(7, "MB", "DC", lambda k: k - 0.125, MACT[2][h], h)
             count(7, "MB", h)
-            mm(PB(h), ONES(128), R("C24"), True, False, inc=True) if h == 0 else None
+            if h == 0:
+                for t in (0, 1):
+                    mm(PB(t), ONES(128), R("C24"), True, False, inc=True)
         if rnd:
             wait("v", "lt", per * rnd)
-        else:
-            constants_4()
-        red(R("MS", 1, 2), R("PU", 16, 32), OP.min)
+        red(R(XB, 4 * rank + 1, 4 * rank + 2), R("PU", 16, 32), OP.min)
+        pump(7)
         digit(7, "L3", 2, 1)
         for h in (0, 1):
             mm(PA(h), R("L3", p=56), cols("ST7", h, 56), True, True)
-        mm(PB(1), ONES(128), R("C24"), True, False, inc=True)
+        mm(R("PU", 0, 1), R("SR7", p=56), R("L1", 0, 1, p=56), True, False)
+        mm(R("PU", 0, 1), R("SR15", p=120), R("L2", 0, 1, p=120), False, False)
+        mm(R("PU", 0, 1), R("SR7", p=56), R("L3", 0, 1, p=56), False, True)
+        act(R(XB, 4 * rank, 4 * rank + 1), R("PU", 0, 1))
+        mine = T[XB][:, 4 * rank:4 * rank + 4]
+        before("p", R(XB, 4 * rank, 4 * rank + 4)[0] + R("SREP")[0] + R("FP")[0] + R("UT")[0], [])
+        to_all(lambda c: mine, mine, "rt", "lt")
         for h in (0, 1):
             tt(cols("KEP", h), cols("DC", h), PA(h), OP.is_lt)
             mm(R("PL", h, h + 1), cols("KEP", h), ONES(1), True, True)
@@ -512,108 +553,92 @@ def rank_program(g, core, T, topo):
             for t in (0, 1):
                 mm(PB(h), cols("TOTB", t), cols("LE%d" % t, h), False, t == 1)
         for t in (0, 1):
-            for t2 in (0, 1):
-                mm(R("PL", 2 + t, 3 + t), cols("LI%d" % t2, t), R("TOTB", 128 * t2, 128 * t2 + 1), t2 == 0, t2 == 1)
-        mm(R("PU", 0, 1), R("SR7", p=56), R("L1", 0, 1, p=56), True, False)
-        mm(R("PU", 0, 1), R("SR15", p=120), R("L2", 0, 1, p=120), False, False)
-        mm(R("PU", 0, 1), R("SR7", p=56), R("L3", 0, 1, p=56), False, True)
-        act(R("MS", 0, 1), R("PU", 0, 1))
-        before("p", R("MS")[0] + R("SREP")[0] + R("FP")[0] + R("UT")[0], [])
-        to_all(lambda c: T.MS[:, 0:4], T[XB][:, 4 * rank:4 * rank + 4], "rt", "lt")
-        for h in (0, 1):
-            ts(cols("ZR", h), PB(h), -7.5, OP.add)
-            tt(cols("BR", h), PB(h), cols("ZR", h), OP.subtract)
-            for c in range(16 - HACT, 16):
-                step(half("H", c, 16, h), cols("ZR", h), 2816.0 + 16 * c + 8)
-            if h == 0:
-                for t in (0, 1):
-                    ts(R("MK", 256 * t, 256 * t + 256), R("IO256"), R("PL", 2 + t, 3 + t), OP.is_ge)
-                for t in (0, 1):
-                    for k in range(16):
-                        mm(R("PU", 0, 16), R("JS", 15 - k, 143 - k), R("MK", 256 * t + k, 256 * t + 256, 16), t == 0 and k == 0, t == 1 and k == 15)
+            mm(R("PL", 2, 3), R("LI"), R("TOTB", 128 * t, 128 * t + 1), t == 0, t == 1)
+        ts(cols("ZR", 0), PB(0), -7.5, OP.add)
+        lin(cols("ZR", 1), PB(1), 1.0, -7.5)
+        ts(R("MK"), R("IO256"), R("PL", 2, 3), OP.is_ge)
+        for k in range(16):
+            mm(R("PU", 0, 16), R("JS", 15 - k, 143 - k), R("MK", k, 256, 16), k == 0, k == 15)
+        tt(cols("BR", 0), PB(0), cols("ZR", 0), OP.subtract)
+        mm(R("PX", 0, 128), R("IDB"), R("Z256", 0, 128), True, False, inc=True)
+
+        def steps(h, s):
+            for c in range(8):
+                out, thr = half("H%d" % s, c, 8, h), 2816.0 + 16 * (8 * s + c) + 8
+                if s:
+                    step(out, cols("ZR", h), thr)
+                else:
+                    ts(out, cols("ZR", h), thr, OP.is_lt)
+
+        def places(h):
             for c in range(16):
-                ts(half("A", c, 16, h), cols("BR", h), float(c), OP.is_equal, PCOL, OP.mult)
-            for c in range(16 - HACT):
-                ts(half("H", c, 16, h), cols("ZR", h), 2816.0 + 16 * c + 8, OP.is_lt)
+                ts(half("A", c, 16, h), cols("BR", h), float(c), OP.is_equal, (PCOL, PC1)[h], OP.mult)
+
+        def sums(h, s):
             for x in range(16 * h, 16 * h + 16):
-                mm(R("PX", 0, 128), R("A", 128 * x, 128 * x + 128), R("H", 128 * x, 128 * x + 128), x == 0, x == 31)
-        act(R(XB, 4 * rank, 4 * rank + 2), R("MS", 0, 2))
-        act(R("PLS"), R("PU", 0, 16))
+                mm(R("PX", 64 * s, 64 * s + 64), R("A", 128 * x, 128 * x + 128), R("H%d" % s, 64 * x, 64 * x + 64), False, (x, s) == (31, 0))
+        steps(0, 1)
+        steps(1, 1)
+        steps(0, 0)
+        tt(cols("BR", 1), PB(1), cols("ZR", 1), OP.subtract)
+        places(0)
+        sums(0, 0)
+        sums(0, 1)
+        places(1)
+        sums(1, 1)
+        steps(1, 0)
+        sums(1, 0)
+        mm(R("PI", 0, 144), ONES(128), R("OC2"), True, False, inc=True)
+        pump(99)
+        cp(R("PLS", 0, 16), R("PU", 0, 16))
+        ts(R("PLS", 16, 32), R("PU", 0, 16), 4096.0, OP.is_ge, 256.0, OP.mult)
         wait("v", "rt", per * (rnd + 1))
         red(L("TG"), R(XB, 0, None, 4), OP.min)
         red(L("MG"), R(XB, 1, None, 4), OP.min)
-        clo, e, U, m = L("clo"), R(ST, 9, 10), R(ST, 10, 11), R("MI")
-        eN, UN = R(SN, 9, 10), R(SN, 10, 11)
-        ts(L("B"), L("TG"), clo, OP.add, 1023.0, OP.min)
-        ts(m, L("MG"), clo, OP.add, -900.5, OP.add)
-        ts(L("TB"), L("B"), clo, OP.subtract, 0.125, OP.subtract)
-        ts(R("LQ"), R("ROWI"), e, OP.is_equal, 0.25, OP.mult)
-        ts(R("RB", 1, None, 2), R("SELA"), L("TB"), OP.mult)
-        mm(R("PC", 0, 32), R("ONEF"), R("RB"), True, False, inc=True)
-        mm(R("PI", 0, 144), ONES(128), R("OC2"), True, False, inc=True)
-        lts = lambda *x: lev.append((ts, x))
-        ltt = lambda *x: lev.append((tt, x))
-        lts(L("e2"), e, 2.0, OP.is_equal)
-        lts(L("ne2"), e, 2.0, OP.is_lt)
-        lts(L("g0"), e, 0.0, OP.is_gt)
-        lts(L("nel", 9), R("IO9", 0, 9), e, OP.not_equal)
+        lts(L("B"), L("TG"), clo, OP.add, 1023.0, OP.min)
+        lts(m, L("MG"), clo, OP.add, -900.5, OP.add)
+        lts(L("TB"), L("B"), clo, OP.subtract, 0.125, OP.subtract)
+        lts(R("RB", 1, None, 2), R("SELA"), L("TB"), OP.mult)
+        lts(L("q"), m, L("B"), OP.is_ge, 4096.0, OP.mult)
         lts(L("nlo"), clo, 1.0, OP.add, L("B"), OP.max)
-        lts(L("ea"), m, L("B"), OP.is_lt, L("e2"), OP.mult)
-        lts(L("el", 3), R("IO9", 0, 3), e, OP.is_equal)
-        lts(L("q"), L("ea"), -4096.0, OP.mult, 4096.0, OP.add)
-        ltt(L("t1", 9), R(ST, 0, 9), L("nel"), OP.mult)
-        lts(UN, m, L("q"), OP.add, U, OP.min)
-        L("t2", 9)
-        lts(L("t2", a=0, b=3), L("el"), float(rnd + 2), OP.mult)
-        ltt(L("mbu"), L("B"), UN, OP.min)
-        lts(L("bk0"), L("nlo"), UN, OP.is_ge, L("g0"), OP.mult)
-        lts(L("adv"), m, L("mbu"), OP.is_lt, L("ne2"), OP.mult)
+        lts(L("mk"), m, L("q"), OP.add)
         lts(L("t2", a=6, b=9), L("el"), L("B"), OP.mult)
-        lts(L("nadv"), L("adv"), -1.0, OP.mult, 1.0, OP.add)
-        lts(L("va"), clo, L("adv"), OP.mult)
-        ltt(L("back"), L("bk0"), L("nadv"), OP.mult)
-        ltt(L("stay"), L("nadv"), L("back"), OP.subtract)
+        lts(UN, L("mk"), L("n2"), OP.add, U, OP.min)
+        lts(L("adv"), L("mk"), U, OP.is_lt, L("ne2"), OP.mult)
+        lts(L("bk0"), L("nlo"), UN, OP.is_ge, L("g0"), OP.mult)
+        lts(L("i1"), L("adv"), L("da"), OP.mult, L("idx"), OP.add)
+        lts(L("back"), L("bk0"), L("adv"), OP.is_gt)
+        lts(L("va"), L("adv"), clo, OP.mult)
+        lts(L("idx"), L("back"), L("db"), OP.mult, L("i1"), OP.add)
         lts(eN, e, L("adv"), OP.add, L("back"), OP.subtract)
-        lts(L("val"), L("nlo"), L("stay"), OP.mult, L("va"), OP.add)
-        lts(L("ep", 3), R("IO9", 9, 12), eN, OP.is_equal)
-        lts(L("t2", a=3, b=6), L("el"), L("val"), OP.mult)
-        lts(L("e811"), eN, 811.0, OP.mult, -0.25, OP.add)
-        ltt(L("t3", 9), L("t1"), L("t2"), OP.add)
-        lts(L("en", 3), R("IO9", 0, 3), eN, OP.is_equal)
-        ltt(L("w7", 3), L("t3", a=0, b=3), L("ep"), OP.mult)
-        lo1, hi1 = L("t3", a=3, b=6), L("t3", a=6, b=9)
-        lts(L("w1", 3), lo1, 1.0, OP.add)
-        lev.append((red, (L("idx"), L("w7"), OP.add)))
-        ltt(L("ch"), L("adv"), L("back"), OP.add)
-        lts(R("SLIST"), R("SBASE"), L("idx"), OP.add, 256.0, OP.mult)
         lts(R("ULIST", 0, 1), I16C, L("idx"), OP.add, 16.0, OP.mult)
-        ltt(L("w2", 3), L("w1"), hi1, OP.max)
-        lts(L("enc", 3), L("en"), L("ch"), OP.mult)
-        lts(L("w3", 3), L("w2"), L("back"), OP.mult)
-        lev.append((cp, (R(SN, 0, 9), L("t3"))))
-        ltt(L("w4", 3), L("w3"), lo1, OP.subtract)
-        ltt(L("w5", 3), L("w4"), L("enc"), OP.mult)
-        ltt(R(SN, 3, 6), lo1, L("w5"), OP.add)
-        ltt(L("w6", 3), L("en"), R(SN, 3, 6), OP.mult)
-        lev.append((red, (clo, L("w6"), OP.add)))
+        lts(R("SLIST"), R("SBASE"), L("idx"), OP.add, 256.0, OP.mult)
+        lts(L("stay"), L("adv"), L("back"), OP.add, 0.0, OP.is_equal)
+        lts(L("e811"), eN, 811.0, OP.mult, -0.25, OP.add)
+        lts(L("x"), L("nlo"), L("stay"), OP.mult)
+        lts(L("x3", 3), L("dvm"), L("back"), OP.mult)
+        lts(clo, L("back"), L("wprev"), OP.mult, L("x"), OP.add)
+        ltt(L("val"), L("x"), L("va"), OP.add)
         lts(R("RC", 0, 1), clo, 0.125, OP.mult)
+        lts(L("t2", a=3, b=6), L("el"), L("val"), OP.mult)
         lts(L("x1"), R("RC", 0, 1), AM, OP.mult)
+        ltt(L("t1", a=3, b=6), L("t1", a=3, b=6), L("x3"), OP.add)
         lts(L("lod"), clo, NB6, OP.mult, L("x1"), OP.add)
-        pump(14)
+        ltt(R(SN, 0, 9), L("t1"), L("t2"), OP.add)
+        pump(PUMP)
         cp(R("PXS", 0, 128), R("PX", 0, 128))
-        PD0, PD1 = R("PD", 0, 16), R("PD", 16, 32)
+        pump(2)
+        PD = [R("PD", 16 * k, 16 * k + 16) for k in range(4)]
+        for k in (1, 0):
+            tt(PD[k], IND(R("PXS"), R("LAB", 2, 3)), R("PLS", 16 * k, 16 * k + 16), OP.subtract)
         pump(1)
-        tt(PD0, IND(R("PXS"), R("LAB", 0, 1)), R("PLS"), OP.add)
+        for k in (1, 0):
+            tt(PD[2 + k], IND(R("PXS"), R("LAB", 0, 1)), PD[k], OP.subtract)
         pump(1)
-        tt(PD1, IND(R("PXS"), R("LAB", 2, 3)), PD0, OP.subtract)
-        pump(1)
-        ts(R("LN"), PD1, -1.0, OP.mult, 4095.0, OP.min)
-        ts(R("NI", 0, 16), PD1, -1.0, OP.mult)
+        cp(R("LP"), PD[3])
+        ts(R("LN"), PD[2], 4095.0, OP.min)
+        mm(R("PC", 0, 32), R("ONEF"), R("RB"), True, False, inc=True)
         act(R("D"), IND(R("C"), R("LN")))
-        pump(1)
-        ts(R("NI", 16, 32), R("NI", 0, 16), 4096 + 255, OP.bitwise_and)
-        pump(1)
-        ts(R("LP"), R("NI", 16, 32), 256.0, OP.min)
         pump(1)
         cp(R("E"), IND(R("FP"), R("LP")))
         for h in (0, 1):
@@ -632,7 +657,7 @@ def rank_program(g, core, T, topo):
         tt(R("OH2"), IND(R("KQ", 0, 48), R("L9", 0, 9)), R("IOT2"), OP.is_equal)
         mm(R("PI", 72, 144), ONES(128), R("OH2", 0, 72), False, False)
         mm(R("PI", 0, 144), R("TRI2"), R("OH2"), False, True)
-        ts(R("E2"), R("PX", 0, 256), M1, OP.add, M1, OP.subtract)
+        pump(2)
         run("v", V.tensor_tensor_scan, [R("S2")], [R("D0"), R("PI", 0, 144)], 0.0, OP.add, OP.max)
         pump(1)
         tt(R("LT2"), IND(R("S2"), R("L16")), R("DEL"), OP.mult)
@@ -642,6 +667,8 @@ def rank_program(g, core, T, topo):
         ts(R("DOFF"), R("PU", 0, 16), 256.0, OP.add)
         pump(1)
         for buf, src, win, rs, ls in (("SEND", "D", "WS", "rn", "ln"), ("SENDC", "E2", "WC", "rc", "lc")):
+            if src == "E2":
+                ts(R("E2"), R("PX", 0, 256), M1, OP.add, M1, OP.subtract)
             scat(R(buf), R("DOFF"), R(src))
             act(R(win, land + 32 * rank, land + 32 * rank + 32), R(buf, 32 * rank, 32 * rank + 32))
             before("p", R(buf)[0], [])

from concourse.bass import DstId, RemoteDMATransfer
from concourse.mybir import AluOpType, AxisListType, ActivationFunctionType
import comms_topo

N, RO, J = 8, 8, 16
HACT = 7
PUMP = 0
MACT = ((1, 4), (4, 4), (2, 2))
WT = [1, 3, 7, 13, 21, 35, 49, 67, 85, 107, 129, 155, 181, 211, 241, 253]
KA = [17, 101, 263, 389, 547, 701, 859, 1021, 1171, 1319, 1487, 1637, 1801, 1949, 2111, 2269]
M1, M8 = 1.5 * 2 ** 23, 1.5 * 2 ** 26
EPS = 2.0 ** -10
BF, F32, I32, U16 = "bfloat16", "float32", "int32", "uint16"
_B = {
    "OPR": (8192, BF), "CR": (4096, BF), "C": (4096, BF), "WS": (2560, BF), "WC": (2560, BF), "SREP": (512, BF), "FP": (272, BF),
    "MA": (3840, BF), "MB": (1792, BF), "OH": (2048, BF), "A": (4096, BF), "H0": (2048, BF), "H1": (2048, BF), "OG": (1024, BF),
    "D1": (256, BF), "DB": (256, BF), "DC": (256, BF), "OK": (256, BF), "F": (256, BF), "KEP": (256, BF), "ZR": (256, BF), "BR": (256, BF),
    "MK": (256, BF), "TOTB": (256, BF), "D": (256, BF), "E": (256, BF), "E2": (256, BF), "OH2": (144, BF), "LT2": (256, BF),
    "SEND": (512, BF), "SENDC": (512, BF), "SC": (256, BF), "L1": (128, BF), "L2": (128, BF), "L3": (128, BF), "LQ": (128, BF),
    "YL": (768, BF), "YC": (768, BF),
    "ONES": (256, BF), "Z256": (256, BF), "C32": (128, BF), "C24": (128, BF), "IDB": (128, BF), "NID": (128, BF), "TB1": (256, BF), "TB2": (256, BF),
    "BLK": (128, BF), "W16": (16, BF), "W4": (16, BF), "WE4": (16, BF), "WF": (128, BF), "CST": (512, BF), "LBW": (144, BF), "JS": (144, BF),
    "TRIM": (128, BF), "TRI2": (128, BF), "I8R": (256, BF), "LE0": (256, BF), "LE1": (256, BF), "LI": (128, BF),
    "BD15": (64, BF), "ST15": (256, BF), "SR15": (128, BF), "BD7": (64, BF), "ST7": (256, BF), "SR7": (128, BF),
    "OC2": (144, BF), "IOT2": (144, BF), "D0": (144, BF), "IO256": (256, BF), "W81": (8, BF), "DEL": (256, BF), "RA": (8, BF), "IK": (128, BF),
    "ROWI": (128, BF), "J16": (16, F32),
    "IDF": (128, F32), "ONEF": (128, F32), "G8F": (128, F32), "TREE": (128, F32), "I16": (16, F32), "I8": (8, F32), "VEC": (80, F32),
    "KT": (256, F32), "KU": (256, F32), "Y0": (256, F32), "ZO": (256, F32), "SBASE": (32, F32), "IO9": (12, F32), "SELA": (16, F32), "RB": (32, F32),
    "COL": (32, F32), "ST0": (11, F32), "ST1": (11, F32), "LW": (128, F32), "XB0": (32, F32), "XB1": (32, F32),
    "MX": (4, F32), "MJ": (16, F32), "PXS": (136, F32), "PLS": (32, F32), "PD": (64, F32), "KQ": (64, F32), "S2": (144, F32), "YF": (768, F32),
    "F0": (256, I32), "UT": (160, I32), "UI": (48, I32), "HI": (256, I32), "HM": (256, I32), "NI": (32, I32), "RC": (2, I32), "MI": (1, I32),
    "OFFC": (256, U16), "SLIST": (32, U16), "ULIST": (2, U16), "LN": (16, U16), "LP": (16, U16), "DOFF": (16, U16), "REPL": (16, U16),
    "LAB": (4, U16), "L9": (10, U16), "L16": (16, U16), "OLIST": (48, U16),
}
_PS = ["PT0", "PT1", "PU", "PC", "PI", "PR", "PX", "PL"]
_JOIN = {"ORD": ("LE0", "LE1", "LI"), "KM": ("ST15", "ST7", "SR15", "SR7", "BD15", "BD7"), "WTS": ("W16", "W4", "WE4", "W81", "RA")}
_AT = {k: (k, 0, n) for k, (n, d) in _B.items()}
for _k, _names in _JOIN.items():
    _B[_k] = (0, BF)
    for _x in _names:
        _AT[_x] = (_k, _B[_k][0], _B[_x][0])
        _B[_k] = (_B[_k][0] + _B.pop(_x)[0], BF)
_AT.update({k: (k, 0, 512) for k in _PS})
SCRATCH = {k: ("sbuf", [128, n], d) for k, (n, d) in _B.items()}
SCRATCH.update({k: ("psum", [128, 512], F32) for k in _PS})
SEMAPHORES = ["sv", "st", "sa", "sp", "dopr", "ds0", "df0", "dout", "rt", "lt", "rn", "ln", "rc", "lc"]
OP, ACT, AX = AluOpType, ActivationFunctionType, AxisListType.X


def rank_program(g, core, T, topo):
    rank = T.rank_of(core)
    if rank is None:
        return
    Q = {"v": g.vector, "t": g.tensor, "a": g.scalar, "p": g, "y": g.sync}
    SEM = {"v": "sv", "t": "st", "a": "sa", "p": "sp"}
    cnt = {"v": 0, "t": 0, "a": 0, "p": 0}
    seen, log = {}, {}

    def wait(e, sem, val):
        if seen.get((e, sem), 0) < val:
            Q[e].wait_ge(T.sem[sem], val)
            seen[(e, sem)] = val

    def before(e, reads, writes):
        need, own = {}, SEM.get(e)
        for names, wr in ((reads, False), (writes, True)):
            for name, m in names:
                for m2, w2, s, v in log.get(name, ()):
                    bank = name in _PS and s != own
                    if (bank or (m & m2 and (wr or w2))) and not (e == "t" and s == own):
                        need[s] = max(need.get(s, 0), v)
        for s, v in need.items():
            wait(e, s, v)

    def after(sem, val, reads, writes):
        for name, m in writes:
            log[name] = [x for x in log.get(name, ()) if x[0] & ~m] + [(m, True, sem, val)]
        for name, m in reads:
            log[name] = [x for x in log.get(name, ()) if x[1] or x[2] != sem or x[0] & ~m] + [(m, False, sem, val)]

    def R(name, a=None, b=None, s=None, p=None):
        name, at, n = _AT[name]
        cols = range(at, at + n)[a:b:s]
        m = ((1 << len(cols)) - 1) << cols[0] if s is None else sum(1 << c for c in cols)
        a, b = cols[0], cols[-1] + 1
        return ([(name, m)], T[name][:, a:b:s] if p is None else T[name][0:p, a:b:s])

    def IND(w, o):
        return (w[0] + o[0], w[1].indirect(o[1]))

    def run(e, fn, outs, ins, *args, inc=True, **kw):
        reads = [k for x in ins if isinstance(x, tuple) for k in x[0]]
        writes = [k for x in outs for k in x[0]]
        before(e, reads, writes)
        u = [x[1] if isinstance(x, tuple) else x for x in list(outs) + list(ins)]
        ins_ = fn(*u, *args, **kw)
        if inc:
            ins_.then_inc(T.sem[SEM[e]], 1)
            cnt[e] += 1
        after(SEM[e], cnt[e] + (0 if inc else 1), reads, writes)

    V = g.vector

    def ts(out, in0, s1, op0, s2=None, op1=None):
        reads = [in0] + [x for x in (s1, s2) if isinstance(x, tuple)]
        u1 = s1[1] if isinstance(s1, tuple) else s1
        u2 = s2[1] if isinstance(s2, tuple) else s2
        f = lambda o, i, *rest: (V.tensor_scalar(o, i, u1, u2, op0) if op1 is None else V.tensor_scalar(o, i, u1, u2, op0, op1))
        run("v", f, [out], reads)

    def tt(out, a, b, op):
        run("v", V.tensor_tensor, [out], [a, b], op)

    def cp(out, a):
        run("v", V.tensor_copy, [out], [a])

    def scat(win, offs, src):
        run("v", lambda o, i, x: V.tensor_copy(o, i), [(win[0], win[1].indirect(offs[1]))], [src, offs])

    def fill(out, c):
        run("v", V.memset, [out], [], c)

    def red(out, a, op):
        run("v", V.tensor_reduce, [out], [a], AX, op)

    def mm(out, lhsT, rhs, start, stop, inc=None):
        run("t", g.tensor.matmul, [out], [lhsT, rhs], start, stop, inc=stop if inc is None else inc)

    def act(out, a, func=ACT.Copy, **kw):
        col = [x for x in kw.values() if isinstance(x, tuple)]
        kw = {k: x[1] if isinstance(x, tuple) else x for k, x in kw.items()}
        run("a", lambda o, i, *rest: g.scalar.activation(o, i, func, **kw), [out], [a] + col)

    def lin(out, a, scale, bias=0.0):
        act(out, a, ACT.Identity, scale=scale, bias=bias)

    def step(out, a, thr):
        act(out, a, ACT.Sigmoid, scale=-4096.0, bias=4096.0 * thr)

    def sel(out, a, pat, op, base, cm, other=0.0):
        run("p", g.affine_select, [out], [a], pat, op, other, base, cm)

    def iota(out, pat, base, cm):
        run("p", g.iota, [out], [], pat, base, cm, allow_small_or_imprecise_dtypes=True)

    def spread(name, n, full):
        while n < full:
            act(R(name, n, 2 * n), R(name, 0, n))
            n *= 2

    ICOL, WCOL, RCOL, WY, W81C, CF, AM, NB6, PCOL, I16C, PC1 = [R("COL", i, i + 1) for i in range(11)]
    TMP = [R("COL", i, i + 1) for i in range(11, 32)]

    g.sync.dma_start(T.WS[:, 0:256], T.s0[:, :]).then_inc(T.sem.ds0, 16)
    after("ds0", 16, [], R("WS", 0, 256)[0])
    for q in range(4):
        g.sync.dma_start(T.OPR[32 * q:32 * q + 32, :], T.opr[32 * q:32 * q + 32, :]).then_inc(T.sem.dopr, 16)
    after("dopr", 64, [], R("OPR")[0])
    fill(R("ONES"), 1.0)
    fill(R("F0"), 0)
    wait("a", "sv", cnt["v"])
    g.scalar.dma_start(T.F0[0:128:16, :], T.f0[:, :]).then_inc(T.sem.df0, 16)
    g.scalar.dma_start(T.F0[1:128:16, :], T.f0[:, :]).then_inc(T.sem.df0, 16)
    after("df0", 32, [], R("F0")[0])

    ONES = lambda n: R("ONES", 0, n)
    IO16, WROW = R("VEC", 0, 16), R("VEC", 16, 32)
    sel(R("IDB"), ONES(128), [[-1, 128]], OP.is_equal, 0, 1)
    sel(R("TB1", 0, 128), ONES(128), [[-16, 8], [0, 16]], OP.is_ge, 0, 1)
    sel(R("BLK"), R("TB1", 0, 128), [[16, 8], [0, 16]], OP.is_ge, 15, -1)
    iota(IO16, [[1, 16]], 0, 0)
    iota(R("SBASE"), [[0, 2], [16, 16]], 0, 0)
    iota(PCOL, [[0, 1]], 0, 1)
    iota(R("PD", 0, 9), [[16, 9]], 0, 0)
    iota(R("IO9", 0, 9), [[0, 3], [1, 3]], 0, 0)
    iota(R("IO9", 9, 12), [[1, 3]], 1, 0)
    BLK8 = R("BLK", 0, None, 16)
    fill(R("Z256"), 0.0)
    fill(R("LBW"), 0.0)
    for i in range(16):
        fill(R("VEC", 16 + i, 17 + i), float(WT[i]))
    TRE = lambda a, b: R("TREE", a, b)
    tt(TRE(0, 64), R("IDB", 0, 64), R("IDB", 64, 128), OP.add)
    fill(R("UT", 16, 32), 0)
    tt(TRE(64, 96), TRE(0, 32), TRE(32, 64), OP.add)
    fill(R("WS", 256, 512), 0.0)
    tt(R("I16"), TRE(64, 80), TRE(80, 96), OP.add)
    ROW = lambda i: R("I16", i, i + 1)
    LWn = {}

    def L(name, n=1, a=0, b=None):
        if name not in LWn:
            LWn[name] = (sum(x[1] for x in LWn.values()), n)
        at, n = LWn[name]
        return R("LW", at + a, at + (n if b is None else b))
    fill(L("clo"), 0.0)
    tt(TRE(0, 16), R("I16"), WROW, OP.mult)
    tt(TRE(16, 32), R("I16"), IO16, OP.mult)
    red(WCOL, TRE(0, 16), OP.add)
    red(ICOL, TRE(16, 32), OP.add)
    ts(R("LBW", 15, 128, 16), BLK8, WCOL, OP.mult)
    ts(R("SBASE"), R("SBASE"), ICOL, OP.add)
    cp(R("ULIST", 0, 1), ICOL)
    cp(R("SLIST"), R("SBASE"))
    ts(R("REPL"), R("Z256", 0, 16), ICOL, OP.add)
    tt(R("I8"), R("I16", 0, 8), R("I16", 8, 16), OP.add)
    fill(L("lod"), 0.0)
    fill(L("e811"), -0.25)
    for j in range(J):
        fill(R("KT", 16 * j, 16 * j + 16), float(KA[j]))
    step(R("ST15"), ONES(256), 2.0)
    lin(R("ST7"), ONES(256), 1.0)
    lin(R("ONEF"), ONES(128), 1.0)
    act(R("I8R", 0, 8), R("I8"))
    spread("I8R", 8, 256)
    for k, p in ((7, 56), (15, 120)):
        for nm, w, n in (("BD", [[-k, 8], [0, 8]], 64), ("ST", [[0, 32], [-k, 8]], 256), ("SR", [[-k, 8], [0, 16]], 128)):
            far = -4096.0 if nm == "BD" else 0.0
            sel(R("TB2", 0, n, p=p), R("Z256" if far else "ONES", 0, n, p=p), w, OP.is_ge, 0, 1, far)
            sel(R(nm + str(k), p=p), R("TB2", 0, n, p=p), [[-a, b] for a, b in w], OP.is_ge, k - 1, -1, far)
    sel(R("TB2", 0, 16), ONES(16), [[-8, 16]], OP.is_ge, 0, 1)
    sel(R("J16"), R("TB2", 0, 16), [[8, 16]], OP.is_ge, 7, -1)
    sel(R("TB2", 128, 256), ONES(128), [[1, 128]], OP.is_gt, 0, -1)
    sel(R("TRIM"), R("TB2", 128, 256), [[1, 128]], OP.not_equal, 0, -1, -256.0)
    for t in (0, 1):
        sel(R("LE%d" % t), R("I8R"), [[8, 2], [16, 16], [2, 8]], OP.is_gt, -8 * t, -2)
    sel(R("LI"), R("I8R", 0, 128), [[8, 16], [1, 8]], OP.is_ge, 0, -1)
    iota(R("IO256"), [[1, 256]], 0, 0)
    iota(R("TB1", 0, 128), [[0, 8], [1, 16]], -2, 0)
    sel(R("TB1", 128, 256), R("TB1", 0, 128), [[-16, 8], [0, 16]], OP.is_ge, 0, 1, -9.0)
    sel(R("ROWI"), R("TB1", 128, 256), [[16, 8], [0, 16]], OP.is_ge, 15, -1, -9.0)
    sel(R("TRI2"), R("TB2", 128, 256), [[1, 128]], OP.not_equal, 0, -1, 1024.0)
    iota(R("OC2"), [[0, 16], [1, 9]], 0, 0)
    sel(R("D0"), R("Z256", 0, 144), [[0, 16], [1, 9]], OP.not_equal, 0, 0, -4096.0)

    def constants_1():
        runs = ((0, 1, 8.0), (1, 5, 1.0), (5, 16, 0.0), (16, 17, 127.0), (17, 18, 7.0), (18, 31, 0.0), (31, 32, 1.0))
        for a, b, v in runs:
            fill(R("VEC", 32 + a, 32 + b), v)
        cp(R("RC", 0, 1), WCOL)
        tt(TRE(0, 16), R("I16"), R("VEC", 32, 48), OP.mult)
        ts(R("RC", 1, 2), R("RC", 0, 1), 7, OP.bitwise_and)
        tt(TRE(16, 32), R("I16"), R("VEC", 48, 64), OP.mult)
        red(W81C, TRE(0, 16), OP.add)
        cp(RCOL, R("RC", 1, 2))
        red(CF, TRE(16, 32), OP.add)
        ts(TMP[0], ROW(5), 8.0, OP.mult, ROW(6), OP.add)
        ts(TMP[1], R("IDB", 0, 1), 896.0, OP.mult)
        ts(R("W16", 0, 8), BLK8, 0.25, OP.mult)
        tt(WY, TMP[0], W81C, OP.add)
        ts(TMP[2], R("IDB", 1, 2), 4.125, OP.mult, TMP[1], OP.add)
        ts(R("W16", 8, 16), BLK8, RCOL, OP.mult)
        ts(R("WF", 0, 8), BLK8, WY, OP.mult)
        lin(R("NID"), R("IDB"), -1.0)
        lin(R("CST", 0, 256), ONES(256), TMP[2])
        lin(R("CST", 256, 512), ONES(256), -3.5 / 128)
        spread("WF", 8, 128)
        lin(R("SC"), ONES(256), CF)
        act(R("WC", 256, 512), R("SC"))
        ts(R("HI"), R("F0"), 3, OP.arith_shift_right)
        ts(R("HM"), R("F0"), 7, OP.bitwise_and)
        ts(R("KEP"), R("HI"), ROW(0), OP.mult, ROW(15), OP.add)
        ts(R("ZR"), R("HM"), ROW(1), OP.mult)
        ts(TMP[3], R("IDB", 56, 57), 896.0, OP.mult)
        tt(R("WC", 0, 256), R("KEP"), R("ZR"), OP.add)
        ts(TMP[4], R("IDB", 57, 58), 4.25, OP.mult, TMP[3], OP.add)
        ts(TMP[5], R("IDB", 120, 121), -0.125, OP.mult)
        lin(R("L1"), ONES(128), TMP[4])
        lin(R("L2"), ONES(128), TMP[5])
        lin(R("C32"), ONES(128), 32.5)
        lin(R("C24"), ONES(128), 24.0)
        act(R("IDF"), R("IDB"))
        for xb in ("XB0", "XB1"):
            fill(R(xb, 4 * rank, 4 * rank + 4), 0.0)
        fill(L("idx"), 0.0)
        ts(PC1, PCOL, 128.0, OP.add)
        fill(R("JS"), 0.0)
        fill(R("RB"), 0.0)
        fill(R("PXS", 128, 136), 0.0)
        fill(R("ST0", 0, 3), 1.0)
        fill(R("ST0", 3, 10), 0.0)
        fill(R("ST0", 10, 11), 1023.0)
        ts(R("JS", 15, 128, 16), R("I8"), 256.0, OP.mult)

    def constants_2():
        cp(R("LN"), IO16)
        ts(R("SBASE"), R("SBASE"), 1.0 / 256, OP.mult)
        cp(R("G8F"), IND(R("I8"), R("LN", 0, 8)))
        ts(I16C, ICOL, 1.0 / 16, OP.mult)
        ts(AM, ROW(6), 8.0, OP.mult, ROW(5), OP.subtract)
        ts(NB6, ROW(6), -1.0, OP.mult)

    def constants_3():
        ts(TMP[6], ROW(0), 128.0, OP.mult, ROW(15), OP.add)
        tt(TMP[7], ROW(5), ROW(6), OP.add)
        ts(TMP[9], ROW(15), 4.0, OP.mult)
        ts(R("FP", 256, 272), ONES(16), TMP[6], OP.mult)
        ts(TMP[8], TMP[7], -1.0, OP.mult, 1.0, OP.add)
        ts(TMP[10], WY, EPS, OP.mult, TMP[9], OP.add)
        ts(R("E", 128, 256), R("BLK"), ROW(15), OP.mult, -0.375, OP.mult)
        ts(R("E", 0, 128), R("IDB"), TMP[8], OP.mult)
        ts(R("WE4", 1, None, 2), BLK8, TMP[10], OP.mult)
        ts(R("W4", 0, None, 2), BLK8, RCOL, OP.mult)
        tt(R("IK"), R("E", 0, 128), R("E", 128, 256), OP.add)
        ts(R("W4", 1, None, 2), BLK8, EPS / 4, OP.mult)
        ts(R("WE4", 0, None, 2), BLK8, ROW(15), OP.mult, -3.5, OP.mult)
        for h in (0, 1):
            ts(R("SELA", 8 * h, 8 * h + 8), BLK8, ROW(0), OP.mult, -EPS, OP.mult)
        cp(R("RA"), BLK8)
        ts(R("W81"), BLK8, W81C, OP.mult)
        cp(R("DEL"), IND(R("I16"), R("REPL")))

    def constants_5():
        lin(R("IOT2"), R("OC2"), 1.0, -3.5)
        lin(R("IOT2", 8, None, 9), ONES(16), 8.0)
        lin(R("OC2"), R("OC2"), 0.25, -10.0)
        for buf in ("SEND", "SENDC"):
            act(R(buf, 256, 512), R("Z256"))

    def constants_4():
        ts(R("PD", 0, 9), R("PD", 0, 9), ICOL, OP.add)
        ts(TMP[11], PCOL, ICOL, OP.subtract, 0.5, OP.mult)
        ts(TMP[12], ICOL, 8.0, OP.is_ge, 56.0, OP.mult)
        ts(R("NI", 0, 9), R("PD", 0, 9), 1.0 / 9, OP.mult, -4.0 / 9, OP.add)
        ts(TMP[13], TMP[11], ICOL, OP.add, TMP[12], OP.add)
        ts(TMP[14], TMP[11], -1.0, OP.mult, 129.0, OP.add)
        ts(R("PD", 16, 25), R("NI", 0, 9), -9.0, OP.mult, -8.0, OP.add)
        ts(TMP[15], ROW(8), -56.0, OP.mult, TMP[13], OP.add)
        cp(R("LAB", 0, 1), TMP[13])
        tt(R("PD", 0, 9), R("PD", 0, 9), R("PD", 16, 25), OP.add)
        ts(TMP[16], TMP[14], ROW(0), OP.mult, TMP[15], OP.add)
        ts(R("PD", 16, 25), R("NI", 0, 9), 17.0, OP.add)
        ts(R("PD", 0, 9), R("PD", 0, 9), 0.0, OP.is_equal)
        ts(R("LAB", 2, 3), TMP[16], -1.0, OP.add)
        ts(R("L16"), IO16, 9.0, OP.mult, 8.0, OP.add)
        tt(R("PD", 0, 9), R("PD", 0, 9), R("PD", 16, 25), OP.mult)
        tt(R("PD", 16, 25), R("PD", 0, 9), R("NI", 0, 9), OP.add)
        cp(R("L9", 0, 9), R("PD", 16, 25))

    dests = [c for c in T.cores if c != core]
    dests.sort(key=lambda c: len(topo.engines(core, c)))
    used, plan = set(), []
    for c in dests:
        free = [x for x in topo.engines(core, c) if x not in used][:2]
        used.update(free)
        rid, pid, _s = topo.addr(c)
        plan.append((c, DstId(rid=rid, pnc=pid), sum(1 << x for x in free), len(free)))
    per = sum(x[3] for x in plan)

    def to_all(src, dst, rsem, lsem):
        g.remote_dma_fused([RemoteDMATransfer(dst_ids=[d], dma_engine_mask=m, remote_sem=T.sem[rsem], src=src(c), dst=dst)
                            for c, d, m, _n in plan], local_sem=T.sem[lsem])

    def half(name, k, K, h):
        return R(name, 128 * K * h + k, 128 * K * (h + 1), K)

    def cols(name, h, p=None):
        return R(name, 128 * h, 128 * h + 128, p=p)

    lev = []

    def pump(k):
        for f, x in lev[:k]:
            f(*x)
        del lev[:k]

    blocks = [(512 * c, 512) for c in range(7)] + [(3584, 256), (3840, 256)]
    PA = lambda h: R("PT%d" % h, 256, 384)
    PB = lambda h: R(("PI", "PR")[h], 0, 128)

    for rnd in range(RO):
        ST, SN = ("ST0", "ST1") if rnd % 2 == 0 else ("ST1", "ST0")
        XB = "XB%d" % (rnd % 2)
        new = rnd + 1 if rnd else 0
        land = 256 * (rnd + 2)
        if rnd:
            wait("t", "rn", per * rnd)
            wait("a", "rn", per * rnd)
        for b in range(16):
            mm(R("PU", 0, 16), R("LBW", 15 - b, 143 - b), R("WS", 256 * new + b, 256 * new + 256, 16), b == 0, b == 15)
        act(R("SREP"), IND(R("WS", 0, land), R("SLIST")))
        um, sq, s4 = [R("UI", 16 * k, 16 * k + 16) for k in range(3)]
        cp(R("UT", 16 * new, 16 * new + 16), R("PU", 0, 16))
        ts(um, IND(R("UT", 0, 16 * (rnd + 2)), R("ULIST", 0, 1)), 4095, OP.bitwise_and)
        tt(sq, um, um, OP.mult)
        ku = lambda a, b: tt(R("KU", a, b), IND(um, R("REPL", a // 16, b // 16)), R("KT", a, b), OP.mult)
        hi = lambda a, b: tt(R("HI", a, b), IND(s4, R("REPL", a // 16, b // 16)), R("KU", a, b), OP.add)
        hm = lambda a, b: ts(R("HM", a, b), R("HI", a, b), 8191, OP.bitwise_and)
        of = lambda a, b: cp(R("OFFC", a, b), R("HM", a, b))
        ku(0, 64)
        ts(s4, sq, 1.0 / 16, OP.mult, L("e811"), OP.add)
        for f, a, b in ((ku, 64, 160), (hi, 0, 64), (hi, 64, 160), (hm, 0, 64), (ku, 160, 256), (of, 0, 64), (hm, 64, 160), (hi, 160, 256),
                        (of, 64, 160), (hm, 160, 256)):
            f(a, b)
        if rnd == 0:
            of(160, 256)
            for f in (constants_1, constants_2, constants_4, constants_3):
                f()
        for c, bank in ((0, "PX"), (1, "PR")):
            mm(R(bank), R("IDB"), R("SREP"), True, False, inc=True)
            act(R("OG", 512 * c, 512 * c + 512), IND(R("OPR"), R("OFFC", 32 * c, 32 * c + 32)))
        for s in (0, 1):
            mm(R("PT%d" % s, 0, 256), ONES(128), R("CST", 256 * s, 256 * s + 256), True, False, inc=True)
        for c, bank in ((0, "PX"), (1, "PR")):
            mm(R(bank), R("NID"), R("OG", 512 * c, 512 * c + 512), False, True)
        for c in (0, 2, 1, 3, 4, 5, 6, 7, 8):
            a, n = blocks[c]
            cr = R("CR", a, a + n)
            if c < 2:
                cr = R(("PX", "PR")[c])
            else:
                tt(cr, IND(R("OPR"), R("OFFC", a // 16, (a + n) // 16)), R("SREP", 0, n), OP.subtract)
            if c == 2 and rnd:
                of(160, 256)
            act(R("C", a, a + n), cr, ACT.Abs)
            if c == 8:
                if rnd:
                    wait("v", "rc", per * rnd)
                ts(R("FP", 0, 256), IND(R("WC", 0, land), R("SLIST", 0, 16)), L("lod"), OP.add)
                for h in (0, 1):
                    mm(cols("PT0", h), cols("FP", h), R("WF"), False, False, inc=True)
            for s in (1, 0):
                for x in range(a // 128, (a + n) // 128):
                    at = 128 * (x % 2) + 8 * (x // 2)
                    mm(R("PT%d" % s, at, at + 8), R("C", 128 * x, 128 * x + 128), R("W16", 8 * s, 8 * s + 8), False, x == 31, inc=(x + 1) * 128 == a + n)

        def hots(h):
            for o in range(8):
                ts(half("OH", o, 8, h), cols("OK", h), o - 3.5, OP.is_equal)

        def masks(K, M, src, thr, na, h):
            for k in range(K - na, K):
                step(half(M, k, K, h), cols(src, h), thr(k + 1))
            for k in range(K - na):
                ts(half(M, k, K, h), cols(src, h), thr(k + 1), OP.is_lt)

        def count(K, M, h):
            p = 8 * K
            if h == 0:
                mm(R("PC", 0, 64, p=p), R("IDB", 0, p, p=p), R("BD%d" % K, p=p), True, False, inc=True)
            for x in range(16 * h, 16 * h + 16):
                mm(R("PC", 0, 64, p=p), R(M, p * x, p * x + p), R("OH", 64 * x, 64 * x + 64), False, x == 31)

        def digit(K, Lx, mx, stp):
            p = 8 * K
            red(R("MX", mx, mx + 1, p=p), R("PC", 0, 64, p=p), OP.max)
            ts(R(Lx, p=p), R("C32", p=p), R("MX", mx, mx + 1, p=p), OP.is_ge, float(stp), OP.mult)

        def turn(h):
            mm(R("PX", 128 * h, 128 * h + 128), cols("Y0", h), R("IDF"), True, False, inc=True)
            mm(R("PX", 128 * h, 128 * h + 128), cols("F", h), R("IDB"), False, True)
        th1 = lambda k: 128.0 * k + 900.0
        act(R("F"), R("PT0", 0, 256), ACT.Relu, scale=-65536.0, bias=65536.0 * 899.9375)
        for h in (0, 1):
            ts(cols("ZO", h), cols("PT1", h), M8, OP.add, M8, OP.subtract)
        for h in (0, 1):
            tt(cols("OK", h), cols("PT1", h), cols("ZO", h), OP.subtract)
        for h in (0, 1):
            tt(cols("D1", h), cols("PT0", h), cols("F", h), OP.add)
        hots(0)
        masks(7, "MB", "D1", th1, MACT[0][0], 0)
        count(7, "MB", 0)
        hots(1)
        masks(7, "MB", "D1", th1, MACT[0][1], 1)
        act(R("Y0"), R("PT0", 0, 256))
        count(7, "MB", 1)
        for h in (1, 0):
            mm(PA(h), R("NID"), cols("F", h), True, False, inc=True)
        if rnd:
            wait("a", "ln", per * rnd)
        act(R("SEND", 0, 256), R("Z256"))
        clo, e, U, m = L("clo"), R(ST, 9, 10), R(ST, 10, 11), R("MI")
        eN, UN = R(SN, 9, 10), R(SN, 10, 11)
        lts = lambda *x: lev.append((ts, x))
        ltt = lambda *x: lev.append((tt, x))
        L("t2", 9)
        lts(L("nel", 9), R("IO9", 0, 9), e, OP.not_equal)
        lts(L("w1", 3), R(ST, 3, 6), 1.0, OP.add)
        lts(L("el", 3), R("IO9", 0, 3), e, OP.is_equal)
        lts(L("em", 3), R("IO9", 9, 12), e, OP.is_equal)
        ltt(L("W", 3), L("w1"), R(ST, 6, 9), OP.max)
        lts(L("em2", 3), R("IO9", 0, 3), 2.0, OP.add, e, OP.is_equal)
        ltt(L("t1", 9), R(ST, 0, 9), L("nel"), OP.mult)
        ltt(L("w2", 3), L("W"), L("em"), OP.mult)
        ltt(L("dv", 3), L("W"), R(ST, 3, 6), OP.subtract)
        ltt(L("w3", 3), R(ST, 0, 3), L("em2"), OP.mult)
        lev.append((red, (L("wprev"), L("w2"), OP.add)))
        ltt(L("dvm", 3), L("dv"), L("em"), OP.mult)
        lev.append((red, (L("pprev"), L("w3"), OP.add)))
        lts(L("t2", a=0, b=3), L("el"), float(rnd + 2), OP.mult)
        lts(L("n2"), e, 2.0, OP.is_lt, 4096.0, OP.mult)
        lts(L("ne2"), e, 2.0, OP.is_lt)
        lts(L("g0"), e, 0.0, OP.is_gt)
        lts(L("da"), L("idx"), -1.0, OP.mult, float(rnd + 2), OP.add)
        ltt(L("db"), L("pprev"), L("idx"), OP.subtract)
        lts(R("LQ"), R("ROWI"), e, OP.is_equal, 0.25, OP.mult)
        pump(8)
        digit(7, "L1", 0, 128)
        for h in (0, 1):
            mm(PA(h), R("L1", p=58), cols("ST7", h, 58), False, True)
        turn(0)
        turn(1)
        for h in (0, 1):
            tt(cols("DB", h), cols("Y0", h), PA(h), OP.subtract)
        for h in (0, 1):
            masks(15, "MA", "DB", lambda k: 8.0 * k - 0.1875, MACT[1][h], h)
            mm(PB(h), R("NID"), cols("F", h), True, False, inc=True)
            mm(PB(h), R("L1", p=58), cols("ST7", h, 58), False, False, inc=True)
            count(15, "MA", h)
        red(R("MX", 3, 4), R("PX", 0, 256), OP.min)
        if rnd:
            wait("a", "lc", per * rnd)
        else:
            constants_5()
        act(R("SENDC", 0, 256), R("SC"))
        pump(1)
        ts(R("MJ"), R("J16"), R("MX", 3, 4), OP.mult)
        pump(4)
        digit(15, "L2", 1, 8)
        for h in (0, 1):
            mm(PB(h), R("L2", p=121), cols("ST15", h, 121), False, True)
        mm(R("PU", 16, 32), R("G8F"), R("MJ"), True, True)
        for h in (0, 1):
            tt(cols("DC", h), cols("Y0", h), PB(h), OP.subtract)
        for h in (0, 1):
            masks(7, "MB", "DC", lambda k: k - 0.125, MACT[2][h], h)
            count(7, "MB", h)
            if h == 0:
                for t in (0, 1):
                    mm(PB(t), ONES(128), R("C24"), True, False, inc=True)
        if rnd:
            wait("v", "lt", per * rnd)
        red(R(XB, 4 * rank + 1, 4 * rank + 2), R("PU", 16, 32), OP.min)
        pump(7)
        digit(7, "L3", 2, 1)
        for h in (0, 1):
            mm(PA(h), R("L3", p=56), cols("ST7", h, 56), True, True)
        mm(R("PU", 0, 1), R("SR7", p=56), R("L1", 0, 1, p=56), True, False)
        mm(R("PU", 0, 1), R("SR15", p=120), R("L2", 0, 1, p=120), False, False)
        mm(R("PU", 0, 1), R("SR7", p=56), R("L3", 0, 1, p=56), False, True)
        act(R(XB, 4 * rank, 4 * rank + 1), R("PU", 0, 1))
        mine = T[XB][:, 4 * rank:4 * rank + 4]
        before("p", R(XB, 4 * rank, 4 * rank + 4)[0] + R("SREP")[0] + R("FP")[0] + R("UT")[0], [])
        to_all(lambda c: mine, mine, "rt", "lt")
        for h in (0, 1):
            tt(cols("KEP", h), cols("DC", h), PA(h), OP.is_lt)
            mm(R("PL", h, h + 1), cols("KEP", h), ONES(1), True, True)
        for h in (0, 1):
            mm(PB(h), R("TRIM"), cols("KEP", h), False, False, inc=True)
        for t in (0, 1):
            ts(cols("TOTB", t), R("Z256", 0, 128), R("PL", t, t + 1), OP.add)
        for h in (0, 1):
            for t in (0, 1):
                mm(PB(h), cols("TOTB", t), cols("LE%d" % t, h), False, t == 1)
        for t in (0, 1):
            mm(R("PL", 2, 3), R("LI"), R("TOTB", 128 * t, 128 * t + 1), t == 0, t == 1)
        ts(cols("ZR", 0), PB(0), -7.5, OP.add)
        lin(cols("ZR", 1), PB(1), 1.0, -7.5)
        ts(R("MK"), R("IO256"), R("PL", 2, 3), OP.is_ge)
        for k in range(16):
            mm(R("PU", 0, 16), R("JS", 15 - k, 143 - k), R("MK", k, 256, 16), k == 0, k == 15)
        tt(cols("BR", 0), PB(0), cols("ZR", 0), OP.subtract)
        mm(R("PX", 0, 128), R("IDB"), R("Z256", 0, 128), True, False, inc=True)

        def steps(h, s):
            for c in range(8):
                out, thr = half("H%d" % s, c, 8, h), 2816.0 + 16 * (8 * s + c) + 8
                if s:
                    step(out, cols("ZR", h), thr)
                else:
                    ts(out, cols("ZR", h), thr, OP.is_lt)

        def places(h):
            for c in range(16):
                ts(half("A", c, 16, h), cols("BR", h), float(c), OP.is_equal, (PCOL, PC1)[h], OP.mult)

        def sums(h, s):
            for x in range(16 * h, 16 * h + 16):
                mm(R("PX", 64 * s, 64 * s + 64), R("A", 128 * x, 128 * x + 128), R("H%d" % s, 64 * x, 64 * x + 64), False, (x, s) == (31, 0))
        steps(0, 1)
        steps(1, 1)
        steps(0, 0)
        tt(cols("BR", 1), PB(1), cols("ZR", 1), OP.subtract)
        places(0)
        sums(0, 0)
        sums(0, 1)
        places(1)
        sums(1, 1)
        steps(1, 0)
        sums(1, 0)
        mm(R("PI", 0, 144), ONES(128), R("OC2"), True, False, inc=True)
        pump(99)
        cp(R("PLS", 0, 16), R("PU", 0, 16))
        ts(R("PLS", 16, 32), R("PU", 0, 16), 4096.0, OP.is_ge, 256.0, OP.mult)
        wait("v", "rt", per * (rnd + 1))
        red(L("TG"), R(XB, 0, None, 4), OP.min)
        red(L("MG"), R(XB, 1, None, 4), OP.min)
        lts(L("B"), L("TG"), clo, OP.add, 1023.0, OP.min)
        lts(m, L("MG"), clo, OP.add, -900.5, OP.add)
        lts(L("TB"), L("B"), clo, OP.subtract, 0.125, OP.subtract)
        lts(R("RB", 1, None, 2), R("SELA"), L("TB"), OP.mult)
        lts(L("q"), m, L("B"), OP.is_ge, 4096.0, OP.mult)
        lts(L("nlo"), clo, 1.0, OP.add, L("B"), OP.max)
        lts(L("mk"), m, L("q"), OP.add)
        lts(L("t2", a=6, b=9), L("el"), L("B"), OP.mult)
        lts(UN, L("mk"), L("n2"), OP.add, U, OP.min)
        lts(L("adv"), L("mk"), U, OP.is_lt, L("ne2"), OP.mult)
        lts(L("bk0"), L("nlo"), UN, OP.is_ge, L("g0"), OP.mult)
        lts(L("i1"), L("adv"), L("da"), OP.mult, L("idx"), OP.add)
        lts(L("back"), L("bk0"), L("adv"), OP.is_gt)
        lts(L("va"), L("adv"), clo, OP.mult)
        lts(L("idx"), L("back"), L("db"), OP.mult, L("i1"), OP.add)
        lts(eN, e, L("adv"), OP.add, L("back"), OP.subtract)
        lts(R("ULIST", 0, 1), I16C, L("idx"), OP.add, 16.0, OP.mult)
        lts(R("SLIST"), R("SBASE"), L("idx"), OP.add, 256.0, OP.mult)
        lts(L("stay"), L("adv"), L("back"), OP.add, 0.0, OP.is_equal)
        lts(L("e811"), eN, 811.0, OP.mult, -0.25, OP.add)
        lts(L("x"), L("nlo"), L("stay"), OP.mult)
        lts(L("x3", 3), L("dvm"), L("back"), OP.mult)
        lts(clo, L("back"), L("wprev"), OP.mult, L("x"), OP.add)
        ltt(L("val"), L("x"), L("va"), OP.add)
        lts(R("RC", 0, 1), clo, 0.125, OP.mult)
        lts(L("t2", a=3, b=6), L("el"), L("val"), OP.mult)
        lts(L("x1"), R("RC", 0, 1), AM, OP.mult)
        ltt(L("t1", a=3, b=6), L("t1", a=3, b=6), L("x3"), OP.add)
        lts(L("lod"), clo, NB6, OP.mult, L("x1"), OP.add)
        ltt(R(SN, 0, 9), L("t1"), L("t2"), OP.add)
        pump(PUMP)
        cp(R("PXS", 0, 128), R("PX", 0, 128))
        pump(2)
        PD = [R("PD", 16 * k, 16 * k + 16) for k in range(4)]
        for k in (1, 0):
            tt(PD[k], IND(R("PXS"), R("LAB", 2, 3)), R("PLS", 16 * k, 16 * k + 16), OP.subtract)
        pump(1)
        for k in (1, 0):
            tt(PD[2 + k], IND(R("PXS"), R("LAB", 0, 1)), PD[k], OP.subtract)
        pump(1)
        cp(R("LP"), PD[3])
        ts(R("LN"), PD[2], 4095.0, OP.min)
        mm(R("PC", 0, 32), R("ONEF"), R("RB"), True, False, inc=True)
        act(R("D"), IND(R("C"), R("LN")))
        pump(1)
        cp(R("E"), IND(R("FP"), R("LP")))
        for h in (0, 1):
            mm(R("PC", 16 * h, 16 * h + 16), cols("D", h), R("W4"), False, False)
        for h in (0, 1):
            mm(R("PC", 16 * h, 16 * h + 16), cols("E", h), R("WE4"), False, h == 1)
        mm(R("PX", 0, 256), R("IK"), R("E"), True, False)
        mm(R("PX", 0, 256), R("LQ"), R("D"), False, True)
        pump(2)
        ts(R("KQ", 16, 48), R("PC", 0, 32), M8, OP.add, M8, OP.subtract)
        pump(1)
        tt(R("KQ", 48, 64), R("PC", 0, 32, 2), R("KQ", 16, 48, 2), OP.subtract)
        pump(1)
        tt(R("KQ", 0, 16), R("KQ", 48, 64), R("KQ", 17, 48, 2), OP.add)
        pump(1)
        tt(R("OH2"), IND(R("KQ", 0, 48), R("L9", 0, 9)), R("IOT2"), OP.is_equal)
        mm(R("PI", 72, 144), ONES(128), R("OH2", 0, 72), False, False)
        mm(R("PI", 0, 144), R("TRI2"), R("OH2"), False, True)
        pump(2)
        run("v", V.tensor_tensor_scan, [R("S2")], [R("D0"), R("PI", 0, 144)], 0.0, OP.add, OP.max)
        pump(1)
        tt(R("LT2"), IND(R("S2"), R("L16")), R("DEL"), OP.mult)
        for h in (0, 1):
            mm(R("PU", 8 * h, 8 * h + 8), cols("LT2", h), R("RA"), True, True)
        pump(2)
        ts(R("DOFF"), R("PU", 0, 16), 256.0, OP.add)
        pump(1)
        for buf, src, win, rs, ls in (("SEND", "D", "WS", "rn", "ln"), ("SENDC", "E2", "WC", "rc", "lc")):
            if src == "E2":
                ts(R("E2"), R("PX", 0, 256), M1, OP.add, M1, OP.subtract)
            scat(R(buf), R("DOFF"), R(src))
            act(R(win, land + 32 * rank, land + 32 * rank + 32), R(buf, 32 * rank, 32 * rank + 32))
            before("p", R(buf)[0], [])
            to_all(lambda c: T[buf][:, 32 * T.rank_of(c):32 * T.rank_of(c) + 32], T[win][:, land + 32 * rank:land + 32 * rank + 32], rs, ls)
        pump(99)

    SF = "ST%d" % (RO % 2)
    for l in range(3):
        ts(R("OLIST", 16 * l, 16 * l + 16), R("SBASE", 0, 16), R(SF, l, l + 1), OP.add, 256.0, OP.mult)
    before("y", R(SF)[0], [])
    g.sync.dma_start(T.yt[:, :], T[SF][0:128:16, 3:11]).then_inc(T.sem.dout, 16)
    wait("v", "rn", per * RO)
    wait("a", "rc", per * RO)
    cp(R("YL"), IND(R("WS"), R("OLIST")))
    before("y", R("YL")[0], [])
    g.sync.dma_start(T.yl[:, :], T.YL[:, :]).then_inc(T.sem.dout, 16)
    for l in range(3):
        act(R("YC", 256 * l, 256 * l + 256), IND(R("WC"), R("OLIST", 16 * l, 16 * l + 16)))
        o = R(("PT0", "PX", "PL")[l], 0, 256, p=8)
        mm(o, R("W81"), R("YC", 256 * l, 256 * l + 256), True, True)
        cp(R("YF", 256 * l, 256 * l + 256, p=8), o)
    before("y", R("YF")[0], [])
    g.sync.dma_start(T.yf[:, :], T.YF[0:8, :]).then_inc(T.sem.dout, 16)
    for sem, val in (("dout", 48), ("lt", per * RO), ("ln", per * RO), ("lc", per * RO), ("rt", per * RO), ("rn", per * RO), ("rc", per * RO),
                     ("sv", cnt["v"]), ("st", cnt["t"]), ("sa", cnt["a"]), ("sp", cnt["p"])):
        g.wait_ge(T.sem[sem], val)
